import numpy as np
import ml_dtypes


def mxq(x, axis, fmt="e4m3"):
    dtype, down = {"e4m3": (ml_dtypes.float8_e4m3fn, 7), "e5m2": (ml_dtypes.float8_e5m2, 14)}[fmt]
    v = np.moveaxis(np.asarray(x, np.float32).astype(ml_dtypes.bfloat16).astype(np.float64), axis, -1)
    blocks = v.reshape(v.shape[:-1] + (-1, 32))
    amax = np.abs(blocks).max(-1, keepdims=True)
    byte = np.maximum(np.where(amax > 0, np.frexp(amax)[1] - 1 + 127, 0) - down, 1)
    scale = np.exp2(byte - 127.0)
    codes = (blocks / scale).astype(np.float32).astype(dtype).astype(np.float64)
    return np.moveaxis((codes * scale).reshape(v.shape), -1, axis)


WIDE = False


def mx_kscale(k):
    if not WIDE:
        return np.ones(k)
    levels = np.array([30, -30])
    if k % 512:
        return np.exp2(np.random.permutation(np.resize(levels, k // 32))).repeat(32)
    a = np.empty((k // 512, 16))
    for p in range(k // 512):
        a[p, :8] = np.random.permutation(np.resize(levels, 8))
        for g in range(8):
            far = levels[np.abs(levels - a[p, g]) >= 10]
            a[p, g + 8] = far[np.random.randint(len(far))]
    return np.exp2(a.ravel()).repeat(32)


def f64(x):
    return np.asarray(x).astype(np.float64)


def striped(idx):
    return np.tile(idx.reshape(-1, 16).T, (8, 1)).astype(np.uint16)


def unstriped(offs):
    return offs[:16].T.reshape(-1).astype(np.int64)


E2M1 = np.array([0.0, 0.5, 1.0, 1.5, 2.0, 3.0, 4.0, 6.0, -0.0, -0.5, -1.0, -1.5, -2.0, -3.0, -4.0, -6.0])


def pack_weight(w, fmt):
    k, n = w.shape
    w = f64(np.asarray(w, np.float32).astype(ml_dtypes.bfloat16)).reshape(k // 32, 32, n)
    amax = np.abs(w).max(1)
    if fmt == "e4m3":
        byte = np.frexp(amax)[1] - 1 + 127 - 7
    elif fmt == "e5m2":
        byte = np.frexp(amax)[1] - 1 + 127 - 14
    else:
        mant, ex = np.frexp(amax / 6.0)
        byte = np.where(mant > 0.5, ex, ex - 1) + 127
    byte = np.clip(np.where(amax > 0, byte, 1), 1, 254)
    scaled = (w * np.exp2(127.0 - byte)[:, None, :]).reshape(k, n).astype(np.float32)
    by_word = np.ascontiguousarray(scaled.reshape(k // 512, 128, 4, n).transpose(0, 1, 3, 2))
    if fmt == "e4m3":
        words = by_word.astype(ml_dtypes.float8_e4m3fn).view(np.uint8)
    elif fmt == "e5m2":
        words = by_word.astype(ml_dtypes.float8_e5m2).view(np.uint8)
    else:
        c = by_word.astype(ml_dtypes.float4_e2m1fn).view(np.uint8) & 0xF
        words = (c[..., 0::2] | (c[..., 1::2] << 4)).reshape(k // 512, 128, 2 * n)
    return np.ascontiguousarray(words), np.ascontiguousarray(byte.astype(np.uint8).reshape(k // 512, 16, n))


def unpack_weight(words, scales, fmt):
    g, _, n = scales.shape
    words = np.ascontiguousarray(words).reshape(g, 128, n, -1)
    if fmt == "e4m3":
        vals = words.view(ml_dtypes.float8_e4m3fn).astype(np.float64)
    elif fmt == "e5m2":
        vals = words.view(ml_dtypes.float8_e5m2).astype(np.float64)
    else:
        nib = np.empty((g, 128, n, 4), np.uint8)
        nib[..., 0::2] = words & 0xF
        nib[..., 1::2] = words >> 4
        vals = E2M1[nib]
    vals = vals * np.repeat(np.exp2(scales.astype(np.float64) - 127.0), 8, axis=1)[..., None]
    return vals.transpose(0, 1, 3, 2).reshape(g * 512, n)


def d_relu(v):
    return (v > 0).astype(np.float64)


K, T, E, C, H, N = 256, 1024, 2, 512, 512, 1024


def by_expert(wq, xq):
    return np.concatenate([wq[e].T @ xq[:, e * C:(e + 1) * C] for e in range(E)], axis=1)


def setup_inputs():
    n = np.random.standard_normal
    v = mx_kscale(N)
    u = mx_kscale(H)
    slot_token = np.random.permutation(T)[:E * C]
    dy = pack_weight(n((N, T)) * v[:, None], "e5m2")
    w2t = [pack_weight(m, "e4m3") for m in n((E, N, H)) / np.sqrt(N) / v[None, :, None] * u]
    return {
        "dy_words": dy[0],
        "dy_scales": dy[1],
        "w2t_words": np.stack([m[0] for m in w2t]),
        "w2t_scales": np.stack([m[1] for m in w2t]),
        "w1t": (n((H, K)) / np.sqrt(H) / u[:, None]).astype(np.float32),
        "a": (n((H, T))).astype(np.float32),
        "gate": np.tile(np.random.uniform(0.2, 1.0, E * C), (128, 1)).astype(np.float32),
        "offs": striped(slot_token),
    }


def reference(dy_words, dy_scales, w2t_words, w2t_scales, w1t, a, gate, offs):
    w2t = np.stack([unpack_weight(w2t_words[e], w2t_scales[e], "e4m3") for e in range(E)])
    w1tq = mxq(f64(w1t), 0, "e4m3")
    idx = unstriped(offs)
    gq = unpack_weight(dy_words, dy_scales, "e5m2")[:, idx]
    y = by_expert(w2t, gq)
    dh = np.zeros((H, T))
    dh[:, idx] = f64(gate[:1]) * y
    return w1tq.T @ mxq(dh * d_relu(f64(a)), 0, "e5m2")

@@ -1,0 +1,175 @@
+from contextlib import ExitStack
+
+import concourse.mybir as mybir
+from concourse.masks import make_identity
+
+K, T, E, C, H, N = 256, 1024, 2, 512, 512, 1024
+FLOPS = 2 * N * H * E * C + 2 * H * K * T
+
+F32 = mybir.dt.float32
+BF16 = mybir.dt.bfloat16
+I32 = mybir.dt.int32
+U32 = mybir.dt.uint32
+U16 = mybir.dt.uint16
+U8 = mybir.dt.uint8
+E4M3 = mybir.dt.float8_e4m3fn_x4
+E5M2 = mybir.dt.float8_e5m2_x4
+ACT = mybir.ActivationFunctionType
+MULT = mybir.AluOpType.mult
+
+P = 128
+PASSES = N // 512
+PIECES = (128, 128, 256, 256, 256)
+HALF = 512
+QUARTER = 256
+
+
+def tile_moe_sub_relu_kernel(tc, dy_words, dy_scales, w2t_words, w2t_scales, w1t, a, gate, offs, out):
+    nc = tc.nc
+    starts = [sum(PIECES[:c]) for c in range(len(PIECES))]
+    with ExitStack() as ctx:
+        keep = ctx.enter_context(tc.tile_pool(name="keep", bufs=1))
+        ring = ctx.enter_context(tc.tile_pool(name="ring", bufs=3))
+        ps_y = ctx.enter_context(tc.psum_pool(name="ps_y", bufs=4))
+        ps_t = ctx.enter_context(tc.psum_pool(name="ps_t", bufs=3))
+
+        offsets = keep.tile([P, E * C // 16], U16, name="offsets")
+        nc.sync.dma_start(offsets[:], offs)
+
+        def entries(first, count):
+            return offsets[:, first // 16:(first + count) // 16]
+
+        dy_sc = keep.tile([P, PASSES * T], U8, name="dy_sc", align_bytes=64)
+        w2_sc = keep.tile([P, E * PASSES * H], U8, name="w2_sc", align_bytes=64)
+        nc.vector.memset(dy_sc[:].bitcast(I32), 0)
+        nc.vector.memset(w2_sc[:].bitcast(I32), 0)
+        gate_rows = keep.tile([P, P], F32, name="gate_rows")
+        nc.gpsimd.memset(gate_rows[:], 0.0)
+        ident = keep.tile([P, P], F32, name="ident")
+        make_identity(nc, ident[:])
+
+        dy_w = [keep.tile([P, T], I32, name="dy_w%d" % s, align_bytes=64) for s in range(PASSES)]
+        for s in range(PASSES):
+            nc.sync.dma_start(dy_w[s][:], dy_words[s].rearrange("p t d -> p (t d)").bitcast(I32))
+        dy_sc_src = dy_scales.bitcast(I32).rearrange("s (q r) w -> r q s w", r=4)
+        for r in range(4):
+            nc.sync.dma_start(dy_sc[r:P:32, :].bitcast(I32).rearrange("q (s w) -> q s w", s=PASSES), dy_sc_src[r])
+
+        a_rows = a.rearrange("(p u e) t -> u p e t", u=2, e=2)
+        a_raw = {}
+
+        def load_a(u, h):
+            a_raw[u, h] = keep.tile([P, 2, HALF], F32, name="a_raw%d_%d" % (u, h))
+            nc.sync.dma_start(a_raw[u, h][:], a_rows[u][:, :, h * HALF:(h + 1) * HALF])
+
+        mask = {}
+
+        def make_mask(u, h, tag):
+            sign = ring.tile([P, HALF, 2], BF16, name=tag)
+            nc.scalar.activation(sign[:], a_raw[u, h][:].rearrange("p e t -> p t e"), ACT.Sign)
+            mask[u, h] = keep.tile([P, 2 * HALF], BF16, name="mask%d_%d" % (u, h))
+            nc.scalar.activation(mask[u, h][:], sign[:].rearrange("p t e -> p (t e)"), ACT.Relu)
+
+        load_a(0, 0)
+        nc.sync.dma_start(gate_rows[0:E * C // P, :], gate[0].rearrange("(c p) -> c p", p=P))
+        load_a(0, 1)
+        w2_w = [keep.tile([P, PASSES, H], I32, name="w2_w%d" % e, align_bytes=64) for e in range(E)]
+        nc.sync.dma_start(w2_w[0][:], w2t_words[0].rearrange("s p i d -> p s (i d)").bitcast(I32))
+        w2_sc_src = w2t_scales.bitcast(I32).rearrange("e s (q r) w -> r q (e s) w", r=4)
+        for r in range(4):
+            nc.sync.dma_start(w2_sc[r:P:32, :].bitcast(I32).rearrange("q (x w) -> q x w", x=E * PASSES), w2_sc_src[r])
+        nc.sync.dma_start(w2_w[1][:], w2t_words[1].rearrange("s p i d -> p s (i d)").bitcast(I32))
+        for h in range(2):
+            load_a(1, h)
+        w1_raw = keep.tile([P, 4, K], F32, name="w1_raw")
+        nc.sync.dma_start(w1_raw[:], w1t.rearrange("(p j) k -> p j k", j=4))
+
+        make_mask(0, 0, "sign")
+        gate_ps = ps_t.tile([P, HALF], F32, name="turned")
+        nc.tensor.transpose(gate_ps[:, 0:P], gate_rows[:], ident[:])
+        gate_col = keep.tile([P, E * C // P], F32, name="gate_col")
+        nc.scalar.copy(gate_col[:], gate_ps[:, 0:E * C // P])
+        make_mask(0, 1, "sign")
+
+        g_w = {}
+        for s in range(PASSES):
+            for e in range(E):
+                g_w[e, s] = keep.tile([P, C], U32, name="g_w%d_%d" % (e, s), align_bytes=64)
+                nc.vector.tensor_copy(g_w[e, s][:], dy_w[s][:].bitcast(U32).indirect(entries(e * C, C)))
+        g_sc = {}
+        for c, (first, count) in enumerate(zip(starts, PIECES)):
+            for s in range(PASSES):
+                g_sc[c, s] = keep.tile([P, count], U8, name="g_sc%d_%d" % (c, s), align_bytes=64)
+                nc.vector.tensor_copy(g_sc[c, s][:], dy_sc[:, s * T:(s + 1) * T].indirect(entries(first, count)))
+
+        window = [keep.tile([P, T], F32, name="window%d" % u) for u in range(2)]
+        for c, (first, count) in enumerate(zip(starts, PIECES)):
+            e = first // C
+            turned = ps_t.tile([P, HALF], F32, name="turned")
+            for b in range(count // P):
+                j = first // P + b
+                y = ps_y.tile([P, H], F32, name="bank")
+                for s in range(PASSES):
+                    x = e * PASSES + s
+                    nc.tensor.matmul_mx(
+                        out=y[:],
+                        lhsT=g_w[e, s][:, j * P - e * C:(j + 1) * P - e * C].bitcast(E5M2),
+                        lhsT_scale=g_sc[c, s][:, b * P:(b + 1) * P],
+                        rhs=w2_w[e][:, s, :].bitcast(E4M3),
+                        rhs_scale=w2_sc[:, x * H:(x + 1) * H],
+                        start=(s == 0),
+                        stop=(s == PASSES - 1),
+                    )
+                dh = ring.tile([P, H], BF16, name="dh")
+                nc.scalar.activation(
+                    dh[:].rearrange("p (u q e) -> p u q e", u=2, e=2),
+                    y[:].rearrange("p (q u e) -> p u q e", u=2, e=2),
+                    ACT.Copy, scale=gate_col[:, j:j + 1])
+                for u in range(2):
+                    nc.tensor.transpose(
+                        turned[:, u * count + b * P:u * count + (b + 1) * P],
+                        dh[:].bitcast(F32)[:, u * P:(u + 1) * P], ident[:])
+            pairs = keep.tile([P, 2 * count], F32, name="pairs%d" % c)
+            nc.scalar.copy(pairs[:], turned[:, 0:2 * count])
+
+            for u in range(2):
+                nc.vector.tensor_copy(window[u][:].indirect(entries(first, count)), pairs[:, u * count:(u + 1) * count])
+
+
+        for h in range(2):
+            make_mask(1, h, "dh")
+
+        w1_bf = keep.tile([P, K, 4], BF16, name="w1_bf", align_bytes=64)
+        nc.scalar.copy(w1_bf[:], w1_raw[:].rearrange("p j k -> p k j"))
+        w1_w = keep.tile([P, K], U32, name="w1_w", align_bytes=64)
+        w1_sc = keep.tile([P, K], U8, name="w1_sc", align_bytes=64)
+        nc.vector.quantize_mx(out=w1_w[:].bitcast(E4M3), scales=w1_sc[:], in_=w1_bf[:].rearrange("p k j -> p (k j)"))
+
+        da = [keep.tile([P, HALF, 2], F32, name="da%d" % h, align_bytes=64) for h in range(2)]
+        for g in range(T // QUARTER):
+            h, o = divmod(g * QUARTER, HALF)
+            planes = keep.tile([P, 2, QUARTER], F32, name="planes%d" % g)
+            for u in range(2):
+                nc.vector.tensor_tensor(
+                    planes[:, u, :].bitcast(BF16),
+                    window[u][:, g * QUARTER:(g + 1) * QUARTER].bitcast(BF16),
+                    mask[u, h][:, 2 * o:2 * (o + QUARTER)], MULT)
+            nc.scalar.copy(da[h][:, o:o + QUARTER, :], planes[:].rearrange("p u t -> p t u"))
+        for h in range(2):
+            da_w = keep.tile([P, HALF], U32, name="da_w%d" % h, align_bytes=64)
+            da_sc = keep.tile([P, HALF], U8, name="da_sc%d" % h, align_bytes=64)
+            nc.vector.quantize_mx(out=da_w[:].bitcast(E5M2), scales=da_sc[:],
+                                  in_=da[h][:].rearrange("p t u -> p (t u)").bitcast(BF16))
+            for kb in range(K // P):
+                cols = slice(kb * P, (kb + 1) * P)
+                acc = ps_y.tile([P, HALF], F32, name="bank")
+                nc.tensor.matmul_mx(
+                    out=acc[:], lhsT=w1_w[:, cols].bitcast(E4M3), lhsT_scale=w1_sc[:, cols],
+                    rhs=da_w[:].bitcast(E5M2), rhs_scale=da_sc[:], start=True, stop=True)
+                res = keep.tile([P, HALF], F32, name="res%d_%d" % (h, kb))
+                if kb == 0:
+                    nc.scalar.copy(res[:], acc[:])
+                    nc.scalar.dma_start(out[cols, h * HALF:(h + 1) * HALF], res[:])
+                else:
+                    nc.vector.tensor_copy(res[:], acc[:])
+                    nc.sync.dma_start(out[cols, h * HALF:(h + 1) * HALF], res[:])

@@ -20,6 +20,8 @@ MULT = mybir.AluOpType.mult
 P = 128
 PASSES = N // 512
 PIECES = (128, 128, 256, 256, 256)
+AHEAD = 0
+W2_BYTES = 4 * PASSES * H
 HALF = 512
 QUARTER = 256
 
@@ -29,8 +31,10 @@ def tile_moe_sub_relu_kernel(tc, dy_words, dy_scales, w2t_words, w2t_scales, w1t
     starts = [sum(PIECES[:c]) for c in range(len(PIECES))]
     with ExitStack() as ctx:
         keep = ctx.enter_context(tc.tile_pool(name="keep", bufs=1))
-        ring = ctx.enter_context(tc.tile_pool(name="ring", bufs=3))
-        ps_y = ctx.enter_context(tc.psum_pool(name="ps_y", bufs=4))
+        late = ctx.enter_context(tc.tile_pool(name="late", bufs=1))
+        ring = ctx.enter_context(tc.tile_pool(name="ring", bufs=2))
+        ps_y = ctx.enter_context(tc.psum_pool(name="ps_y", bufs=2))
+        ps_o = ctx.enter_context(tc.psum_pool(name="ps_o", bufs=2))
         ps_t = ctx.enter_context(tc.psum_pool(name="ps_t", bufs=3))
 
         offsets = keep.tile([P, E * C // 16], U16, name="offsets")
@@ -39,87 +43,105 @@ def tile_moe_sub_relu_kernel(tc, dy_words, dy_scales, w2t_words, w2t_scales, w1t
         def entries(first, count):
             return offsets[:, first // 16:(first + count) // 16]
 
-        dy_sc = keep.tile([P, PASSES * T], U8, name="dy_sc", align_bytes=64)
+        dy_sc = late.tile([P, T], U8, name="dy_sc", offset=W2_BYTES - T // 2)
         w2_sc = keep.tile([P, E * PASSES * H], U8, name="w2_sc", align_bytes=64)
         nc.vector.memset(dy_sc[:].bitcast(I32), 0)
         nc.vector.memset(w2_sc[:].bitcast(I32), 0)
         gate_rows = keep.tile([P, P], F32, name="gate_rows")
         nc.gpsimd.memset(gate_rows[:], 0.0)
+        nc.sync.dma_start(gate_rows[0:E * C // P, :], gate[0].rearrange("(c p) -> c p", p=P))
         ident = keep.tile([P, P], F32, name="ident")
         make_identity(nc, ident[:])
 
-        dy_w = [keep.tile([P, T], I32, name="dy_w%d" % s, align_bytes=64) for s in range(PASSES)]
-        for s in range(PASSES):
-            nc.sync.dma_start(dy_w[s][:], dy_words[s].rearrange("p t d -> p (t d)").bitcast(I32))
-        dy_sc_src = dy_scales.bitcast(I32).rearrange("s (q r) w -> r q s w", r=4)
-        for r in range(4):
-            nc.sync.dma_start(dy_sc[r:P:32, :].bitcast(I32).rearrange("q (s w) -> q s w", s=PASSES), dy_sc_src[r])
+        for q in range(4):
+            nc.sync.dma_start(dy_sc[32 * q:32 * q + 4 * PASSES, :].bitcast(I32), dy_scales.bitcast(I32)[:, 4 * q:4 * q + 4, :])
+        dy_w = keep.tile([P, PASSES, T], I32, name="dy_w", align_bytes=64)
+        nc.sync.dma_start(dy_w[:], dy_words.rearrange("s p t d -> p s (t d)").bitcast(I32))
+        moved = [keep.tile([P, C], U8, name="moved%d" % e, align_bytes=64) for e in range(E)]
+        for e in range(E):
+            nc.vector.memset(moved[e][:].bitcast(I32), 0)
 
         a_rows = a.rearrange("(p u e) t -> u p e t", u=2, e=2)
         a_raw = {}
 
-        def load_a(u, h):
-            a_raw[u, h] = keep.tile([P, 2, HALF], F32, name="a_raw%d_%d" % (u, h))
-            nc.sync.dma_start(a_raw[u, h][:], a_rows[u][:, :, h * HALF:(h + 1) * HALF])
+        def load_a(floats, u, h):
+            x = 2 * h + u
+            a_raw[u, h] = floats[:, x * 2 * HALF:(x + 1) * 2 * HALF].rearrange("p (e t) -> p e t", e=2)
+            nc.sync.dma_start(a_raw[u, h], a_rows[u][:, :, h * HALF:(h + 1) * HALF])
 
         mask = {}
 
         def make_mask(u, h, tag):
-            sign = ring.tile([P, HALF, 2], BF16, name=tag)
-            nc.scalar.activation(sign[:], a_raw[u, h][:].rearrange("p e t -> p t e"), ACT.Sign)
+            sign = keep.tile([P, HALF, 2], BF16, name="sign%d_%d" % (u, h), tag=tag, align_bytes=64)
+            nc.scalar.activation(sign[:], a_raw[u, h].rearrange("p e t -> p t e"), ACT.Sign)
             mask[u, h] = keep.tile([P, 2 * HALF], BF16, name="mask%d_%d" % (u, h))
-            nc.scalar.activation(mask[u, h][:], sign[:].rearrange("p t e -> p (t e)"), ACT.Relu)
+            if (u, h) == (0, 0):
+                nc.scalar.activation(mask[u, h][:], sign[:].rearrange("p t e -> p (t e)"), ACT.Relu)
+            else:
+                nc.vector.tensor_scalar_max(mask[u, h][:], sign[:].rearrange("p t e -> p (t e)"), 0.0)
 
-        load_a(0, 0)
-        nc.sync.dma_start(gate_rows[0:E * C // P, :], gate[0].rearrange("(c p) -> c p", p=P))
-        load_a(0, 1)
-        w2_w = [keep.tile([P, PASSES, H], I32, name="w2_w%d" % e, align_bytes=64) for e in range(E)]
+        w2_w = [keep.tile([P, PASSES, H], I32, name="w2_w0", align_bytes=64)]
         nc.sync.dma_start(w2_w[0][:], w2t_words[0].rearrange("s p i d -> p s (i d)").bitcast(I32))
         w2_sc_src = w2t_scales.bitcast(I32).rearrange("e s (q r) w -> r q (e s) w", r=4)
         for r in range(4):
             nc.sync.dma_start(w2_sc[r:P:32, :].bitcast(I32).rearrange("q (x w) -> q x w", x=E * PASSES), w2_sc_src[r])
-        nc.sync.dma_start(w2_w[1][:], w2t_words[1].rearrange("s p i d -> p s (i d)").bitcast(I32))
-        for h in range(2):
-            load_a(1, h)
-        w1_raw = keep.tile([P, 4, K], F32, name="w1_raw")
-        nc.sync.dma_start(w1_raw[:], w1t.rearrange("(p j) k -> p j k", j=4))
 
-        make_mask(0, 0, "sign")
         gate_ps = ps_t.tile([P, HALF], F32, name="turned")
         nc.tensor.transpose(gate_ps[:, 0:P], gate_rows[:], ident[:])
         gate_col = keep.tile([P, E * C // P], F32, name="gate_col")
         nc.scalar.copy(gate_col[:], gate_ps[:, 0:E * C // P])
-        make_mask(0, 1, "sign")
 
-        g_w = {}
-        for s in range(PASSES):
-            for e in range(E):
-                g_w[e, s] = keep.tile([P, C], U32, name="g_w%d_%d" % (e, s), align_bytes=64)
-                nc.vector.tensor_copy(g_w[e, s][:], dy_w[s][:].bitcast(U32).indirect(entries(e * C, C)))
         g_sc = {}
+        for e in range(E):
+            both = keep.tile([P, C], U8, name="g_sc%d" % e, align_bytes=64)
+            nc.vector.tensor_copy(both[:], dy_sc[:].indirect(entries(e * C, C)))
+            nc.sync.dma_start(moved[e][0:100, :].bitcast(I32), both[4:104, :].bitcast(I32))
+            g_sc[e, 0] = both
+            g_sc[e, 1] = moved[e]
+        w2_w.append(late.tile([P, PASSES, H], I32, name="w2_w1", offset=0, align_bytes=64))
+        nc.sync.dma_start(w2_w[1][:], w2t_words[1].rearrange("s p i d -> p s (i d)").bitcast(I32))
+        floats = late.tile([P, 4 * T + 4 * K], F32, name="floats", offset=W2_BYTES)
+        for h in range(2):
+            for u in range(2):
+                load_a(floats, u, h)
+        w1_raw = floats[:, 4 * T:].rearrange("p (j k) -> p j k", j=4)
+        nc.sync.dma_start(w1_raw, w1t.rearrange("(p j) k -> p j k", j=4))
+        g_w = {}
         for c, (first, count) in enumerate(zip(starts, PIECES)):
             for s in range(PASSES):
-                g_sc[c, s] = keep.tile([P, count], U8, name="g_sc%d_%d" % (c, s), align_bytes=64)
-                nc.vector.tensor_copy(g_sc[c, s][:], dy_sc[:, s * T:(s + 1) * T].indirect(entries(first, count)))
+                g_w[c, s] = keep.tile([P, count], U32, name="g_w%d_%d" % (c, s), tag="g_w%d_%d" % (c, s), align_bytes=64)
+                nc.vector.tensor_copy(g_w[c, s][:], dy_w[:, s, :].bitcast(U32).indirect(entries(first, count)))
 
         window = [keep.tile([P, T], F32, name="window%d" % u) for u in range(2)]
+        where = [(c, b) for c, count in enumerate(PIECES) for b in range(count // P)]
+        y_of = {}
+
+        def product_pass(j, s):
+            c, b = where[j]
+            e = j * P // C
+            x = e * PASSES + s
+            if s == 0:
+                y_of[j] = ps_y.tile([P, H], F32, name="bank")
+            nc.tensor.matmul_mx(
+                out=y_of[j][:],
+                lhsT=g_w[c, s][:, b * P:(b + 1) * P].bitcast(E5M2),
+                lhsT_scale=g_sc[e, s][:, j * P - e * C:(j + 1) * P - e * C],
+                rhs=w2_w[e][:, s, :].bitcast(E4M3),
+                rhs_scale=w2_sc[:, x * H:(x + 1) * H],
+                start=(s == 0),
+                stop=(s == PASSES - 1),
+            )
+
+        for j in range(AHEAD):
+            product_pass(j, 0)
         for c, (first, count) in enumerate(zip(starts, PIECES)):
-            e = first // C
             turned = ps_t.tile([P, HALF], F32, name="turned")
             for b in range(count // P):
                 j = first // P + b
-                y = ps_y.tile([P, H], F32, name="bank")
-                for s in range(PASSES):
-                    x = e * PASSES + s
-                    nc.tensor.matmul_mx(
-                        out=y[:],
-                        lhsT=g_w[e, s][:, j * P - e * C:(j + 1) * P - e * C].bitcast(E5M2),
-                        lhsT_scale=g_sc[c, s][:, b * P:(b + 1) * P],
-                        rhs=w2_w[e][:, s, :].bitcast(E4M3),
-                        rhs_scale=w2_sc[:, x * H:(x + 1) * H],
-                        start=(s == 0),
-                        stop=(s == PASSES - 1),
-                    )
+                if j >= AHEAD:
+                    product_pass(j, 0)
+                product_pass(j, 1)
+                y = y_of[j]
                 dh = ring.tile([P, H], BF16, name="dh")
                 nc.scalar.activation(
                     dh[:].rearrange("p (u q e) -> p u q e", u=2, e=2),
@@ -136,11 +158,13 @@ def tile_moe_sub_relu_kernel(tc, dy_words, dy_scales, w2t_words, w2t_scales, w1t
                 nc.vector.tensor_copy(window[u][:].indirect(entries(first, count)), pairs[:, u * count:(u + 1) * count])
 
 
-        for h in range(2):
-            make_mask(1, h, "dh")
+        make_mask(0, 0, "g_w2_1")
+        make_mask(1, 0, "g_w3_1")
+        make_mask(0, 1, "g_w4_0")
+        make_mask(1, 1, "g_w4_1")
 
         w1_bf = keep.tile([P, K, 4], BF16, name="w1_bf", align_bytes=64)
-        nc.scalar.copy(w1_bf[:], w1_raw[:].rearrange("p j k -> p k j"))
+        nc.scalar.copy(w1_bf[:], w1_raw.rearrange("p j k -> p k j"))
         w1_w = keep.tile([P, K], U32, name="w1_w", align_bytes=64)
         w1_sc = keep.tile([P, K], U8, name="w1_sc", align_bytes=64)
         nc.vector.quantize_mx(out=w1_w[:].bitcast(E4M3), scales=w1_sc[:], in_=w1_bf[:].rearrange("p k j -> p (k j)"))
@@ -162,7 +186,7 @@ def tile_moe_sub_relu_kernel(tc, dy_words, dy_scales, w2t_words, w2t_scales, w1t
                                   in_=da[h][:].rearrange("p t u -> p (t u)").bitcast(BF16))
             for kb in range(K // P):
                 cols = slice(kb * P, (kb + 1) * P)
-                acc = ps_y.tile([P, HALF], F32, name="bank")
+                acc = (ps_y if h == 0 else ps_o).tile([P, HALF], F32, name="bank")
                 nc.tensor.matmul_mx(
                     out=acc[:], lhsT=w1_w[:, cols].bitcast(E4M3), lhsT_scale=w1_sc[:, cols],
                     rhs=da_w[:].bitcast(E5M2), rhs_scale=da_sc[:], start=True, stop=True)

@@ -75,7 +75,7 @@ def tile_moe_sub_relu_kernel(tc, dy_words, dy_scales, w2t_words, w2t_scales, w1t
             sign = keep.tile([P, HALF, 2], BF16, name="sign%d_%d" % (u, h), tag=tag, align_bytes=64)
             nc.scalar.activation(sign[:], a_raw[u, h].rearrange("p e t -> p t e"), ACT.Sign)
             mask[u, h] = keep.tile([P, 2 * HALF], BF16, name="mask%d_%d" % (u, h))
-            if (u, h) == (0, 0):
+            if (u, h) != (1, 1):
                 nc.scalar.activation(mask[u, h][:], sign[:].rearrange("p t e -> p (t e)"), ACT.Relu)
             else:
                 nc.vector.tensor_scalar_max(mask[u, h][:], sign[:].rearrange("p t e -> p (t e)"), 0.0)

@@ -15,27 +15,27 @@ U8 = mybir.dt.uint8
 E4M3 = mybir.dt.float8_e4m3fn_x4
 E5M2 = mybir.dt.float8_e5m2_x4
 ACT = mybir.ActivationFunctionType
-MULT = mybir.AluOpType.mult
+ALU = mybir.AluOpType
 
 P = 128
 PASSES = N // 512
-PIECES = (128, 128, 256, 256, 256)
-AHEAD = 0
+PIECE = 256
+PIECES = E * C // PIECE
 W2_BYTES = 4 * PASSES * H
 HALF = 512
-QUARTER = 256
+SCALE_ROWS = 100
+BYTE_CUTS = ((0, PIECE), (PIECE, E * C))
 
 
 def tile_moe_sub_relu_kernel(tc, dy_words, dy_scales, w2t_words, w2t_scales, w1t, a, gate, offs, out):
     nc = tc.nc
-    starts = [sum(PIECES[:c]) for c in range(len(PIECES))]
     with ExitStack() as ctx:
         keep = ctx.enter_context(tc.tile_pool(name="keep", bufs=1))
         late = ctx.enter_context(tc.tile_pool(name="late", bufs=1))
         ring = ctx.enter_context(tc.tile_pool(name="ring", bufs=2))
         ps_y = ctx.enter_context(tc.psum_pool(name="ps_y", bufs=2))
         ps_o = ctx.enter_context(tc.psum_pool(name="ps_o", bufs=2))
-        ps_t = ctx.enter_context(tc.psum_pool(name="ps_t", bufs=3))
+        ps_t = ctx.enter_context(tc.psum_pool(name="ps_t", bufs=2))
 
         offsets = keep.tile([P, E * C // 16], U16, name="offsets")
         nc.sync.dma_start(offsets[:], offs)
@@ -45,46 +45,27 @@ def tile_moe_sub_relu_kernel(tc, dy_words, dy_scales, w2t_words, w2t_scales, w1t
 
         dy_sc = late.tile([P, T], U8, name="dy_sc", offset=W2_BYTES - T // 2)
         w2_sc = keep.tile([P, E * PASSES * H], U8, name="w2_sc", align_bytes=64)
-        nc.vector.memset(dy_sc[:].bitcast(I32), 0)
-        nc.vector.memset(w2_sc[:].bitcast(I32), 0)
+        moved = [keep.tile([P, hi - lo], U8, name="moved%d" % lo, tag="moved%d" % lo, align_bytes=64) for lo, hi in BYTE_CUTS]
         gate_rows = keep.tile([P, P], F32, name="gate_rows")
-        nc.gpsimd.memset(gate_rows[:], 0.0)
-        nc.sync.dma_start(gate_rows[0:E * C // P, :], gate[0].rearrange("(c p) -> c p", p=P))
         ident = keep.tile([P, P], F32, name="ident")
+        nc.gpsimd.memset(dy_sc[:].bitcast(I32), 0)
+        nc.gpsimd.memset(w2_sc[:].bitcast(I32), 0)
         make_identity(nc, ident[:])
+        nc.vector.memset(gate_rows[:], 0.0)
+        for tile in moved:
+            nc.vector.memset(tile[:].bitcast(I32), 0)
 
         for q in range(4):
             nc.sync.dma_start(dy_sc[32 * q:32 * q + 4 * PASSES, :].bitcast(I32), dy_scales.bitcast(I32)[:, 4 * q:4 * q + 4, :])
-        dy_w = keep.tile([P, PASSES, T], I32, name="dy_w", align_bytes=64)
-        nc.sync.dma_start(dy_w[:], dy_words.rearrange("s p t d -> p s (t d)").bitcast(I32))
-        moved = [keep.tile([P, C], U8, name="moved%d" % e, align_bytes=64) for e in range(E)]
-        for e in range(E):
-            nc.vector.memset(moved[e][:].bitcast(I32), 0)
-
-        a_rows = a.rearrange("(p u e) t -> u p e t", u=2, e=2)
-        a_raw = {}
-
-        def load_a(floats, u, h):
-            x = 2 * h + u
-            a_raw[u, h] = floats[:, x * 2 * HALF:(x + 1) * 2 * HALF].rearrange("p (e t) -> p e t", e=2)
-            nc.sync.dma_start(a_raw[u, h], a_rows[u][:, :, h * HALF:(h + 1) * HALF])
-
-        mask = {}
-
-        def make_mask(u, h, tag):
-            sign = keep.tile([P, HALF, 2], BF16, name="sign%d_%d" % (u, h), tag=tag, align_bytes=64)
-            nc.scalar.activation(sign[:], a_raw[u, h].rearrange("p e t -> p t e"), ACT.Sign)
-            mask[u, h] = keep.tile([P, 2 * HALF], BF16, name="mask%d_%d" % (u, h))
-            if (u, h) != (1, 1):
-                nc.scalar.activation(mask[u, h][:], sign[:].rearrange("p t e -> p (t e)"), ACT.Relu)
-            else:
-                nc.vector.tensor_scalar_max(mask[u, h][:], sign[:].rearrange("p t e -> p (t e)"), 0.0)
-
-        w2_w = [keep.tile([P, PASSES, H], I32, name="w2_w0", align_bytes=64)]
-        nc.sync.dma_start(w2_w[0][:], w2t_words[0].rearrange("s p i d -> p s (i d)").bitcast(I32))
+        nc.sync.dma_start(gate_rows[0:E * C // P, :], gate[0].rearrange("(c p) -> c p", p=P))
+        dy_w = keep.tile([P, PASSES * T], I32, name="dy_w", align_bytes=64)
+        nc.sync.dma_start(dy_w[:].rearrange("p (s t) -> p s t", s=PASSES), dy_words.rearrange("s p t d -> p s (t d)").bitcast(I32))
         w2_sc_src = w2t_scales.bitcast(I32).rearrange("e s (q r) w -> r q (e s) w", r=4)
         for r in range(4):
             nc.sync.dma_start(w2_sc[r:P:32, :].bitcast(I32).rearrange("q (x w) -> q x w", x=E * PASSES), w2_sc_src[r])
+
+        w2_w = [keep.tile([P, PASSES, H], I32, name="w2_w0", align_bytes=64)]
+        nc.sync.dma_start(w2_w[0][:], w2t_words[0].rearrange("s p i d -> p s (i d)").bitcast(I32))
 
         gate_ps = ps_t.tile([P, HALF], F32, name="turned")
         nc.tensor.transpose(gate_ps[:, 0:P], gate_rows[:], ident[:])
@@ -92,56 +73,56 @@ def tile_moe_sub_relu_kernel(tc, dy_words, dy_scales, w2t_words, w2t_scales, w1t
         nc.scalar.copy(gate_col[:], gate_ps[:, 0:E * C // P])
 
         g_sc = {}
-        for e in range(E):
-            both = keep.tile([P, C], U8, name="g_sc%d" % e, align_bytes=64)
-            nc.vector.tensor_copy(both[:], dy_sc[:].indirect(entries(e * C, C)))
-            nc.sync.dma_start(moved[e][0:100, :].bitcast(I32), both[4:104, :].bitcast(I32))
-            g_sc[e, 0] = both
-            g_sc[e, 1] = moved[e]
+        for (lo, hi), shifted in zip(BYTE_CUTS, moved):
+            both = keep.tile([P, hi - lo], U8, name="both%d" % lo, tag="both%d" % lo, align_bytes=64)
+            nc.vector.tensor_copy(both[:], dy_sc[:].indirect(entries(lo, hi - lo)))
+            nc.sync.dma_start(shifted[0:SCALE_ROWS, :].bitcast(I32), both[4:SCALE_ROWS + 4, :].bitcast(I32))
+            for j in range(lo // P, hi // P):
+                g_sc[j] = [tile[:, j * P - lo:(j + 1) * P - lo] for tile in (both, shifted)]
+
+        floats = late.tile([P, 4 * T + 4 * K], F32, name="floats", offset=W2_BYTES)
+        a_rows = a.rearrange("(p u e) t -> u p e t", u=2, e=2)
+        a_raw = {}
+
+        def load_a(u):
+            for h in range(2):
+                x = 2 * u + h
+                a_raw[u, h] = floats[:, x * 2 * HALF:(x + 1) * 2 * HALF].rearrange("p (e t) -> p e t", e=2)
+                nc.sync.dma_start(a_raw[u, h], a_rows[u][:, :, h * HALF:(h + 1) * HALF])
+
         w2_w.append(late.tile([P, PASSES, H], I32, name="w2_w1", offset=0, align_bytes=64))
         nc.sync.dma_start(w2_w[1][:], w2t_words[1].rearrange("s p i d -> p s (i d)").bitcast(I32))
-        floats = late.tile([P, 4 * T + 4 * K], F32, name="floats", offset=W2_BYTES)
-        for h in range(2):
-            for u in range(2):
-                load_a(floats, u, h)
+        load_a(1)
+        load_a(0)
         w1_raw = floats[:, 4 * T:].rearrange("p (j k) -> p j k", j=4)
         nc.sync.dma_start(w1_raw, w1t.rearrange("(p j) k -> p j k", j=4))
+
         g_w = {}
-        for c, (first, count) in enumerate(zip(starts, PIECES)):
+        for c in range(PIECES):
             for s in range(PASSES):
-                g_w[c, s] = keep.tile([P, count], U32, name="g_w%d_%d" % (c, s), tag="g_w%d_%d" % (c, s), align_bytes=64)
-                nc.vector.tensor_copy(g_w[c, s][:], dy_w[:, s, :].bitcast(U32).indirect(entries(first, count)))
+                g_w[c, s] = keep.tile([P, PIECE], U32, name="g_w%d_%d" % (c, s), tag="g_w%d_%d" % (c, s), align_bytes=64)
+                nc.vector.tensor_copy(g_w[c, s][:], dy_w[:, s * T:(s + 1) * T].bitcast(U32).indirect(entries(c * PIECE, PIECE)))
 
-        window = [keep.tile([P, T], F32, name="window%d" % u) for u in range(2)]
-        where = [(c, b) for c, count in enumerate(PIECES) for b in range(count // P)]
-        y_of = {}
+        window = [keep.tile([P, 2 * T], F32, name="window%d" % u) for u in range(2)]
+        pairs = keep.tile([P, 2 * E * C], F32, name="pairs")
 
-        def product_pass(j, s):
-            c, b = where[j]
-            e = j * P // C
-            x = e * PASSES + s
-            if s == 0:
-                y_of[j] = ps_y.tile([P, H], F32, name="bank")
-            nc.tensor.matmul_mx(
-                out=y_of[j][:],
-                lhsT=g_w[c, s][:, b * P:(b + 1) * P].bitcast(E5M2),
-                lhsT_scale=g_sc[e, s][:, j * P - e * C:(j + 1) * P - e * C],
-                rhs=w2_w[e][:, s, :].bitcast(E4M3),
-                rhs_scale=w2_sc[:, x * H:(x + 1) * H],
-                start=(s == 0),
-                stop=(s == PASSES - 1),
-            )
-
-        for j in range(AHEAD):
-            product_pass(j, 0)
-        for c, (first, count) in enumerate(zip(starts, PIECES)):
+        def make_piece(c):
             turned = ps_t.tile([P, HALF], F32, name="turned")
-            for b in range(count // P):
-                j = first // P + b
-                if j >= AHEAD:
-                    product_pass(j, 0)
-                product_pass(j, 1)
-                y = y_of[j]
+            for b in range(PIECE // P):
+                j = c * PIECE // P + b
+                e = j * P // C
+                y = ps_y.tile([P, H], F32, name="bank")
+                for s in reversed(range(PASSES)):
+                    x = e * PASSES + s
+                    nc.tensor.matmul_mx(
+                        out=y[:],
+                        lhsT=g_w[c, s][:, b * P:(b + 1) * P].bitcast(E5M2),
+                        lhsT_scale=g_sc[j][s],
+                        rhs=w2_w[e][:, s, :].bitcast(E4M3),
+                        rhs_scale=w2_sc[:, x * H:(x + 1) * H],
+                        start=(s == PASSES - 1),
+                        stop=(s == 0),
+                    )
                 dh = ring.tile([P, H], BF16, name="dh")
                 nc.scalar.activation(
                     dh[:].rearrange("p (u q e) -> p u q e", u=2, e=2),
@@ -149,41 +130,64 @@ def tile_moe_sub_relu_kernel(tc, dy_words, dy_scales, w2t_words, w2t_scales, w1t
                     ACT.Copy, scale=gate_col[:, j:j + 1])
                 for u in range(2):
                     nc.tensor.transpose(
-                        turned[:, u * count + b * P:u * count + (b + 1) * P],
+                        turned[:, u * PIECE + b * P:u * PIECE + (b + 1) * P],
                         dh[:].bitcast(F32)[:, u * P:(u + 1) * P], ident[:])
-            pairs = keep.tile([P, 2 * count], F32, name="pairs%d" % c)
-            nc.scalar.copy(pairs[:], turned[:, 0:2 * count])
+            if c == 0:
+                for u in range(2):
+                    nc.scalar.copy(pairs[:, u * E * C:u * E * C + PIECE], turned[:, u * PIECE:(u + 1) * PIECE])
+            else:
+                nc.scalar.copy(
+                    pairs[:].rearrange("p (u j) -> p u j", u=2)[:, :, c * PIECE:(c + 1) * PIECE],
+                    turned[:].rearrange("p (u j) -> p u j", u=2))
 
+        def scatter(u, first, count):
+            nc.vector.tensor_copy(window[u][:].indirect(entries(first, count)),
+                                  pairs[:, u * E * C + first:u * E * C + first + count])
+
+        sign = {}
+        holder = {(1, 0): "g_w3_0", (1, 1): "g_w3_1", (0, 0): "both256", (0, 1): "moved256"}
+
+        def make_sign(u):
+            for h in range(2):
+                sign[u, h] = keep.tile([P, HALF, 2], BF16, name="sign%d_%d" % (u, h), tag=holder[u, h], align_bytes=64)
+                nc.scalar.activation(sign[u, h][:], a_raw[u, h].rearrange("p e t -> p t e"), ACT.Sign)
+
+        def make_mask(u):
+            for h in range(2):
+                nc.gpsimd.tensor_scalar(
+                    window[1 - u][:, T + h * HALF:T + (h + 1) * HALF].bitcast(BF16),
+                    sign[u, h][:].rearrange("p t e -> p (t e)"), 1.0, 0.0, ALU.min, ALU.max)
+
+        for c in range(2):
+            make_piece(c)
             for u in range(2):
-                nc.vector.tensor_copy(window[u][:].indirect(entries(first, count)), pairs[:, u * count:(u + 1) * count])
-
-
-        make_mask(0, 0, "g_w2_1")
-        make_mask(1, 0, "g_w3_1")
-        make_mask(0, 1, "g_w4_0")
-        make_mask(1, 1, "g_w4_1")
+                scatter(u, c * PIECE, PIECE)
+        for c in range(2, PIECES):
+            make_piece(c)
+            scatter(1, c * PIECE, PIECE)
+        make_sign(1)
+        make_mask(1)
+        make_sign(0)
+        make_mask(0)
+        scatter(0, 2 * PIECE, 2 * PIECE)
 
         w1_bf = keep.tile([P, K, 4], BF16, name="w1_bf", align_bytes=64)
-        nc.scalar.copy(w1_bf[:], w1_raw.rearrange("p j k -> p k j"))
-        w1_w = keep.tile([P, K], U32, name="w1_w", align_bytes=64)
+        nc.gpsimd.tensor_scalar(w1_bf[:], w1_raw.rearrange("p j k -> p k j"), 1.0, 0.0, ALU.mult, ALU.add)
+        w1_w = keep.tile([P, K], U32, name="w1_w", tag="g_w2_1", align_bytes=64)
         w1_sc = keep.tile([P, K], U8, name="w1_sc", align_bytes=64)
         nc.vector.quantize_mx(out=w1_w[:].bitcast(E4M3), scales=w1_sc[:], in_=w1_bf[:].rearrange("p k j -> p (k j)"))
 
-        da = [keep.tile([P, HALF, 2], F32, name="da%d" % h, align_bytes=64) for h in range(2)]
-        for g in range(T // QUARTER):
-            h, o = divmod(g * QUARTER, HALF)
-            planes = keep.tile([P, 2, QUARTER], F32, name="planes%d" % g)
-            for u in range(2):
-                nc.vector.tensor_tensor(
-                    planes[:, u, :].bitcast(BF16),
-                    window[u][:, g * QUARTER:(g + 1) * QUARTER].bitcast(BF16),
-                    mask[u, h][:, 2 * o:2 * (o + QUARTER)], MULT)
-            nc.scalar.copy(da[h][:, o:o + QUARTER, :], planes[:].rearrange("p u t -> p t u"))
+        views = [window[u][:].bitcast(BF16).rearrange("p (u t e) -> p t u e", u=2, e=2) for u in range(2)]
+        da = []
+        for h in range(2):
+            da.append(keep.tile([P, HALF, 2, 2], BF16, name="da%d" % h, align_bytes=64))
+            nc.vector.tensor_tensor(da[h][:], views[0][:, h * HALF:(h + 1) * HALF, :, :],
+                                    views[1][:, h * HALF:(h + 1) * HALF, ::-1, :], ALU.mult)
         for h in range(2):
             da_w = keep.tile([P, HALF], U32, name="da_w%d" % h, align_bytes=64)
             da_sc = keep.tile([P, HALF], U8, name="da_sc%d" % h, align_bytes=64)
             nc.vector.quantize_mx(out=da_w[:].bitcast(E5M2), scales=da_sc[:],
-                                  in_=da[h][:].rearrange("p t u -> p (t u)").bitcast(BF16))
+                                  in_=da[h][:].rearrange("p t u e -> p (t u e)"))
             for kb in range(K // P):
                 cols = slice(kb * P, (kb + 1) * P)
                 acc = (ps_y if h == 0 else ps_o).tile([P, HALF], F32, name="bank")
@@ -191,9 +195,8 @@ def tile_moe_sub_relu_kernel(tc, dy_words, dy_scales, w2t_words, w2t_scales, w1t
                     out=acc[:], lhsT=w1_w[:, cols].bitcast(E4M3), lhsT_scale=w1_sc[:, cols],
                     rhs=da_w[:].bitcast(E5M2), rhs_scale=da_sc[:], start=True, stop=True)
                 res = keep.tile([P, HALF], F32, name="res%d_%d" % (h, kb))
-                if kb == 0:
-                    nc.scalar.copy(res[:], acc[:])
-                    nc.scalar.dma_start(out[cols, h * HALF:(h + 1) * HALF], res[:])
-                else:
+                if h == 1 and kb == 1:
                     nc.vector.tensor_copy(res[:], acc[:])
-                    nc.sync.dma_start(out[cols, h * HALF:(h + 1) * HALF], res[:])
+                else:
+                    nc.scalar.copy(res[:], acc[:])
+                nc.sync.dma_start(out[cols, h * HALF:(h + 1) * HALF], res[:])

@@ -23,19 +23,21 @@ PIECE = 256
 PIECES = E * C // PIECE
 W2_BYTES = 4 * PASSES * H
 HALF = 512
+QUARTER = 256
 SCALE_ROWS = 100
-BYTE_CUTS = ((0, PIECE), (PIECE, E * C))
+BYTE_CUTS = ((0, PIECE), (PIECE, C), (C, E * C))
 
 
 def tile_moe_sub_relu_kernel(tc, dy_words, dy_scales, w2t_words, w2t_scales, w1t, a, gate, offs, out):
     nc = tc.nc
     with ExitStack() as ctx:
         keep = ctx.enter_context(tc.tile_pool(name="keep", bufs=1))
+        last = ctx.enter_context(tc.tile_pool(name="last", bufs=1))
         late = ctx.enter_context(tc.tile_pool(name="late", bufs=1))
-        ring = ctx.enter_context(tc.tile_pool(name="ring", bufs=2))
-        ps_y = ctx.enter_context(tc.psum_pool(name="ps_y", bufs=2))
-        ps_o = ctx.enter_context(tc.psum_pool(name="ps_o", bufs=2))
-        ps_t = ctx.enter_context(tc.psum_pool(name="ps_t", bufs=2))
+        psum = ctx.enter_context(tc.psum_pool(name="psum", bufs=1))
+
+        def bank(n):
+            return psum.tile([P, HALF], F32, name="bank%d" % n, tag="bank%d" % n)
 
         offsets = keep.tile([P, E * C // 16], U16, name="offsets")
         nc.sync.dma_start(offsets[:], offs)
@@ -43,10 +45,10 @@ def tile_moe_sub_relu_kernel(tc, dy_words, dy_scales, w2t_words, w2t_scales, w1t
         def entries(first, count):
             return offsets[:, first // 16:(first + count) // 16]
 
-        dy_sc = late.tile([P, T], U8, name="dy_sc", offset=W2_BYTES - T // 2)
+        dy_sc = last.tile([P, T], U8, name="dy_sc", offset=0)
         w2_sc = keep.tile([P, E * PASSES * H], U8, name="w2_sc", align_bytes=64)
         moved = [keep.tile([P, hi - lo], U8, name="moved%d" % lo, tag="moved%d" % lo, align_bytes=64) for lo, hi in BYTE_CUTS]
-        gate_rows = keep.tile([P, P], F32, name="gate_rows")
+        gate_rows = late.tile([P, P], F32, name="gate_rows", offset=W2_BYTES - 2 * P)
         ident = keep.tile([P, P], F32, name="ident")
         nc.gpsimd.memset(dy_sc[:].bitcast(I32), 0)
         nc.gpsimd.memset(w2_sc[:].bitcast(I32), 0)
@@ -55,148 +57,189 @@ def tile_moe_sub_relu_kernel(tc, dy_words, dy_scales, w2t_words, w2t_scales, w1t
         for tile in moved:
             nc.vector.memset(tile[:].bitcast(I32), 0)
 
+        w2_w = [keep.tile([P, H], I32, name="w2_w%d" % s, align_bytes=64) for s in range(PASSES)]
+        nc.sync.dma_start(w2_w[0][:], w2t_words[0, 0].rearrange("p i d -> p (i d)").bitcast(I32))
         for q in range(4):
             nc.sync.dma_start(dy_sc[32 * q:32 * q + 4 * PASSES, :].bitcast(I32), dy_scales.bitcast(I32)[:, 4 * q:4 * q + 4, :])
         nc.sync.dma_start(gate_rows[0:E * C // P, :], gate[0].rearrange("(c p) -> c p", p=P))
         dy_w = keep.tile([P, PASSES * T], I32, name="dy_w", align_bytes=64)
-        nc.sync.dma_start(dy_w[:].rearrange("p (s t) -> p s t", s=PASSES), dy_words.rearrange("s p t d -> p s (t d)").bitcast(I32))
+        for s in range(PASSES):
+            nc.sync.dma_start(dy_w[:, s * T:(s + 1) * T], dy_words[s].rearrange("p t d -> p (t d)").bitcast(I32))
         w2_sc_src = w2t_scales.bitcast(I32).rearrange("e s (q r) w -> r q (e s) w", r=4)
         for r in range(4):
             nc.sync.dma_start(w2_sc[r:P:32, :].bitcast(I32).rearrange("q (x w) -> q x w", x=E * PASSES), w2_sc_src[r])
 
-        w2_w = [keep.tile([P, PASSES, H], I32, name="w2_w0", align_bytes=64)]
-        nc.sync.dma_start(w2_w[0][:], w2t_words[0].rearrange("s p i d -> p s (i d)").bitcast(I32))
+        nc.sync.dma_start(w2_w[1][:], w2t_words[0, 1].rearrange("p i d -> p (i d)").bitcast(I32))
 
-        gate_ps = ps_t.tile([P, HALF], F32, name="turned")
+        gate_ps = bank(7)
         nc.tensor.transpose(gate_ps[:, 0:P], gate_rows[:], ident[:])
         gate_col = keep.tile([P, E * C // P], F32, name="gate_col")
         nc.scalar.copy(gate_col[:], gate_ps[:, 0:E * C // P])
 
         g_sc = {}
-        for (lo, hi), shifted in zip(BYTE_CUTS, moved):
-            both = keep.tile([P, hi - lo], U8, name="both%d" % lo, tag="both%d" % lo, align_bytes=64)
-            nc.vector.tensor_copy(both[:], dy_sc[:].indirect(entries(lo, hi - lo)))
-            nc.sync.dma_start(shifted[0:SCALE_ROWS, :].bitcast(I32), both[4:SCALE_ROWS + 4, :].bitcast(I32))
-            for j in range(lo // P, hi // P):
-                g_sc[j] = [tile[:, j * P - lo:(j + 1) * P - lo] for tile in (both, shifted)]
 
-        floats = late.tile([P, 4 * T + 4 * K], F32, name="floats", offset=W2_BYTES)
+        def gather_bytes(n, holder):
+            lo, hi = BYTE_CUTS[n]
+            both = keep.tile([P, hi - lo], U8, name="both%d" % lo, tag=holder, align_bytes=64)
+            nc.vector.tensor_copy(both[:], dy_sc[:].indirect(entries(lo, hi - lo)))
+            nc.sync.dma_start(moved[n][0:SCALE_ROWS, :].bitcast(I32), both[4:SCALE_ROWS + 4, :].bitcast(I32))
+            for j in range(lo // P, hi // P):
+                g_sc[j] = [tile[:, j * P - lo:(j + 1) * P - lo] for tile in (both, moved[n])]
+
+        for n in range(2):
+            gather_bytes(n, "both%d" % n)
+
         a_rows = a.rearrange("(p u e) t -> u p e t", u=2, e=2)
+        floats = late.tile([P, 2 * T + 4 * K], F32, name="floats", offset=W2_BYTES)
         a_raw = {}
 
-        def load_a(u):
-            for h in range(2):
-                x = 2 * u + h
-                a_raw[u, h] = floats[:, x * 2 * HALF:(x + 1) * 2 * HALF].rearrange("p (e t) -> p e t", e=2)
-                nc.sync.dma_start(a_raw[u, h], a_rows[u][:, :, h * HALF:(h + 1) * HALF])
+        def load_a(tile, u, h):
+            a_raw[u, h] = tile[:, h * T:(h + 1) * T].rearrange("p (e t) -> p e t", e=2)
+            nc.sync.dma_start(a_raw[u, h], a_rows[u][:, :, h * HALF:(h + 1) * HALF])
 
-        w2_w.append(late.tile([P, PASSES, H], I32, name="w2_w1", offset=0, align_bytes=64))
-        nc.sync.dma_start(w2_w[1][:], w2t_words[1].rearrange("s p i d -> p s (i d)").bitcast(I32))
-        load_a(1)
-        load_a(0)
-        w1_raw = floats[:, 4 * T:].rearrange("p (j k) -> p j k", j=4)
+        load_a(floats, 1, 0)
+        w1_raw = floats[:, 2 * T:].rearrange("p (j k) -> p j k", j=4)
         nc.sync.dma_start(w1_raw, w1t.rearrange("(p j) k -> p j k", j=4))
+        w2_late = late.tile([P, PASSES, H], I32, name="w2_late", offset=0, align_bytes=64)
+        nc.sync.dma_start(w2_late[:], w2t_words[1].rearrange("s p i d -> p s (i d)").bitcast(I32))
+        w2_w = [tile[:] for tile in w2_w] + [w2_late[:, s, :] for s in range(PASSES)]
+        load_a(floats, 1, 1)
 
         g_w = {}
-        for c in range(PIECES):
-            for s in range(PASSES):
-                g_w[c, s] = keep.tile([P, PIECE], U32, name="g_w%d_%d" % (c, s), tag="g_w%d_%d" % (c, s), align_bytes=64)
-                nc.vector.tensor_copy(g_w[c, s][:], dy_w[:, s * T:(s + 1) * T].bitcast(U32).indirect(entries(c * PIECE, PIECE)))
+
+        def gather_words(c, s):
+            g_w[c, s] = keep.tile([P, PIECE], U32, name="g_w%d_%d" % (c, s), tag="g_w%d_%d" % (c % 3, s), align_bytes=64)
+            end = T if c < 2 and s == 0 else PASSES * T
+            nc.vector.tensor_copy(g_w[c, s][:], dy_w[:, s * T:end].bitcast(U32).indirect(entries(c * PIECE, PIECE)))
+
+        for c, s in ((0, 0), (1, 0), (0, 1), (1, 1), (2, 0), (2, 1)):
+            gather_words(c, s)
+
+        w1_bf = keep.tile([P, K, 4], BF16, name="w1_bf", align_bytes=64)
+        nc.gpsimd.tensor_scalar(w1_bf[:], w1_raw.rearrange("p j k -> p k j"), 1.0, 0.0, ALU.mult, ALU.add)
+        w1_w = keep.tile([P, K], U32, name="w1_w", align_bytes=64)
+        w1_sc = keep.tile([P, K], U8, name="w1_sc", align_bytes=64)
+        nc.vector.quantize_mx(out=w1_w[:].bitcast(E4M3), scales=w1_sc[:], in_=w1_bf[:].rearrange("p k j -> p (k j)"))
 
         window = [keep.tile([P, 2 * T], F32, name="window%d" % u) for u in range(2)]
         pairs = keep.tile([P, 2 * E * C], F32, name="pairs")
 
         def make_piece(c):
-            turned = ps_t.tile([P, HALF], F32, name="turned")
+            if c == 0:
+                turned = [bank(2 + u)[:, 0:PIECE] for u in range(2)]
+            else:
+                both_planes = bank(3 + c)
+                turned = [both_planes[:, u * PIECE:(u + 1) * PIECE] for u in range(2)]
             for b in range(PIECE // P):
                 j = c * PIECE // P + b
                 e = j * P // C
-                y = ps_y.tile([P, H], F32, name="bank")
-                for s in reversed(range(PASSES)):
+                y = bank(j if j < 2 else 1 + (j - 2) % 3)
+                for s in range(PASSES):
                     x = e * PASSES + s
                     nc.tensor.matmul_mx(
                         out=y[:],
                         lhsT=g_w[c, s][:, b * P:(b + 1) * P].bitcast(E5M2),
                         lhsT_scale=g_sc[j][s],
-                        rhs=w2_w[e][:, s, :].bitcast(E4M3),
+                        rhs=w2_w[x].bitcast(E4M3),
                         rhs_scale=w2_sc[:, x * H:(x + 1) * H],
-                        start=(s == PASSES - 1),
-                        stop=(s == 0),
+                        start=(s == 0),
+                        stop=(s == PASSES - 1),
                     )
-                dh = ring.tile([P, H], BF16, name="dh")
+                dh = keep.tile([P, H], BF16, name="dh%d" % j, tag="dh%d" % j, align_bytes=64)
                 nc.scalar.activation(
                     dh[:].rearrange("p (u q e) -> p u q e", u=2, e=2),
                     y[:].rearrange("p (q u e) -> p u q e", u=2, e=2),
                     ACT.Copy, scale=gate_col[:, j:j + 1])
                 for u in range(2):
-                    nc.tensor.transpose(
-                        turned[:, u * PIECE + b * P:u * PIECE + (b + 1) * P],
-                        dh[:].bitcast(F32)[:, u * P:(u + 1) * P], ident[:])
+                    nc.tensor.transpose(turned[u][:, b * P:(b + 1) * P], dh[:].bitcast(F32)[:, u * P:(u + 1) * P], ident[:])
             if c == 0:
                 for u in range(2):
-                    nc.scalar.copy(pairs[:, u * E * C:u * E * C + PIECE], turned[:, u * PIECE:(u + 1) * PIECE])
+                    nc.scalar.copy(pairs[:, u * E * C:u * E * C + PIECE], turned[u])
             else:
                 nc.scalar.copy(
                     pairs[:].rearrange("p (u j) -> p u j", u=2)[:, :, c * PIECE:(c + 1) * PIECE],
-                    turned[:].rearrange("p (u j) -> p u j", u=2))
+                    both_planes[:].rearrange("p (u j) -> p u j", u=2))
 
         def scatter(u, first, count):
             nc.vector.tensor_copy(window[u][:].indirect(entries(first, count)),
                                   pairs[:, u * E * C + first:u * E * C + first + count])
 
         sign = {}
-        holder = {(1, 0): "g_w3_0", (1, 1): "g_w3_1", (0, 0): "both256", (0, 1): "moved256"}
 
-        def make_sign(u):
-            for h in range(2):
-                sign[u, h] = keep.tile([P, HALF, 2], BF16, name="sign%d_%d" % (u, h), tag=holder[u, h], align_bytes=64)
-                nc.scalar.activation(sign[u, h][:], a_raw[u, h].rearrange("p e t -> p t e"), ACT.Sign)
+        def make_sign(u, first, count, holder):
+            h, o = divmod(first, HALF)
+            sign[u, first] = keep.tile([P, count, 2], BF16, name="sign%d_%d" % (u, first), tag=holder, align_bytes=64)
+            nc.scalar.activation(sign[u, first][:], a_raw[u, h][:, :, o:o + count].rearrange("p e t -> p t e"), ACT.Sign)
 
-        def make_mask(u):
-            for h in range(2):
-                nc.gpsimd.tensor_scalar(
-                    window[1 - u][:, T + h * HALF:T + (h + 1) * HALF].bitcast(BF16),
-                    sign[u, h][:].rearrange("p t e -> p (t e)"), 1.0, 0.0, ALU.min, ALU.max)
+        def make_mask(u, first, on_scalar=False):
+            signs = sign[u, first][:].rearrange("p t e -> p (t e)")
+            spare = window[1 - u][:, T + first:T + first + signs.shape[1] // 2].bitcast(BF16)
+            if on_scalar:
+                nc.scalar.activation(spare, signs, ACT.Relu)
+            else:
+                nc.gpsimd.tensor_scalar(spare, signs, 1.0, 0.0, ALU.min, ALU.max)
 
-        for c in range(2):
-            make_piece(c)
-            for u in range(2):
-                scatter(u, c * PIECE, PIECE)
-        for c in range(2, PIECES):
-            make_piece(c)
-            scatter(1, c * PIECE, PIECE)
-        make_sign(1)
-        make_mask(1)
-        make_sign(0)
-        make_mask(0)
-        scatter(0, 2 * PIECE, 2 * PIECE)
-
-        w1_bf = keep.tile([P, K, 4], BF16, name="w1_bf", align_bytes=64)
-        nc.gpsimd.tensor_scalar(w1_bf[:], w1_raw.rearrange("p j k -> p k j"), 1.0, 0.0, ALU.mult, ALU.add)
-        w1_w = keep.tile([P, K], U32, name="w1_w", tag="g_w2_1", align_bytes=64)
-        w1_sc = keep.tile([P, K], U8, name="w1_sc", align_bytes=64)
-        nc.vector.quantize_mx(out=w1_w[:].bitcast(E4M3), scales=w1_sc[:], in_=w1_bf[:].rearrange("p k j -> p (k j)"))
+        make_piece(0)
+        make_sign(1, 0, QUARTER, "dh0")
+        gather_bytes(2, "both0")
+        a_last = last.tile([P, 2 * T], F32, name="a_last", offset=0)
+        for h in range(2):
+            load_a(a_last, 0, h)
+        for s in range(PASSES):
+            gather_words(3, s)
+        for u in range(2):
+            scatter(u, 0, PIECE)
+        make_piece(1)
+        make_sign(1, QUARTER, QUARTER, "dh2")
+        for u in range(2):
+            scatter(u, PIECE, PIECE)
+        make_piece(2)
+        make_sign(1, HALF, HALF, "dh4")
+        scatter(0, 2 * PIECE, PIECE)
+        for first in (0, QUARTER, HALF):
+            make_mask(1, first)
+        scatter(1, 2 * PIECE, PIECE)
+        make_piece(3)
+        scatter(1, 3 * PIECE, PIECE)
+        make_sign(0, 0, HALF, "dh6")
+        make_sign(0, HALF, HALF, "dh7")
+        make_mask(0, 0)
+        make_mask(0, HALF, on_scalar=True)
+        scatter(0, 3 * PIECE, PIECE)
 
         views = [window[u][:].bitcast(BF16).rearrange("p (u t e) -> p t u e", u=2, e=2) for u in range(2)]
-        da = []
-        for h in range(2):
-            da.append(keep.tile([P, HALF, 2, 2], BF16, name="da%d" % h, align_bytes=64))
-            nc.vector.tensor_tensor(da[h][:], views[0][:, h * HALF:(h + 1) * HALF, :, :],
-                                    views[1][:, h * HALF:(h + 1) * HALF, ::-1, :], ALU.mult)
-        for h in range(2):
-            da_w = keep.tile([P, HALF], U32, name="da_w%d" % h, align_bytes=64)
-            da_sc = keep.tile([P, HALF], U8, name="da_sc%d" % h, align_bytes=64)
-            nc.vector.quantize_mx(out=da_w[:].bitcast(E5M2), scales=da_sc[:],
-                                  in_=da[h][:].rearrange("p t u e -> p (t u e)"))
+        da = keep.tile([P, T, 2, 2], BF16, name="da", align_bytes=64)
+        da_w = keep.tile([P, T], U32, name="da_w", align_bytes=64)
+        da_sc = keep.tile([P, T], U8, name="da_sc", align_bytes=64)
+
+        def quantise(g):
+            tokens = slice(g * QUARTER, (g + 1) * QUARTER)
+            nc.vector.quantize_mx(out=da_w[:, tokens].bitcast(E5M2), scales=da_sc[:, tokens],
+                                  in_=da[:, tokens, :, :].rearrange("p t u e -> p (t u e)"))
+
+        def finish(first, new):
+            tokens = slice(first, first + HALF)
+            fresh = slice(HALF - new, HALF)
             for kb in range(K // P):
                 cols = slice(kb * P, (kb + 1) * P)
-                acc = (ps_y if h == 0 else ps_o).tile([P, HALF], F32, name="bank")
+                acc = bank(first // P + kb)
                 nc.tensor.matmul_mx(
                     out=acc[:], lhsT=w1_w[:, cols].bitcast(E4M3), lhsT_scale=w1_sc[:, cols],
-                    rhs=da_w[:].bitcast(E5M2), rhs_scale=da_sc[:], start=True, stop=True)
-                res = keep.tile([P, HALF], F32, name="res%d_%d" % (h, kb))
-                if h == 1 and kb == 1:
-                    nc.vector.tensor_copy(res[:], acc[:])
+                    rhs=da_w[:, tokens].bitcast(E5M2), rhs_scale=da_sc[:, tokens], start=True, stop=True)
+                res = keep.tile([P, new], F32, name="res%d_%d" % (first, kb))
+                if first == HALF and kb == 1:
+                    nc.vector.tensor_copy(res[:], acc[:, fresh])
                 else:
-                    nc.scalar.copy(res[:], acc[:])
-                nc.sync.dma_start(out[cols, h * HALF:(h + 1) * HALF], res[:])
+                    nc.scalar.copy(res[:], acc[:, fresh])
+                nc.sync.dma_start(out[cols, first + HALF - new:first + HALF], res[:])
+
+        for g in range(T // QUARTER):
+            tokens = slice(g * QUARTER, (g + 1) * QUARTER)
+            nc.vector.tensor_tensor(da[:, tokens, :, :], views[0][:, tokens, :, :], views[1][:, tokens, ::-1, :], ALU.mult)
+            if g > 0:
+                quantise(g - 1)
+            if g == 2:
+                finish(0, HALF)
+        finish(QUARTER, QUARTER)
+        quantise(T // QUARTER - 1)
+        finish(HALF, QUARTER)

@@ -60,7 +60,7 @@ def tile_moe_sub_relu_kernel(tc, dy_words, dy_scales, w2t_words, w2t_scales, w1t
         w2_w = [keep.tile([P, H], I32, name="w2_w%d" % s, align_bytes=64) for s in range(PASSES)]
         nc.sync.dma_start(w2_w[0][:], w2t_words[0, 0].rearrange("p i d -> p (i d)").bitcast(I32))
         for q in range(4):
-            nc.sync.dma_start(dy_sc[32 * q:32 * q + 4 * PASSES, :].bitcast(I32), dy_scales.bitcast(I32)[:, 4 * q:4 * q + 4, :])
+            (nc.sync if q % 2 == 0 else nc.scalar).dma_start(dy_sc[32 * q:32 * q + 4 * PASSES, :].bitcast(I32), dy_scales.bitcast(I32)[:, 4 * q:4 * q + 4, :])
         nc.sync.dma_start(gate_rows[0:E * C // P, :], gate[0].rearrange("(c p) -> c p", p=P))
         dy_w = keep.tile([P, PASSES * T], I32, name="dy_w", align_bytes=64)
         for s in range(PASSES):
@@ -85,6 +85,7 @@ def tile_moe_sub_relu_kernel(tc, dy_words, dy_scales, w2t_words, w2t_scales, w1t
             nc.sync.dma_start(moved[n][0:SCALE_ROWS, :].bitcast(I32), both[4:SCALE_ROWS + 4, :].bitcast(I32))
             for j in range(lo // P, hi // P):
                 g_sc[j] = [tile[:, j * P - lo:(j + 1) * P - lo] for tile in (both, moved[n])]
+            return both[:]
 
         for n in range(2):
             gather_bytes(n, "both%d" % n)
@@ -107,22 +108,22 @@ def tile_moe_sub_relu_kernel(tc, dy_words, dy_scales, w2t_words, w2t_scales, w1t
 
         g_w = {}
 
-        def gather_words(c, s):
-            g_w[c, s] = keep.tile([P, PIECE], U32, name="g_w%d_%d" % (c, s), tag="g_w%d_%d" % (c % 3, s), align_bytes=64)
-            end = T if c < 2 and s == 0 else PASSES * T
-            nc.vector.tensor_copy(g_w[c, s][:], dy_w[:, s * T:end].bitcast(U32).indirect(entries(c * PIECE, PIECE)))
+        def gather_words(s, lo, hi, holder, end):
+            words = keep.tile([P, hi - lo], U32, name="g_w%d_%d" % (s, lo), tag=holder, align_bytes=64)
+            nc.vector.tensor_copy(words[:], dy_w[:, s * T:end].bitcast(U32).indirect(entries(lo, hi - lo)))
+            for j in range(lo // P, hi // P):
+                g_w[j, s] = words[:, j * P - lo:(j + 1) * P - lo]
+            return words[:]
 
-        for c, s in ((0, 0), (1, 0), (0, 1), (1, 1), (2, 0), (2, 1)):
-            gather_words(c, s)
+        gather_words(0, 0, C, "words_a", T)
+        gather_words(1, 0, PIECE, "words_b", PASSES * T)
+        gather_words(1, PIECE, E * C, "words_c", PASSES * T)
 
         w1_bf = keep.tile([P, K, 4], BF16, name="w1_bf", align_bytes=64)
         nc.gpsimd.tensor_scalar(w1_bf[:], w1_raw.rearrange("p j k -> p k j"), 1.0, 0.0, ALU.mult, ALU.add)
-        w1_w = keep.tile([P, K], U32, name="w1_w", align_bytes=64)
-        w1_sc = keep.tile([P, K], U8, name="w1_sc", align_bytes=64)
-        nc.vector.quantize_mx(out=w1_w[:].bitcast(E4M3), scales=w1_sc[:], in_=w1_bf[:].rearrange("p k j -> p (k j)"))
 
         window = [keep.tile([P, 2 * T], F32, name="window%d" % u) for u in range(2)]
-        pairs = keep.tile([P, 2 * E * C], F32, name="pairs")
+        pairs = keep.tile([P, 2 * E * C], F32, name="pairs", tag="pairs", align_bytes=64)
 
         def make_piece(c):
             if c == 0:
@@ -133,12 +134,12 @@ def tile_moe_sub_relu_kernel(tc, dy_words, dy_scales, w2t_words, w2t_scales, w1t
             for b in range(PIECE // P):
                 j = c * PIECE // P + b
                 e = j * P // C
-                y = bank(j if j < 2 else 1 + (j - 2) % 3)
+                y = bank(j if j < 2 else 1 + j % 2)
                 for s in range(PASSES):
                     x = e * PASSES + s
                     nc.tensor.matmul_mx(
                         out=y[:],
-                        lhsT=g_w[c, s][:, b * P:(b + 1) * P].bitcast(E5M2),
+                        lhsT=g_w[j, s].bitcast(E5M2),
                         lhsT_scale=g_sc[j][s],
                         rhs=w2_w[x].bitcast(E4M3),
                         rhs_scale=w2_sc[:, x * H:(x + 1) * H],
@@ -180,13 +181,12 @@ def tile_moe_sub_relu_kernel(tc, dy_words, dy_scales, w2t_words, w2t_scales, w1t
                 nc.gpsimd.tensor_scalar(spare, signs, 1.0, 0.0, ALU.min, ALU.max)
 
         make_piece(0)
-        make_sign(1, 0, QUARTER, "dh0")
-        gather_bytes(2, "both0")
+        make_sign(1, 0, QUARTER, "dh1")
+        warm_scales = gather_bytes(2, "both0")
         a_last = last.tile([P, 2 * T], F32, name="a_last", offset=0)
         for h in range(2):
             load_a(a_last, 0, h)
-        for s in range(PASSES):
-            gather_words(3, s)
+        warm_words = gather_words(0, C, E * C, "words_b", T)
         for u in range(2):
             scatter(u, 0, PIECE)
         make_piece(1)
@@ -208,6 +208,8 @@ def tile_moe_sub_relu_kernel(tc, dy_words, dy_scales, w2t_words, w2t_scales, w1t
         scatter(0, 3 * PIECE, PIECE)
 
         views = [window[u][:].bitcast(BF16).rearrange("p (u t e) -> p t u e", u=2, e=2) for u in range(2)]
+        w1_w = keep.tile([P, K], U32, name="w1_w", tag="pairs", align_bytes=64)
+        w1_sc = keep.tile([P, K], U8, name="w1_sc", align_bytes=64)
         da = keep.tile([P, T, 2, 2], BF16, name="da", align_bytes=64)
         da_w = keep.tile([P, T], U32, name="da_w", align_bytes=64)
         da_sc = keep.tile([P, T], U8, name="da_sc", align_bytes=64)
@@ -217,29 +219,34 @@ def tile_moe_sub_relu_kernel(tc, dy_words, dy_scales, w2t_words, w2t_scales, w1t
             nc.vector.quantize_mx(out=da_w[:, tokens].bitcast(E5M2), scales=da_sc[:, tokens],
                                   in_=da[:, tokens, :, :].rearrange("p t u e -> p (t u e)"))
 
-        def finish(first, new):
-            tokens = slice(first, first + HALF)
-            fresh = slice(HALF - new, HALF)
+        def finish(h):
+            tokens = slice(h * HALF, (h + 1) * HALF)
             for kb in range(K // P):
                 cols = slice(kb * P, (kb + 1) * P)
-                acc = bank(first // P + kb)
+                acc = bank(2 * h + kb)
                 nc.tensor.matmul_mx(
                     out=acc[:], lhsT=w1_w[:, cols].bitcast(E4M3), lhsT_scale=w1_sc[:, cols],
                     rhs=da_w[:, tokens].bitcast(E5M2), rhs_scale=da_sc[:, tokens], start=True, stop=True)
-                res = keep.tile([P, new], F32, name="res%d_%d" % (first, kb))
-                if first == HALF and kb == 1:
-                    nc.vector.tensor_copy(res[:], acc[:, fresh])
-                else:
-                    nc.scalar.copy(res[:], acc[:, fresh])
-                nc.sync.dma_start(out[cols, first + HALF - new:first + HALF], res[:])
+                res = keep.tile([P, HALF], F32, name="res%d_%d" % (h, kb))
+                for g in range(2):
+                    part = slice(g * QUARTER, (g + 1) * QUARTER)
+                    rows = out[cols, h * HALF + g * QUARTER:h * HALF + (g + 1) * QUARTER]
+                    if h == 1 and kb == 1:
+                        nc.vector.tensor_copy(res[:, part], acc[:, part])
+                    else:
+                        nc.scalar.copy(res[:, part], acc[:, part])
+                    (nc.scalar if (h, kb) == (1, 0) else nc.sync).dma_start(rows, res[:, part])
 
-        for g in range(T // QUARTER):
-            tokens = slice(g * QUARTER, (g + 1) * QUARTER)
-            nc.vector.tensor_tensor(da[:, tokens, :, :], views[0][:, tokens, :, :], views[1][:, tokens, ::-1, :], ALU.mult)
-            if g > 0:
-                quantise(g - 1)
-            if g == 2:
-                finish(0, HALF)
-        finish(QUARTER, QUARTER)
-        quantise(T // QUARTER - 1)
-        finish(HALF, QUARTER)
+        nc.vector.quantize_mx(out=w1_w[:].bitcast(E4M3), scales=w1_sc[:], in_=w1_bf[:].rearrange("p k j -> p (k j)"))
+        for kb in range(K // P):
+            cols = slice(kb * P, (kb + 1) * P)
+            nc.tensor.matmul_mx(
+                out=bank(4 + kb)[:], lhsT=w1_w[:, cols].bitcast(E4M3), lhsT_scale=w1_sc[:, cols],
+                rhs=warm_words.bitcast(E5M2), rhs_scale=warm_scales, start=True, stop=True)
+        for h in range(2):
+            for g in (2 * h, 2 * h + 1):
+                tokens = slice(g * QUARTER, (g + 1) * QUARTER)
+                nc.vector.tensor_tensor(da[:, tokens, :, :], views[0][:, tokens, :, :], views[1][:, tokens, ::-1, :], ALU.mult)
+            for g in (2 * h, 2 * h + 1):
+                quantise(g)
+            finish(h)

@@ -134,7 +134,7 @@ def tile_moe_sub_relu_kernel(tc, dy_words, dy_scales, w2t_words, w2t_scales, w1t
             for b in range(PIECE // P):
                 j = c * PIECE // P + b
                 e = j * P // C
-                y = bank(j if j < 2 else 1 + j % 2)
+                y = bank(j if j < 2 else 1 + (j - 2) % 3)
                 for s in range(PASSES):
                     x = e * PASSES + s
                     nc.tensor.matmul_mx(
@@ -165,23 +165,21 @@ def tile_moe_sub_relu_kernel(tc, dy_words, dy_scales, w2t_words, w2t_scales, w1t
             nc.vector.tensor_copy(window[u][:].indirect(entries(first, count)),
                                   pairs[:, u * E * C + first:u * E * C + first + count])
 
-        sign = {}
-
-        def make_sign(u, first, count, holder):
+        def take_sign(into, u, first):
             h, o = divmod(first, HALF)
-            sign[u, first] = keep.tile([P, count, 2], BF16, name="sign%d_%d" % (u, first), tag=holder, align_bytes=64)
-            nc.scalar.activation(sign[u, first][:], a_raw[u, h][:, :, o:o + count].rearrange("p e t -> p t e"), ACT.Sign)
+            nc.scalar.activation(into, a_raw[u, h][:, :, o:o + into.shape[1]].rearrange("p e t -> p t e"), ACT.Sign)
+            return into
 
-        def make_mask(u, first, on_scalar=False):
-            signs = sign[u, first][:].rearrange("p t e -> p (t e)")
-            spare = window[1 - u][:, T + first:T + first + signs.shape[1] // 2].bitcast(BF16)
-            if on_scalar:
-                nc.scalar.activation(spare, signs, ACT.Relu)
+        def make_mask(u, first, sign):
+            spare = window[1 - u][:, T + first:T + first + sign.shape[1]].bitcast(BF16)
+            if (u, first) == (0, HALF):
+                nc.scalar.activation(spare, sign.rearrange("p t e -> p (t e)"), ACT.Relu)
             else:
-                nc.gpsimd.tensor_scalar(spare, signs, 1.0, 0.0, ALU.min, ALU.max)
+                nc.gpsimd.tensor_scalar(spare, sign.rearrange("p t e -> p (t e)"), 1.0, 0.0, ALU.min, ALU.max)
 
         make_piece(0)
-        make_sign(1, 0, QUARTER, "dh1")
+        early_signs = keep.tile([P, QUARTER, 2], BF16, name="early_signs", tag="dh1", align_bytes=64)
+        take_sign(early_signs[:], 1, 0)
         warm_scales = gather_bytes(2, "both0")
         a_last = last.tile([P, 2 * T], F32, name="a_last", offset=0)
         for h in range(2):
@@ -190,21 +188,20 @@ def tile_moe_sub_relu_kernel(tc, dy_words, dy_scales, w2t_words, w2t_scales, w1t
         for u in range(2):
             scatter(u, 0, PIECE)
         make_piece(1)
-        make_sign(1, QUARTER, QUARTER, "dh2")
         for u in range(2):
             scatter(u, PIECE, PIECE)
         make_piece(2)
-        make_sign(1, HALF, HALF, "dh4")
         scatter(0, 2 * PIECE, PIECE)
-        for first in (0, QUARTER, HALF):
-            make_mask(1, first)
-        scatter(1, 2 * PIECE, PIECE)
         make_piece(3)
-        scatter(1, 3 * PIECE, PIECE)
-        make_sign(0, 0, HALF, "dh6")
-        make_sign(0, HALF, HALF, "dh7")
-        make_mask(0, 0)
-        make_mask(0, HALF, on_scalar=True)
+
+        signs = keep.tile([P, 2 * T - QUARTER, 2], BF16, name="signs", tag="dh7", align_bytes=64)
+        make_mask(1, 0, early_signs[:])
+        make_mask(1, QUARTER, take_sign(signs[:, 0:QUARTER, :], 1, QUARTER))
+        make_mask(1, HALF, take_sign(signs[:, QUARTER:QUARTER + HALF, :], 1, HALF))
+        scatter(1, 2 * PIECE, 2 * PIECE)
+        for h in range(2):
+            first = QUARTER + (h + 1) * HALF
+            make_mask(0, h * HALF, take_sign(signs[:, first:first + HALF, :], 0, h * HALF))
         scatter(0, 3 * PIECE, PIECE)
 
         views = [window[u][:].bitcast(BF16).rearrange("p (u t e) -> p t u e", u=2, e=2) for u in range(2)]

@@ -51,9 +51,9 @@ def tile_moe_sub_relu_kernel(tc, dy_words, dy_scales, w2t_words, w2t_scales, w1t
         gate_rows = late.tile([P, P], F32, name="gate_rows", offset=W2_BYTES - 2 * P)
         ident = keep.tile([P, P], F32, name="ident")
         nc.gpsimd.memset(dy_sc[:].bitcast(I32), 0)
+        nc.gpsimd.memset(gate_rows[:], 0.0)
         nc.gpsimd.memset(w2_sc[:].bitcast(I32), 0)
         make_identity(nc, ident[:])
-        nc.vector.memset(gate_rows[:], 0.0)
         for tile in moved:
             nc.vector.memset(tile[:].bitcast(I32), 0)
 
@@ -147,10 +147,11 @@ def tile_moe_sub_relu_kernel(tc, dy_words, dy_scales, w2t_words, w2t_scales, w1t
                         stop=(s == PASSES - 1),
                     )
                 dh = keep.tile([P, H], BF16, name="dh%d" % j, tag="dh%d" % j, align_bytes=64)
-                nc.scalar.activation(
-                    dh[:].rearrange("p (u q e) -> p u q e", u=2, e=2),
-                    y[:].rearrange("p (q u e) -> p u q e", u=2, e=2),
-                    ACT.Copy, scale=gate_col[:, j:j + 1])
+                for planes in ((slice(0, 1), slice(1, 2)) if j == 1 else (slice(0, 2),)):
+                    nc.scalar.activation(
+                        dh[:].rearrange("p (u q e) -> p u q e", u=2, e=2)[:, planes, :, :],
+                        y[:].rearrange("p (q u e) -> p u q e", u=2, e=2)[:, planes, :, :],
+                        ACT.Copy, scale=gate_col[:, j:j + 1])
                 for u in range(2):
                     nc.tensor.transpose(turned[u][:, b * P:(b + 1) * P], dh[:].bitcast(F32)[:, u * P:(u + 1) * P], ident[:])
             if c == 0:

@@ -60,7 +60,7 @@ def tile_moe_sub_relu_kernel(tc, dy_words, dy_scales, w2t_words, w2t_scales, w1t
         w2_w = [keep.tile([P, H], I32, name="w2_w%d" % s, align_bytes=64) for s in range(PASSES)]
         nc.sync.dma_start(w2_w[0][:], w2t_words[0, 0].rearrange("p i d -> p (i d)").bitcast(I32))
         for q in range(4):
-            (nc.sync if q % 2 == 0 else nc.scalar).dma_start(dy_sc[32 * q:32 * q + 4 * PASSES, :].bitcast(I32), dy_scales.bitcast(I32)[:, 4 * q:4 * q + 4, :])
+            nc.sync.dma_start(dy_sc[32 * q:32 * q + 4 * PASSES, :].bitcast(I32), dy_scales.bitcast(I32)[:, 4 * q:4 * q + 4, :])
         nc.sync.dma_start(gate_rows[0:E * C // P, :], gate[0].rearrange("(c p) -> c p", p=P))
         dy_w = keep.tile([P, PASSES * T], I32, name="dy_w", align_bytes=64)
         for s in range(PASSES):

@@ -181,11 +181,11 @@ def tile_moe_sub_relu_kernel(tc, dy_words, dy_scales, w2t_words, w2t_scales, w1t
         make_piece(0)
         early_signs = keep.tile([P, QUARTER, 2], BF16, name="early_signs", tag="dh1", align_bytes=64)
         take_sign(early_signs[:], 1, 0)
-        warm_scales = gather_bytes(2, "both0")
+        gather_bytes(2, "both0")
         a_last = last.tile([P, 2 * T], F32, name="a_last", offset=0)
         for h in range(2):
             load_a(a_last, 0, h)
-        warm_words = gather_words(0, C, E * C, "words_b", T)
+        gather_words(0, C, E * C, "words_b", T)
         for u in range(2):
             scatter(u, 0, PIECE)
         make_piece(1)
@@ -217,34 +217,27 @@ def tile_moe_sub_relu_kernel(tc, dy_words, dy_scales, w2t_words, w2t_scales, w1t
             nc.vector.quantize_mx(out=da_w[:, tokens].bitcast(E5M2), scales=da_sc[:, tokens],
                                   in_=da[:, tokens, :, :].rearrange("p t u e -> p (t u e)"))
 
-        def finish(h):
-            tokens = slice(h * HALF, (h + 1) * HALF)
+        def finish(g):
+            tokens = slice(g * QUARTER, (g + 1) * QUARTER)
             for kb in range(K // P):
                 cols = slice(kb * P, (kb + 1) * P)
-                acc = bank(2 * h + kb)
+                acc = bank(2 * g + kb)[:, 0:QUARTER]
                 nc.tensor.matmul_mx(
-                    out=acc[:], lhsT=w1_w[:, cols].bitcast(E4M3), lhsT_scale=w1_sc[:, cols],
+                    out=acc, lhsT=w1_w[:, cols].bitcast(E4M3), lhsT_scale=w1_sc[:, cols],
                     rhs=da_w[:, tokens].bitcast(E5M2), rhs_scale=da_sc[:, tokens], start=True, stop=True)
-                res = keep.tile([P, HALF], F32, name="res%d_%d" % (h, kb))
-                for g in range(2):
-                    part = slice(g * QUARTER, (g + 1) * QUARTER)
-                    rows = out[cols, h * HALF + g * QUARTER:h * HALF + (g + 1) * QUARTER]
-                    if h == 1 and kb == 1:
-                        nc.vector.tensor_copy(res[:, part], acc[:, part])
-                    else:
-                        nc.scalar.copy(res[:, part], acc[:, part])
-                    (nc.scalar if (h, kb) == (1, 0) else nc.sync).dma_start(rows, res[:, part])
+                res = keep.tile([P, QUARTER], F32, name="res%d_%d" % (g, kb))
+                if g >= 2 and kb == 1:
+                    nc.vector.tensor_copy(res[:], acc)
+                else:
+                    nc.scalar.copy(res[:], acc)
+                (nc.scalar if (g, kb) == (3, 0) else nc.sync).dma_start(out[cols, tokens], res[:])
 
         nc.vector.quantize_mx(out=w1_w[:].bitcast(E4M3), scales=w1_sc[:], in_=w1_bf[:].rearrange("p k j -> p (k j)"))
-        for kb in range(K // P):
-            cols = slice(kb * P, (kb + 1) * P)
-            nc.tensor.matmul_mx(
-                out=bank(4 + kb)[:], lhsT=w1_w[:, cols].bitcast(E4M3), lhsT_scale=w1_sc[:, cols],
-                rhs=warm_words.bitcast(E5M2), rhs_scale=warm_scales, start=True, stop=True)
         for h in range(2):
             for g in (2 * h, 2 * h + 1):
                 tokens = slice(g * QUARTER, (g + 1) * QUARTER)
                 nc.vector.tensor_tensor(da[:, tokens, :, :], views[0][:, tokens, :, :], views[1][:, tokens, ::-1, :], ALU.mult)
             for g in (2 * h, 2 * h + 1):
                 quantise(g)
-            finish(h)
+            for g in (2 * h, 2 * h + 1):
+                finish(g)

@@ -19,13 +19,20 @@ ALU = mybir.AluOpType
 
 P = 128
 PASSES = N // 512
+SLOTS = E * C
 PIECE = 256
-PIECES = E * C // PIECE
+PIECES = SLOTS // PIECE
 W2_BYTES = 4 * PASSES * H
 HALF = 512
 QUARTER = 256
 SCALE_ROWS = 100
-BYTE_CUTS = ((0, PIECE), (PIECE, C), (C, E * C))
+BYTE_CUTS = ((0, PIECE), (PIECE, 5 * P), (5 * P, SLOTS))
+OVERLAP = 64
+PRODUCT_BANKS = (0, 1, 3, 0, 1, 3, 0, 1)
+LATE_BYTES = 4 * PASSES * (SLOTS - PIECE)
+TURNED_BANKS = (2, 4, 5, 6)
+DH_BUFFERS = (0, 1, 2, 3, 4, 3, 6, 3)
+TINY = 2.0 ** -126
 
 
 def tile_moe_sub_relu_kernel(tc, dy_words, dy_scales, w2t_words, w2t_scales, w1t, a, gate, offs, out):
@@ -39,16 +46,16 @@ def tile_moe_sub_relu_kernel(tc, dy_words, dy_scales, w2t_words, w2t_scales, w1t
         def bank(n):
             return psum.tile([P, HALF], F32, name="bank%d" % n, tag="bank%d" % n)
 
-        offsets = keep.tile([P, E * C // 16], U16, name="offsets")
+        offsets = keep.tile([P, SLOTS // 16], U16, name="offsets")
         nc.sync.dma_start(offsets[:], offs)
 
         def entries(first, count):
             return offsets[:, first // 16:(first + count) // 16]
 
-        dy_sc = last.tile([P, T], U8, name="dy_sc", offset=0)
+        dy_sc = last.tile([P, T], U8, name="dy_sc", offset=LATE_BYTES - T // 2, align_bytes=64)
         w2_sc = keep.tile([P, E * PASSES * H], U8, name="w2_sc", align_bytes=64)
-        moved = [keep.tile([P, hi - lo], U8, name="moved%d" % lo, tag="moved%d" % lo, align_bytes=64) for lo, hi in BYTE_CUTS]
-        gate_rows = late.tile([P, P], F32, name="gate_rows", offset=W2_BYTES - 2 * P)
+        moved = [keep.tile([P, hi - lo], U8, name="moved%d" % lo, align_bytes=64) for lo, hi in BYTE_CUTS]
+        gate_rows = late.tile([P, P], F32, name="gate_rows", offset=W2_BYTES - OVERLAP, align_bytes=64)
         ident = keep.tile([P, P], F32, name="ident")
         nc.gpsimd.memset(dy_sc[:].bitcast(I32), 0)
         nc.gpsimd.memset(gate_rows[:], 0.0)
@@ -57,153 +64,179 @@ def tile_moe_sub_relu_kernel(tc, dy_words, dy_scales, w2t_words, w2t_scales, w1t
         for tile in moved:
             nc.vector.memset(tile[:].bitcast(I32), 0)
 
+        window = [keep.tile([P, 2 * T], F32, name="window%d" % u) for u in range(2)]
+        single = [keep.tile([P, T], F32, name="single%d" % e) for e in range(2)]
+        for e in range(2):
+            nc.gpsimd.memset(single[e][:], 1.0)
+        nc.gpsimd.memset(window[1][:, 0:T].bitcast(BF16), 1.0)
+
         w2_w = [keep.tile([P, H], I32, name="w2_w%d" % s, align_bytes=64) for s in range(PASSES)]
         nc.sync.dma_start(w2_w[0][:], w2t_words[0, 0].rearrange("p i d -> p (i d)").bitcast(I32))
         for q in range(4):
             nc.sync.dma_start(dy_sc[32 * q:32 * q + 4 * PASSES, :].bitcast(I32), dy_scales.bitcast(I32)[:, 4 * q:4 * q + 4, :])
-        nc.sync.dma_start(gate_rows[0:E * C // P, :], gate[0].rearrange("(c p) -> c p", p=P))
         dy_w = keep.tile([P, PASSES * T], I32, name="dy_w", align_bytes=64)
         for s in range(PASSES):
             nc.sync.dma_start(dy_w[:, s * T:(s + 1) * T], dy_words[s].rearrange("p t d -> p (t d)").bitcast(I32))
+            if s == 0:
+                nc.sync.dma_start(gate_rows[0:SLOTS // P, :], gate[0].rearrange("(c p) -> c p", p=P))
         w2_sc_src = w2t_scales.bitcast(I32).rearrange("e s (q r) w -> r q (e s) w", r=4)
         for r in range(4):
             nc.sync.dma_start(w2_sc[r:P:32, :].bitcast(I32).rearrange("q (x w) -> q x w", x=E * PASSES), w2_sc_src[r])
-
         nc.sync.dma_start(w2_w[1][:], w2t_words[0, 1].rearrange("p i d -> p (i d)").bitcast(I32))
 
         gate_ps = bank(7)
         nc.tensor.transpose(gate_ps[:, 0:P], gate_rows[:], ident[:])
-        gate_col = keep.tile([P, E * C // P], F32, name="gate_col")
-        nc.scalar.copy(gate_col[:], gate_ps[:, 0:E * C // P])
+        gate_col = keep.tile([P, SLOTS // P], F32, name="gate_col")
+        nc.scalar.copy(gate_col[:], gate_ps[:, 0:SLOTS // P])
 
         g_sc = {}
 
-        def gather_bytes(n, holder):
+        def gather_bytes(n, both):
             lo, hi = BYTE_CUTS[n]
-            both = keep.tile([P, hi - lo], U8, name="both%d" % lo, tag=holder, align_bytes=64)
             nc.vector.tensor_copy(both[:], dy_sc[:].indirect(entries(lo, hi - lo)))
             nc.sync.dma_start(moved[n][0:SCALE_ROWS, :].bitcast(I32), both[4:SCALE_ROWS + 4, :].bitcast(I32))
             for j in range(lo // P, hi // P):
                 g_sc[j] = [tile[:, j * P - lo:(j + 1) * P - lo] for tile in (both, moved[n])]
-            return both[:]
-
-        for n in range(2):
-            gather_bytes(n, "both%d" % n)
-
-        a_rows = a.rearrange("(p u e) t -> u p e t", u=2, e=2)
-        floats = late.tile([P, 2 * T + 4 * K], F32, name="floats", offset=W2_BYTES)
-        a_raw = {}
-
-        def load_a(tile, u, h):
-            a_raw[u, h] = tile[:, h * T:(h + 1) * T].rearrange("p (e t) -> p e t", e=2)
-            nc.sync.dma_start(a_raw[u, h], a_rows[u][:, :, h * HALF:(h + 1) * HALF])
-
-        load_a(floats, 1, 0)
-        w1_raw = floats[:, 2 * T:].rearrange("p (j k) -> p j k", j=4)
-        nc.sync.dma_start(w1_raw, w1t.rearrange("(p j) k -> p j k", j=4))
-        w2_late = late.tile([P, PASSES, H], I32, name="w2_late", offset=0, align_bytes=64)
-        nc.sync.dma_start(w2_late[:], w2t_words[1].rearrange("s p i d -> p s (i d)").bitcast(I32))
-        w2_w = [tile[:] for tile in w2_w] + [w2_late[:, s, :] for s in range(PASSES)]
-        load_a(floats, 1, 1)
 
         g_w = {}
 
-        def gather_words(s, lo, hi, holder, end):
-            words = keep.tile([P, hi - lo], U32, name="g_w%d_%d" % (s, lo), tag=holder, align_bytes=64)
-            nc.vector.tensor_copy(words[:], dy_w[:, s * T:end].bitcast(U32).indirect(entries(lo, hi - lo)))
+        def gather_words(s, lo, hi, words):
+            end = T if (s, lo) == (0, 0) else PASSES * T
+            nc.vector.tensor_copy(words, dy_w[:, s * T:end].bitcast(U32).indirect(entries(lo, hi - lo)))
             for j in range(lo // P, hi // P):
                 g_w[j, s] = words[:, j * P - lo:(j + 1) * P - lo]
-            return words[:]
 
-        gather_words(0, 0, C, "words_a", T)
-        gather_words(1, 0, PIECE, "words_b", PASSES * T)
-        gather_words(1, PIECE, E * C, "words_c", PASSES * T)
+        a_rows = a.rearrange("(p u e) t -> u p e t", u=2, e=2)
 
-        w1_bf = keep.tile([P, K, 4], BF16, name="w1_bf", align_bytes=64)
-        nc.gpsimd.tensor_scalar(w1_bf[:], w1_raw.rearrange("p j k -> p k j"), 1.0, 0.0, ALU.mult, ALU.add)
+        def load_half(tile, h):
+            nc.sync.dma_start(tile[:].rearrange("p (e t) -> p e t", e=2), a_rows[0][:, :, h * HALF:(h + 1) * HALF])
 
-        window = [keep.tile([P, 2 * T], F32, name="window%d" % u) for u in range(2)]
-        pairs = keep.tile([P, 2 * E * C], F32, name="pairs", tag="pairs", align_bytes=64)
+        for n in range(2):
+            gather_bytes(n, keep.tile([P, BYTE_CUTS[n][1] - BYTE_CUTS[n][0]], U8, name="both%d" % n, tag="both%d" % n, align_bytes=64))
 
-        def make_piece(c):
-            if c == 0:
-                turned = [bank(2 + u)[:, 0:PIECE] for u in range(2)]
-            else:
-                both_planes = bank(3 + c)
-                turned = [both_planes[:, u * PIECE:(u + 1) * PIECE] for u in range(2)]
-            for b in range(PIECE // P):
-                j = c * PIECE // P + b
-                e = j * P // C
-                y = bank(j if j < 2 else 1 + (j - 2) % 3)
-                for s in range(PASSES):
-                    x = e * PASSES + s
-                    nc.tensor.matmul_mx(
-                        out=y[:],
-                        lhsT=g_w[j, s].bitcast(E5M2),
-                        lhsT_scale=g_sc[j][s],
-                        rhs=w2_w[x].bitcast(E4M3),
-                        rhs_scale=w2_sc[:, x * H:(x + 1) * H],
-                        start=(s == 0),
-                        stop=(s == PASSES - 1),
-                    )
-                dh = keep.tile([P, H], BF16, name="dh%d" % j, tag="dh%d" % j, align_bytes=64)
-                for planes in ((slice(0, 1), slice(1, 2)) if j == 1 else (slice(0, 2),)):
-                    nc.scalar.activation(
-                        dh[:].rearrange("p (u q e) -> p u q e", u=2, e=2)[:, planes, :, :],
-                        y[:].rearrange("p (q u e) -> p u q e", u=2, e=2)[:, planes, :, :],
-                        ACT.Copy, scale=gate_col[:, j:j + 1])
-                for u in range(2):
-                    nc.tensor.transpose(turned[u][:, b * P:(b + 1) * P], dh[:].bitcast(F32)[:, u * P:(u + 1) * P], ident[:])
-            if c == 0:
-                for u in range(2):
-                    nc.scalar.copy(pairs[:, u * E * C:u * E * C + PIECE], turned[u])
-            else:
-                nc.scalar.copy(
-                    pairs[:].rearrange("p (u j) -> p u j", u=2)[:, :, c * PIECE:(c + 1) * PIECE],
-                    both_planes[:].rearrange("p (u j) -> p u j", u=2))
+        def early_words(s, lo):
+            return keep.tile([P, PIECE], U32, name="words%d_%d" % (s, lo), tag="words%d_%d" % (s, lo), align_bytes=64)[:]
+
+        gather_words(0, 0, PIECE, early_words(0, 0))
+        a_first = [late.tile([P, T], F32, name="a_first0", offset=W2_BYTES + 3 * P, align_bytes=64)]
+        load_half(a_first[0], 0)
+        w2_late = late.tile([P, PASSES, H], I32, name="w2_late", offset=0, align_bytes=64)
+        nc.sync.dma_start(w2_late[:], w2t_words[1].rearrange("s p i d -> p s (i d)").bitcast(I32))
+        w2_w = [tile[:] for tile in w2_w] + [w2_late[:, s, :] for s in range(PASSES)]
+        gather_bytes(2, late.tile([P, 3 * P], U8, name="both2", offset=W2_BYTES, align_bytes=64))
+        a_first.append(last.tile([P, T], F32, name="a_first1", offset=LATE_BYTES, align_bytes=64))
+        load_half(a_first[1], 1)
+        gather_words(1, 0, PIECE, early_words(1, 0))
+        rest = SLOTS - PIECE
+        late_words = last.tile([P, PASSES * rest], U32, name="late_words", offset=0, align_bytes=64)
+        for lo in range(PIECE, SLOTS, PIECE):
+            hi = lo + PIECE
+            for s in reversed(range(PASSES)):
+                gather_words(s, lo, hi, late_words[:, s * rest + lo - PIECE:s * rest + hi - PIECE])
+
+        for h in range(2):
+            clamped = keep.tile([P, T], BF16, name="clamped0_%d" % h, align_bytes=64)
+            nc.gpsimd.tensor_scalar(clamped[:], a_first[h][:], TINY, 0.0, ALU.min, ALU.max)
+            spare = window[1][:, T + h * HALF:T + (h + 1) * HALF].bitcast(BF16).rearrange("p (t e) -> p t e", e=2)
+            nc.gpsimd.tensor_scalar(spare, clamped[:].rearrange("p (e t) -> p t e", e=2), 1.0 / TINY, 0.0, ALU.mult, ALU.add)
+
+        pairs = keep.tile([P, 2 * SLOTS], F32, name="pairs", tag="pairs", align_bytes=64)
+
+        def product(j):
+            y = bank(PRODUCT_BANKS[j])
+            e = j * P // C
+            order = range(PASSES) if j < PIECE // P else reversed(range(PASSES))
+            for n, s in enumerate(order):
+                x = e * PASSES + s
+                nc.tensor.matmul_mx(
+                    out=y[:],
+                    lhsT=g_w[j, s].bitcast(E5M2),
+                    lhsT_scale=g_sc[j][s],
+                    rhs=w2_w[x].bitcast(E4M3),
+                    rhs_scale=w2_sc[:, x * H:(x + 1) * H],
+                    start=(n == 0),
+                    stop=(n == PASSES - 1),
+                )
+            return y[:].rearrange("p (q u e) -> p u q e", u=2, e=2)
 
         def scatter(u, first, count):
             nc.vector.tensor_copy(window[u][:].indirect(entries(first, count)),
-                                  pairs[:, u * E * C + first:u * E * C + first + count])
+                                  pairs[:, u * SLOTS + first:u * SLOTS + first + count])
 
-        def take_sign(into, u, first):
-            h, o = divmod(first, HALF)
-            nc.scalar.activation(into, a_raw[u, h][:, :, o:o + into.shape[1]].rearrange("p e t -> p t e"), ACT.Sign)
-            return into
+        def scatter_single(e, first, count, values):
+            nc.scalar.activation(single[e][:].indirect(entries(first, count)), values, ACT.Copy)
 
-        def make_mask(u, first, sign):
-            spare = window[1 - u][:, T + first:T + first + sign.shape[1]].bitcast(BF16)
-            if (u, first) == (0, HALF):
-                nc.scalar.activation(spare, sign.rearrange("p t e -> p (t e)"), ACT.Relu)
-            else:
-                nc.gpsimd.tensor_scalar(spare, sign.rearrange("p t e -> p (t e)"), 1.0, 0.0, ALU.min, ALU.max)
+        turned = {}
+        dh = {}
 
-        make_piece(0)
-        early_signs = keep.tile([P, QUARTER, 2], BF16, name="early_signs", tag="dh1", align_bytes=64)
-        take_sign(early_signs[:], 1, 0)
-        gather_bytes(2, "both0")
-        a_last = last.tile([P, 2 * T], F32, name="a_last", offset=0)
-        for h in range(2):
-            load_a(a_last, 0, h)
-        gather_words(0, C, E * C, "words_b", T)
-        for u in range(2):
-            scatter(u, 0, PIECE)
-        make_piece(1)
-        for u in range(2):
-            scatter(u, PIECE, PIECE)
-        make_piece(2)
-        scatter(0, 2 * PIECE, PIECE)
-        make_piece(3)
+        def turn(j, u):
+            c = j * P // PIECE
+            if c not in turned:
+                turned[c] = bank(TURNED_BANKS[c])
+            first = u * PIECE + j * P % PIECE
+            nc.tensor.transpose(turned[c][:, first:first + P], dh[j][:].bitcast(F32)[:, u * P:(u + 1) * P], ident[:])
 
-        signs = keep.tile([P, 2 * T - QUARTER, 2], BF16, name="signs", tag="dh7", align_bytes=64)
-        make_mask(1, 0, early_signs[:])
-        make_mask(1, QUARTER, take_sign(signs[:, 0:QUARTER, :], 1, QUARTER))
-        make_mask(1, HALF, take_sign(signs[:, QUARTER:QUARTER + HALF, :], 1, HALF))
-        scatter(1, 2 * PIECE, 2 * PIECE)
-        for h in range(2):
-            first = QUARTER + (h + 1) * HALF
-            make_mask(0, h * HALF, take_sign(signs[:, first:first + HALF, :], 0, h * HALF))
-        scatter(0, 3 * PIECE, PIECE)
+        def gate_block(j):
+            y = product(j)
+            dh[j] = keep.tile([P, H], BF16, name="dh%d" % j, tag="dh%d" % DH_BUFFERS[j], align_bytes=64)
+            nc.scalar.activation(dh[j][:].rearrange("p (u q e) -> p u q e", u=2, e=2), y, ACT.Copy, scale=gate_col[:, j:j + 1])
+
+        def take_pairs(c):
+            nc.scalar.copy(
+                pairs[:].rearrange("p (u j) -> p u j", u=2)[:, :, c * PIECE:(c + 1) * PIECE],
+                turned[c][:].rearrange("p (u j) -> p u j", u=2))
+
+        y = product(0)
+        dh[0] = keep.tile([P, 2 * P], BF16, name="dh0", tag="dh0", align_bytes=64)
+        dh_single = keep.tile([P, 2, P], F32, name="dh_single", align_bytes=64)
+        nc.scalar.activation(dh[0][:].rearrange("p (q e) -> p q e", e=2), y[:, 0, :, :], ACT.Copy, scale=gate_col[:, 0:1])
+        nc.scalar.activation(dh_single[:], y[:, 1, :, :].rearrange("p q e -> p e q"), ACT.Copy, scale=gate_col[:, 0:1])
+        turn(0, 0)
+        gate_block(1)
+        turn(1, 0)
+
+        a_second = keep.tile([P, 2 * T], F32, name="a_second", tag="both0", align_bytes=64)
+        for e in range(2):
+            nc.sync.dma_start(a_second[:, e * T:(e + 1) * T], a_rows[1][:, e, :])
+        w1_raw = keep.tile([P, 4, K], F32, name="w1_raw", tag="words1_0", align_bytes=64)
+        nc.sync.dma_start(w1_raw[:], w1t.rearrange("(p j) k -> p j k", j=4))
+        clamped1 = keep.tile([P, T], BF16, name="clamped1", align_bytes=64)
+        nc.gpsimd.tensor_scalar(clamped1[:], a_second[:, 0:T], TINY, 0.0, ALU.min, ALU.max)
+        mask1 = [keep.tile([P, T], BF16, name="mask1_0", align_bytes=64)]
+        nc.gpsimd.tensor_scalar(mask1[0][:], clamped1[:], 1.0 / TINY, 0.0, ALU.mult, ALU.add)
+
+        for c in range(1, PIECES):
+            for j in (2 * c, 2 * c + 1):
+                gate_block(j)
+                if j == 2:
+                    nc.scalar.copy(pairs[:, 0:PIECE], turned[0][:, 0:PIECE])
+                    scatter(0, 0, PIECE)
+                for u in range(2):
+                    turn(j, u)
+            take_pairs(c)
+            scatter(0, c * PIECE, PIECE)
+            if c == 1:
+                aside = bank(7)
+                for e in range(2):
+                    nc.tensor.transpose(aside[:, e * P:(e + 1) * P], dh_single[:, e, :], ident[:])
+                nc.tensor.transpose(aside[:, 2 * P:3 * P], dh[1][:].bitcast(F32)[:, P:2 * P], ident[:])
+
+        values = keep.tile([P, 2 * P], F32, name="values", tag="dh3", align_bytes=64)
+        nc.scalar.copy(values[:], aside[:, 0:2 * P])
+        nc.scalar.copy(pairs[:, SLOTS + P:SLOTS + PIECE], aside[:, 2 * P:3 * P])
+        for e in range(2):
+            scatter_single(e, 0, P, values[:, e * P:(e + 1) * P])
+        signs = keep.tile([P, T], BF16, name="signs", tag="dh3", align_bytes=64)
+        mask1.append(keep.tile([P, T], BF16, name="mask1_1", align_bytes=64))
+        nc.scalar.activation(signs[:], a_second[:, T:2 * T], ACT.Sign)
+        nc.scalar.activation(mask1[1][:], signs[:], ACT.Relu)
+        w1_bf = keep.tile([P, 4 * K], BF16, name="w1_bf", tag="dh3", align_bytes=64)[:]
+        nc.scalar.copy(w1_bf.rearrange("p (k j) -> p k j", j=4), w1_raw[:].rearrange("p j k -> p k j"))
+
+        scatter(1, P, SLOTS - P)
+        factor1 = window[0][:, T:2 * T].bitcast(BF16).rearrange("p (t e) -> p e t", e=2)
+        for e in range(2):
+            nc.gpsimd.tensor_tensor(factor1[:, e, :], single[e][:], mask1[e][:], ALU.mult)
 
         views = [window[u][:].bitcast(BF16).rearrange("p (u t e) -> p t u e", u=2, e=2) for u in range(2)]
         w1_w = keep.tile([P, K], U32, name="w1_w", tag="pairs", align_bytes=64)
@@ -232,7 +265,7 @@ def tile_moe_sub_relu_kernel(tc, dy_words, dy_scales, w2t_words, w2t_scales, w1t
                     nc.scalar.copy(res[:], acc)
                 (nc.scalar if (g, kb) == (3, 0) else nc.sync).dma_start(out[cols, tokens], res[:])
 
-        nc.vector.quantize_mx(out=w1_w[:].bitcast(E4M3), scales=w1_sc[:], in_=w1_bf[:].rearrange("p k j -> p (k j)"))
+        nc.vector.quantize_mx(out=w1_w[:].bitcast(E4M3), scales=w1_sc[:], in_=w1_bf)
         for h in range(2):
             for g in (2 * h, 2 * h + 1):
                 tokens = slice(g * QUARTER, (g + 1) * QUARTER)

@@ -28,10 +28,9 @@ QUARTER = 256
 SCALE_ROWS = 100
 BYTE_CUTS = ((0, PIECE), (PIECE, 5 * P), (5 * P, SLOTS))
 OVERLAP = 64
-PRODUCT_BANKS = (0, 1, 3, 0, 1, 3, 0, 1)
-LATE_BYTES = 4 * PASSES * (SLOTS - PIECE)
-TURNED_BANKS = (2, 4, 5, 6)
-DH_BUFFERS = (0, 1, 2, 3, 4, 3, 6, 3)
+PRODUCT_BANKS = (0, 1, 3, 1, 3, 3, 6, 2)
+LATE_BYTES = 4 * PASSES * C
+MASK_SPLIT = 768
 TINY = 2.0 ** -126
 
 
@@ -64,11 +63,11 @@ def tile_moe_sub_relu_kernel(tc, dy_words, dy_scales, w2t_words, w2t_scales, w1t
         for tile in moved:
             nc.vector.memset(tile[:].bitcast(I32), 0)
 
-        window = [keep.tile([P, 2 * T], F32, name="window%d" % u) for u in range(2)]
+        window = [keep.tile([P, (u + 1) * T], F32, name="window%d" % u, tag="window%d" % u, align_bytes=64) for u in range(2)]
         single = [keep.tile([P, T], F32, name="single%d" % e) for e in range(2)]
         for e in range(2):
             nc.gpsimd.memset(single[e][:], 1.0)
-        nc.gpsimd.memset(window[1][:, 0:T].bitcast(BF16), 1.0)
+        nc.scalar.activation(window[1][:, 0:T].bitcast(BF16), ident[:, 0:1].to_broadcast([P, 2 * T]), ACT.Copy, bias=1.0, scale=0.0)
 
         w2_w = [keep.tile([P, H], I32, name="w2_w%d" % s, align_bytes=64) for s in range(PASSES)]
         nc.sync.dma_start(w2_w[0][:], w2t_words[0, 0].rearrange("p i d -> p (i d)").bitcast(I32))
@@ -82,6 +81,9 @@ def tile_moe_sub_relu_kernel(tc, dy_words, dy_scales, w2t_words, w2t_scales, w1t
         w2_sc_src = w2t_scales.bitcast(I32).rearrange("e s (q r) w -> r q (e s) w", r=4)
         for r in range(4):
             nc.sync.dma_start(w2_sc[r:P:32, :].bitcast(I32).rearrange("q (x w) -> q x w", x=E * PASSES), w2_sc_src[r])
+        a_rows = a.rearrange("(p r) t -> r p t", r=4)
+        a_early = keep.tile([P, HALF], F32, name="a_early", align_bytes=64)
+        nc.sync.dma_start(a_early[:], a_rows[2][:, 0:HALF])
         nc.sync.dma_start(w2_w[1][:], w2t_words[0, 1].rearrange("p i d -> p (i d)").bitcast(I32))
 
         gate_ps = bank(7)
@@ -101,46 +103,43 @@ def tile_moe_sub_relu_kernel(tc, dy_words, dy_scales, w2t_words, w2t_scales, w1t
         g_w = {}
 
         def gather_words(s, lo, hi, words):
-            end = T if (s, lo) == (0, 0) else PASSES * T
-            nc.vector.tensor_copy(words, dy_w[:, s * T:end].bitcast(U32).indirect(entries(lo, hi - lo)))
+            nc.vector.tensor_copy(words, dy_w[:, s * T:(s + 1) * T].bitcast(U32).indirect(entries(lo, hi - lo)))
             for j in range(lo // P, hi // P):
                 g_w[j, s] = words[:, j * P - lo:(j + 1) * P - lo]
 
-        a_rows = a.rearrange("(p u e) t -> u p e t", u=2, e=2)
-
-        def load_half(tile, h):
-            nc.sync.dma_start(tile[:].rearrange("p (e t) -> p e t", e=2), a_rows[0][:, :, h * HALF:(h + 1) * HALF])
-
         for n in range(2):
             gather_bytes(n, keep.tile([P, BYTE_CUTS[n][1] - BYTE_CUTS[n][0]], U8, name="both%d" % n, tag="both%d" % n, align_bytes=64))
-
-        def early_words(s, lo):
-            return keep.tile([P, PIECE], U32, name="words%d_%d" % (s, lo), tag="words%d_%d" % (s, lo), align_bytes=64)[:]
-
-        gather_words(0, 0, PIECE, early_words(0, 0))
-        a_first = [late.tile([P, T], F32, name="a_first0", offset=W2_BYTES + 3 * P, align_bytes=64)]
-        load_half(a_first[0], 0)
+        gather_words(0, 0, C, keep.tile([P, C], U32, name="words0", align_bytes=64)[:])
+        a_first = late.tile([P, HALF + T], F32, name="a_first", offset=W2_BYTES + 3 * P, align_bytes=64)
+        nc.sync.dma_start(a_first[:, 0:HALF], a_rows[2][:, HALF:T])
+        nc.sync.dma_start(a_first[:, HALF:], a_rows[3])
         w2_late = late.tile([P, PASSES, H], I32, name="w2_late", offset=0, align_bytes=64)
         nc.sync.dma_start(w2_late[:], w2t_words[1].rearrange("s p i d -> p s (i d)").bitcast(I32))
         w2_w = [tile[:] for tile in w2_w] + [w2_late[:, s, :] for s in range(PASSES)]
+        gather_words(1, 0, C, keep.tile([P, C], U32, name="words1", align_bytes=64)[:])
         gather_bytes(2, late.tile([P, 3 * P], U8, name="both2", offset=W2_BYTES, align_bytes=64))
-        a_first.append(last.tile([P, T], F32, name="a_first1", offset=LATE_BYTES, align_bytes=64))
-        load_half(a_first[1], 1)
-        gather_words(1, 0, PIECE, early_words(1, 0))
-        rest = SLOTS - PIECE
-        late_words = last.tile([P, PASSES * rest], U32, name="late_words", offset=0, align_bytes=64)
-        for lo in range(PIECE, SLOTS, PIECE):
-            hi = lo + PIECE
-            for s in reversed(range(PASSES)):
-                gather_words(s, lo, hi, late_words[:, s * rest + lo - PIECE:s * rest + hi - PIECE])
+        a_second = last.tile([P, 2 * T], F32, name="a_second", offset=LATE_BYTES, align_bytes=64)
+        for e in range(2):
+            nc.sync.dma_start(a_second[:, e * T:(e + 1) * T], a_rows[e])
+        late_words = last.tile([P, LATE_BYTES // 4], U32, name="late_words", offset=0, align_bytes=64)
+        for s in reversed(range(PASSES)):
+            gather_words(s, C, SLOTS, late_words[:, s * C:(s + 1) * C])
 
-        for h in range(2):
-            clamped = keep.tile([P, T], BF16, name="clamped0_%d" % h, align_bytes=64)
-            nc.gpsimd.tensor_scalar(clamped[:], a_first[h][:], TINY, 0.0, ALU.min, ALU.max)
-            spare = window[1][:, T + h * HALF:T + (h + 1) * HALF].bitcast(BF16).rearrange("p (t e) -> p t e", e=2)
-            nc.gpsimd.tensor_scalar(spare, clamped[:].rearrange("p (e t) -> p t e", e=2), 1.0 / TINY, 0.0, ALU.mult, ALU.add)
+        clamped1 = keep.tile([P, 2 * T], BF16, name="clamped1", align_bytes=64)
+        mask1 = keep.tile([P, 2 * T], BF16, name="mask1", align_bytes=64)
 
-        pairs = keep.tile([P, 2 * SLOTS], F32, name="pairs", tag="pairs", align_bytes=64)
+        def finish_mask1(lo, hi):
+            nc.gpsimd.tensor_scalar(mask1[:, lo:hi], clamped1[:, lo:hi], 1.0 / TINY, 0.0, ALU.mult, ALU.add)
+
+        nc.gpsimd.tensor_scalar(clamped1[:, 0:HALF], a_early[:], TINY, 0.0, ALU.min, ALU.max)
+        finish_mask1(0, HALF)
+        nc.gpsimd.tensor_scalar(clamped1[:, HALF:T], a_first[:, 0:HALF], TINY, 0.0, ALU.min, ALU.max)
+        nc.gpsimd.tensor_scalar(clamped1[:, T:2 * T], a_first[:, HALF:], TINY, 0.0, ALU.min, ALU.max)
+        finish_mask1(HALF, 2 * T)
+        a_plane0 = a_second[:].rearrange("p (e t) -> p e t", e=2)
+        clamped0 = keep.tile([P, 2, MASK_SPLIT], BF16, name="clamped0", align_bytes=64)[:]
+        for e in range(2):
+            nc.gpsimd.tensor_scalar(clamped0[:, e, :], a_second[:, e * T:e * T + MASK_SPLIT], TINY, 0.0, ALU.min, ALU.max)
 
         def product(j):
             y = bank(PRODUCT_BANKS[j])
@@ -159,87 +158,83 @@ def tile_moe_sub_relu_kernel(tc, dy_words, dy_scales, w2t_words, w2t_scales, w1t
                 )
             return y[:].rearrange("p (q u e) -> p u q e", u=2, e=2)
 
-        def scatter(u, first, count):
-            nc.vector.tensor_copy(window[u][:].indirect(entries(first, count)),
-                                  pairs[:, u * SLOTS + first:u * SLOTS + first + count])
-
         def scatter_single(e, first, count, values):
             nc.scalar.activation(single[e][:].indirect(entries(first, count)), values, ACT.Copy)
 
-        turned = {}
-        dh = {}
+        pairs = [keep.tile([P, SLOTS], F32, name="pairs%d" % u, tag="pairs%d" % u, align_bytes=64) for u in range(2)]
 
-        def turn(j, u):
-            c = j * P // PIECE
-            if c not in turned:
-                turned[c] = bank(TURNED_BANKS[c])
-            first = u * PIECE + j * P % PIECE
-            nc.tensor.transpose(turned[c][:, first:first + P], dh[j][:].bitcast(F32)[:, u * P:(u + 1) * P], ident[:])
+        def scatter(u, first, end):
+            nc.vector.tensor_copy(window[u][:].indirect(entries(first * P, (end - first) * P)), pairs[u][:, first * P:end * P])
+
+        dh = {}
+        scratch = keep.tile([P, 4 * K], BF16, name="scratch", align_bytes=64)
 
         def gate_block(j):
             y = product(j)
-            dh[j] = keep.tile([P, H], BF16, name="dh%d" % j, tag="dh%d" % DH_BUFFERS[j], align_bytes=64)
-            nc.scalar.activation(dh[j][:].rearrange("p (u q e) -> p u q e", u=2, e=2), y, ACT.Copy, scale=gate_col[:, j:j + 1])
+            dh[j] = keep.tile([P, H], BF16, name="dh%d" % j, tag="dh%d" % j, align_bytes=64)[:] if j < 7 else scratch[:, 0:H]
+            nc.scalar.activation(dh[j].rearrange("p (u q e) -> p u q e", u=2, e=2), y, ACT.Copy, scale=gate_col[:, j:j + 1])
 
-        def take_pairs(c):
-            nc.scalar.copy(
-                pairs[:].rearrange("p (u j) -> p u j", u=2)[:, :, c * PIECE:(c + 1) * PIECE],
-                turned[c][:].rearrange("p (u j) -> p u j", u=2))
-
-        y = product(0)
-        dh[0] = keep.tile([P, 2 * P], BF16, name="dh0", tag="dh0", align_bytes=64)
-        dh_single = keep.tile([P, 2, P], F32, name="dh_single", align_bytes=64)
-        nc.scalar.activation(dh[0][:].rearrange("p (q e) -> p q e", e=2), y[:, 0, :, :], ACT.Copy, scale=gate_col[:, 0:1])
-        nc.scalar.activation(dh_single[:], y[:, 1, :, :].rearrange("p q e -> p e q"), ACT.Copy, scale=gate_col[:, 0:1])
-        turn(0, 0)
-        gate_block(1)
-        turn(1, 0)
-
-        a_second = keep.tile([P, 2 * T], F32, name="a_second", tag="both0", align_bytes=64)
-        for e in range(2):
-            nc.sync.dma_start(a_second[:, e * T:(e + 1) * T], a_rows[1][:, e, :])
-        w1_raw = keep.tile([P, 4, K], F32, name="w1_raw", tag="words1_0", align_bytes=64)
-        nc.sync.dma_start(w1_raw[:], w1t.rearrange("(p j) k -> p j k", j=4))
-        clamped1 = keep.tile([P, T], BF16, name="clamped1", align_bytes=64)
-        nc.gpsimd.tensor_scalar(clamped1[:], a_second[:, 0:T], TINY, 0.0, ALU.min, ALU.max)
-        mask1 = [keep.tile([P, T], BF16, name="mask1_0", align_bytes=64)]
-        nc.gpsimd.tensor_scalar(mask1[0][:], clamped1[:], 1.0 / TINY, 0.0, ALU.mult, ALU.add)
-
-        for c in range(1, PIECES):
-            for j in (2 * c, 2 * c + 1):
+        def make_piece(first, end, banks):
+            turned = [bank(n) for n in banks]
+            for j in range(first, end):
                 gate_block(j)
                 if j == 2:
-                    nc.scalar.copy(pairs[:, 0:PIECE], turned[0][:, 0:PIECE])
-                    scatter(0, 0, PIECE)
+                    nc.scalar.activation(dh[1].bitcast(F32).rearrange("p (e q) -> p e q", e=2),
+                                         y_first[:, 1, :, :].rearrange("p q e -> p e q"), ACT.Copy, scale=gate_col[:, 0:1])
                 for u in range(2):
-                    turn(j, u)
-            take_pairs(c)
-            scatter(0, c * PIECE, PIECE)
-            if c == 1:
-                aside = bank(7)
-                for e in range(2):
-                    nc.tensor.transpose(aside[:, e * P:(e + 1) * P], dh_single[:, e, :], ident[:])
-                nc.tensor.transpose(aside[:, 2 * P:3 * P], dh[1][:].bitcast(F32)[:, P:2 * P], ident[:])
+                    nc.tensor.transpose(turned[u][:, (j - first) * P:(j - first + 1) * P], dh[j].bitcast(F32)[:, u * P:(u + 1) * P], ident[:])
+            for u in range(2):
+                nc.scalar.copy(pairs[u][:, first * P:end * P], turned[u][:, 0:(end - first) * P])
 
-        values = keep.tile([P, 2 * P], F32, name="values", tag="dh3", align_bytes=64)
-        nc.scalar.copy(values[:], aside[:, 0:2 * P])
-        nc.scalar.copy(pairs[:, SLOTS + P:SLOTS + PIECE], aside[:, 2 * P:3 * P])
+        y_first = product(0)
+        dh[0] = keep.tile([P, 2 * P], BF16, name="dh0", tag="dh0", align_bytes=64)
+        nc.scalar.activation(dh[0][:].rearrange("p (q e) -> p q e", e=2), y_first[:, 0, :, :], ACT.Copy, scale=gate_col[:, 0:1])
+        first_turned = bank(2)
+        nc.tensor.transpose(first_turned[:, 0:P], dh[0][:].bitcast(F32), ident[:])
+        nc.scalar.copy(pairs[0][:, 0:P], first_turned[:, 0:P])
+        scatter(0, 0, 1)
+
+        partner = keep.tile([P, 2 * T], F32, name="partner", tag="dh0", align_bytes=64)
+        nc.sync.dma_start(partner[:, 0:T], w1t.rearrange("(p j) k -> p (j k)", j=4))
+        w1_raw = partner[:, 0:T].rearrange("p (j k) -> p k j", j=4)
+        aside = bank(7)
+        factor1 = partner[:, T:2 * T].bitcast(BF16).rearrange("p (t e) -> p e t", e=2)
+
+        def take_single(e, values):
+            nc.scalar.copy(values, aside[:, e * P:(e + 1) * P])
+            scatter_single(e, 0, P, values)
+
+        def make_factor(e):
+            nc.gpsimd.tensor_tensor(factor1[:, e, :], single[e][:], mask1[:, e * T:(e + 1) * T], ALU.mult)
+
+        make_piece(1, 3, (4, 5))
+        scatter(0, 1, 3)
+        scatter(1, 1, 3)
         for e in range(2):
-            scatter_single(e, 0, P, values[:, e * P:(e + 1) * P])
-        signs = keep.tile([P, T], BF16, name="signs", tag="dh3", align_bytes=64)
-        mask1.append(keep.tile([P, T], BF16, name="mask1_1", align_bytes=64))
-        nc.scalar.activation(signs[:], a_second[:, T:2 * T], ACT.Sign)
-        nc.scalar.activation(mask1[1][:], signs[:], ACT.Relu)
-        w1_bf = keep.tile([P, 4 * K], BF16, name="w1_bf", tag="dh3", align_bytes=64)[:]
-        nc.scalar.copy(w1_bf.rearrange("p (k j) -> p k j", j=4), w1_raw[:].rearrange("p j k -> p k j"))
+            nc.tensor.transpose(aside[:, e * P:(e + 1) * P], dh[1].bitcast(F32)[:, e * P:(e + 1) * P], ident[:])
+        take_single(0, dh[2].bitcast(F32)[:, 0:P])
+        make_factor(0)
+        make_piece(3, 5, (6, 2))
+        scatter(0, 3, 5)
+        scatter(1, 3, 5)
+        make_piece(5, 8, (4, 5))
+        scatter(0, 5, 8)
 
-        scatter(1, P, SLOTS - P)
-        factor1 = window[0][:, T:2 * T].bitcast(BF16).rearrange("p (t e) -> p e t", e=2)
-        for e in range(2):
-            nc.gpsimd.tensor_tensor(factor1[:, e, :], single[e][:], mask1[e][:], ALU.mult)
+        mask0 = window[1][:, T:2 * T].bitcast(BF16).rearrange("p (t e) -> p t e", e=2)
+        nc.gpsimd.tensor_scalar(mask0[:, 0:MASK_SPLIT, :], clamped0.rearrange("p e t -> p t e"), 1.0 / TINY, 0.0, ALU.mult, ALU.add)
+        signs = scratch[:, 0:2 * (T - MASK_SPLIT)].rearrange("p (t e) -> p t e", e=2)
+        nc.scalar.activation(signs, a_plane0[:, :, MASK_SPLIT:T].rearrange("p e t -> p t e"), ACT.Sign)
+        nc.scalar.activation(mask0[:, MASK_SPLIT:T, :], signs, ACT.Relu)
+        take_single(1, scratch[:].bitcast(F32)[:, 0:P])
+        make_factor(1)
+        scatter(1, 5, 8)
+        w1_bf = scratch[:]
+        nc.scalar.copy(w1_bf.rearrange("p (k j) -> p k j", j=4), w1_raw)
+        for h in range(2):
+            nc.scalar.copy(partner[:, h * HALF:(h + 1) * HALF], window[0][:, h * HALF:(h + 1) * HALF])
 
-        views = [window[u][:].bitcast(BF16).rearrange("p (u t e) -> p t u e", u=2, e=2) for u in range(2)]
-        w1_w = keep.tile([P, K], U32, name="w1_w", tag="pairs", align_bytes=64)
+        views = [tile[:].bitcast(BF16).rearrange("p (u t e) -> p t u e", u=2, e=2) for tile in (partner, window[1])]
+        w1_w = keep.tile([P, K], U32, name="w1_w", tag="pairs1", align_bytes=64)
         w1_sc = keep.tile([P, K], U8, name="w1_sc", align_bytes=64)
         da = keep.tile([P, T, 2, 2], BF16, name="da", align_bytes=64)
         da_w = keep.tile([P, T], U32, name="da_w", align_bytes=64)

@@ -81,10 +81,10 @@ def tile_moe_sub_relu_kernel(tc, dy_words, dy_scales, w2t_words, w2t_scales, w1t
         w2_sc_src = w2t_scales.bitcast(I32).rearrange("e s (q r) w -> r q (e s) w", r=4)
         for r in range(4):
             nc.sync.dma_start(w2_sc[r:P:32, :].bitcast(I32).rearrange("q (x w) -> q x w", x=E * PASSES), w2_sc_src[r])
+        nc.sync.dma_start(w2_w[1][:], w2t_words[0, 1].rearrange("p i d -> p (i d)").bitcast(I32))
         a_rows = a.rearrange("(p r) t -> r p t", r=4)
         a_early = keep.tile([P, HALF], F32, name="a_early", align_bytes=64)
         nc.sync.dma_start(a_early[:], a_rows[2][:, 0:HALF])
-        nc.sync.dma_start(w2_w[1][:], w2t_words[0, 1].rearrange("p i d -> p (i d)").bitcast(I32))
 
         gate_ps = bank(7)
         nc.tensor.transpose(gate_ps[:, 0:P], gate_rows[:], ident[:])
@@ -212,20 +212,20 @@ def tile_moe_sub_relu_kernel(tc, dy_words, dy_scales, w2t_words, w2t_scales, w1t
         scatter(1, 1, 3)
         for e in range(2):
             nc.tensor.transpose(aside[:, e * P:(e + 1) * P], dh[1].bitcast(F32)[:, e * P:(e + 1) * P], ident[:])
-        take_single(0, dh[2].bitcast(F32)[:, 0:P])
-        make_factor(0)
         make_piece(3, 5, (6, 2))
         scatter(0, 3, 5)
         scatter(1, 3, 5)
+        take_single(0, dh[3].bitcast(F32)[:, 0:P])
+        make_factor(0)
         make_piece(5, 8, (4, 5))
         scatter(0, 5, 8)
 
         mask0 = window[1][:, T:2 * T].bitcast(BF16).rearrange("p (t e) -> p t e", e=2)
         nc.gpsimd.tensor_scalar(mask0[:, 0:MASK_SPLIT, :], clamped0.rearrange("p e t -> p t e"), 1.0 / TINY, 0.0, ALU.mult, ALU.add)
-        signs = scratch[:, 0:2 * (T - MASK_SPLIT)].rearrange("p (t e) -> p t e", e=2)
+        signs = scratch[:, 2 * P:2 * P + 2 * (T - MASK_SPLIT)].rearrange("p (t e) -> p t e", e=2)
         nc.scalar.activation(signs, a_plane0[:, :, MASK_SPLIT:T].rearrange("p e t -> p t e"), ACT.Sign)
         nc.scalar.activation(mask0[:, MASK_SPLIT:T, :], signs, ACT.Relu)
-        take_single(1, scratch[:].bitcast(F32)[:, 0:P])
+        take_single(1, dh[7].bitcast(F32)[:, 0:P])
         make_factor(1)
         scatter(1, 5, 8)
         w1_bf = scratch[:]

@@ -261,6 +261,11 @@ def tile_moe_sub_relu_kernel(tc, dy_words, dy_scales, w2t_words, w2t_scales, w1t
                 (nc.scalar if (g, kb) == (3, 0) else nc.sync).dma_start(out[cols, tokens], res[:])
 
         nc.vector.quantize_mx(out=w1_w[:].bitcast(E4M3), scales=w1_sc[:], in_=w1_bf)
+        warm = bank(7)
+        for n in range(2):
+            nc.tensor.matmul_mx(
+                out=warm[:], lhsT=w1_w[:, 0:P].bitcast(E4M3), lhsT_scale=w1_sc[:, 0:P],
+                rhs=w2_w[0].bitcast(E5M2), rhs_scale=w2_sc[:, 0:H], start=True, stop=True)
         for h in range(2):
             for g in (2 * h, 2 * h + 1):
                 tokens = slice(g * QUARTER, (g + 1) * QUARTER)

@@ -28,9 +28,8 @@ QUARTER = 256
 SCALE_ROWS = 100
 BYTE_CUTS = ((0, PIECE), (PIECE, 5 * P), (5 * P, SLOTS))
 OVERLAP = 64
-PRODUCT_BANKS = (0, 1, 3, 1, 3, 3, 6, 2)
+PRODUCT_BANKS = (0, 1, 2, 3, 1, 2, 3, 1)
 LATE_BYTES = 4 * PASSES * C
-MASK_SPLIT = 768
 TINY = 2.0 ** -126
 
 
@@ -83,8 +82,9 @@ def tile_moe_sub_relu_kernel(tc, dy_words, dy_scales, w2t_words, w2t_scales, w1t
             nc.sync.dma_start(w2_sc[r:P:32, :].bitcast(I32).rearrange("q (x w) -> q x w", x=E * PASSES), w2_sc_src[r])
         nc.sync.dma_start(w2_w[1][:], w2t_words[0, 1].rearrange("p i d -> p (i d)").bitcast(I32))
         a_rows = a.rearrange("(p r) t -> r p t", r=4)
-        a_early = keep.tile([P, HALF], F32, name="a_early", align_bytes=64)
-        nc.sync.dma_start(a_early[:], a_rows[2][:, 0:HALF])
+        a_plane0 = a.rearrange("(p u e) t -> u p e t", u=2, e=2)[0]
+        a_early = keep.tile([P, 2, QUARTER], F32, name="a_early", align_bytes=64)
+        nc.sync.dma_start(a_early[:], a_plane0[:, :, 0:QUARTER])
 
         gate_ps = bank(7)
         nc.tensor.transpose(gate_ps[:, 0:P], gate_rows[:], ident[:])
@@ -111,35 +111,44 @@ def tile_moe_sub_relu_kernel(tc, dy_words, dy_scales, w2t_words, w2t_scales, w1t
             gather_bytes(n, keep.tile([P, BYTE_CUTS[n][1] - BYTE_CUTS[n][0]], U8, name="both%d" % n, tag="both%d" % n, align_bytes=64))
         gather_words(0, 0, C, keep.tile([P, C], U32, name="words0", align_bytes=64)[:])
         a_first = late.tile([P, HALF + T], F32, name="a_first", offset=W2_BYTES + 3 * P, align_bytes=64)
-        nc.sync.dma_start(a_first[:, 0:HALF], a_rows[2][:, HALF:T])
-        nc.sync.dma_start(a_first[:, HALF:], a_rows[3])
+        a_next = a_first[:, 0:HALF].rearrange("p (e t) -> p e t", e=2)
+        nc.sync.dma_start(a_next, a_plane0[:, :, QUARTER:HALF])
+        nc.sync.dma_start(a_first[:, HALF:], a_rows[2])
         w2_late = late.tile([P, PASSES, H], I32, name="w2_late", offset=0, align_bytes=64)
         nc.sync.dma_start(w2_late[:], w2t_words[1].rearrange("s p i d -> p s (i d)").bitcast(I32))
         w2_w = [tile[:] for tile in w2_w] + [w2_late[:, s, :] for s in range(PASSES)]
         gather_words(1, 0, C, keep.tile([P, C], U32, name="words1", align_bytes=64)[:])
         gather_bytes(2, late.tile([P, 3 * P], U8, name="both2", offset=W2_BYTES, align_bytes=64))
         a_second = last.tile([P, 2 * T], F32, name="a_second", offset=LATE_BYTES, align_bytes=64)
-        for e in range(2):
-            nc.sync.dma_start(a_second[:, e * T:(e + 1) * T], a_rows[e])
+        nc.sync.dma_start(a_second[:, 0:T], a_rows[3])
+        a_late = a_second[:, T:2 * T].rearrange("p (e t) -> p e t", e=2)
+        nc.sync.dma_start(a_late, a_plane0[:, :, HALF:T])
         late_words = last.tile([P, LATE_BYTES // 4], U32, name="late_words", offset=0, align_bytes=64)
         for s in reversed(range(PASSES)):
             gather_words(s, C, SLOTS, late_words[:, s * C:(s + 1) * C])
 
+        clamped0 = keep.tile([P, 2 * T], BF16, name="clamped0", align_bytes=64)
         clamped1 = keep.tile([P, 2 * T], BF16, name="clamped1", align_bytes=64)
         mask1 = keep.tile([P, 2 * T], BF16, name="mask1", align_bytes=64)
+        mask0 = window[1][:, T:2 * T].bitcast(BF16)
 
-        def finish_mask1(lo, hi):
-            nc.gpsimd.tensor_scalar(mask1[:, lo:hi], clamped1[:, lo:hi], 1.0 / TINY, 0.0, ALU.mult, ALU.add)
+        def clamp(dst, values):
+            nc.gpsimd.tensor_scalar(dst, values, TINY, 0.0, ALU.min, ALU.max)
 
-        nc.gpsimd.tensor_scalar(clamped1[:, 0:HALF], a_early[:], TINY, 0.0, ALU.min, ALU.max)
-        finish_mask1(0, HALF)
-        nc.gpsimd.tensor_scalar(clamped1[:, HALF:T], a_first[:, 0:HALF], TINY, 0.0, ALU.min, ALU.max)
-        nc.gpsimd.tensor_scalar(clamped1[:, T:2 * T], a_first[:, HALF:], TINY, 0.0, ALU.min, ALU.max)
-        finish_mask1(HALF, 2 * T)
-        a_plane0 = a_second[:].rearrange("p (e t) -> p e t", e=2)
-        clamped0 = keep.tile([P, 2, MASK_SPLIT], BF16, name="clamped0", align_bytes=64)[:]
-        for e in range(2):
-            nc.gpsimd.tensor_scalar(clamped0[:, e, :], a_second[:, e * T:e * T + MASK_SPLIT], TINY, 0.0, ALU.min, ALU.max)
+        def clamp_woven(first, end, values):
+            clamp(clamped0[:, 2 * first:2 * end].rearrange("p (t e) -> p t e", e=2), values.rearrange("p e t -> p t e"))
+
+        def rescale(dst, values):
+            nc.gpsimd.tensor_scalar(dst, values, 1.0 / TINY, 0.0, ALU.mult, ALU.add)
+
+        clamp_woven(0, QUARTER, a_early[:])
+        clamp_woven(QUARTER, HALF, a_next)
+        rescale(mask0[:, 0:2 * HALF], clamped0[:, 0:2 * HALF])
+        clamp(clamped1[:, 0:T], a_first[:, HALF:])
+        rescale(mask1[:, 0:T], clamped1[:, 0:T])
+        clamp(clamped1[:, T:2 * T], a_second[:, 0:T])
+        clamp_woven(HALF, T, a_late)
+        rescale(mask1[:, T:2 * T], clamped1[:, T:2 * T])
 
         def product(j):
             y = bank(PRODUCT_BANKS[j])
@@ -158,80 +167,83 @@ def tile_moe_sub_relu_kernel(tc, dy_words, dy_scales, w2t_words, w2t_scales, w1t
                 )
             return y[:].rearrange("p (q u e) -> p u q e", u=2, e=2)
 
-        def scatter_single(e, first, count, values):
-            nc.scalar.activation(single[e][:].indirect(entries(first, count)), values, ACT.Copy)
-
-        pairs = [keep.tile([P, SLOTS], F32, name="pairs%d" % u, tag="pairs%d" % u, align_bytes=64) for u in range(2)]
-
-        def scatter(u, first, end):
-            nc.vector.tensor_copy(window[u][:].indirect(entries(first * P, (end - first) * P)), pairs[u][:, first * P:end * P])
-
+        pairs = keep.tile([P, 2, SLOTS], F32, name="pairs", tag="pairs1", align_bytes=64)
         dh = {}
-        scratch = keep.tile([P, 4 * K], BF16, name="scratch", align_bytes=64)
 
         def gate_block(j):
             y = product(j)
-            dh[j] = keep.tile([P, H], BF16, name="dh%d" % j, tag="dh%d" % j, align_bytes=64)[:] if j < 7 else scratch[:, 0:H]
+            dh[j] = keep.tile([P, H], BF16, name="dh%d" % j, tag="dh%d" % j, align_bytes=64)[:]
             nc.scalar.activation(dh[j].rearrange("p (u q e) -> p u q e", u=2, e=2), y, ACT.Copy, scale=gate_col[:, j:j + 1])
 
-        def make_piece(first, end, banks):
-            turned = [bank(n) for n in banks]
-            for j in range(first, end):
-                gate_block(j)
-                if j == 2:
-                    nc.scalar.activation(dh[1].bitcast(F32).rearrange("p (e q) -> p e q", e=2),
-                                         y_first[:, 1, :, :].rearrange("p q e -> p e q"), ACT.Copy, scale=gate_col[:, 0:1])
-                for u in range(2):
-                    nc.tensor.transpose(turned[u][:, (j - first) * P:(j - first + 1) * P], dh[j].bitcast(F32)[:, u * P:(u + 1) * P], ident[:])
+        def turn(j, u, turned, place):
+            nc.tensor.transpose(turned[:, place * P:(place + 1) * P], dh[j].bitcast(F32)[:, u * P:(u + 1) * P], ident[:])
+
+        def take_pairs(u, first, end, turned):
+            nc.scalar.copy(pairs[:, u, first * P:end * P], turned[:, 0:(end - first) * P])
+
+        def scatter(u, first, end):
+            nc.vector.tensor_copy(window[u][:].indirect(entries(first * P, (end - first) * P)), pairs[:, u, first * P:end * P])
+
+        lead, second0, aside, second1 = bank(4), bank(5), bank(6), bank(7)
+        for j in range(2):
+            gate_block(j)
             for u in range(2):
-                nc.scalar.copy(pairs[u][:, first * P:end * P], turned[u][:, 0:(end - first) * P])
-
-        y_first = product(0)
-        dh[0] = keep.tile([P, 2 * P], BF16, name="dh0", tag="dh0", align_bytes=64)
-        nc.scalar.activation(dh[0][:].rearrange("p (q e) -> p q e", e=2), y_first[:, 0, :, :], ACT.Copy, scale=gate_col[:, 0:1])
-        first_turned = bank(2)
-        nc.tensor.transpose(first_turned[:, 0:P], dh[0][:].bitcast(F32), ident[:])
-        nc.scalar.copy(pairs[0][:, 0:P], first_turned[:, 0:P])
-        scatter(0, 0, 1)
-
+                turn(j, u, lead, 2 * u + j)
+        gate_block(2)
+        nc.scalar.copy(pairs[:, :, 0:PIECE], lead[:].rearrange("p (u j) -> p u j", u=2))
+        scatter(0, 0, 2)
+        scatter(1, 0, 2)
         partner = keep.tile([P, 2 * T], F32, name="partner", tag="dh0", align_bytes=64)
-        nc.sync.dma_start(partner[:, 0:T], w1t.rearrange("(p j) k -> p (j k)", j=4))
-        w1_raw = partner[:, 0:T].rearrange("p (j k) -> p k j", j=4)
-        aside = bank(7)
+        w1_raw = partner[:, 0:T].rearrange("p (b j k) -> p b j k", b=2, j=4)
+        for b in range(2):
+            nc.sync.dma_start(w1_raw[:, b], w1t.rearrange("(p j) k -> p j k", j=4)[:, :, b * P:(b + 1) * P])
         factor1 = partner[:, T:2 * T].bitcast(BF16).rearrange("p (t e) -> p e t", e=2)
+        scratch = keep.tile([P, 4 * K], BF16, name="scratch", align_bytes=64)
+        values = scratch[:].bitcast(F32).rearrange("p (e j) -> p e j", e=2)
 
-        def take_single(e, values):
-            nc.scalar.copy(values, aside[:, e * P:(e + 1) * P])
-            scatter_single(e, 0, P, values)
-
-        def make_factor(e):
+        def scatter_single(e):
+            nc.scalar.activation(single[e][:].indirect(entries(2 * P, PIECE)), values[:, e, :], ACT.Copy)
             nc.gpsimd.tensor_tensor(factor1[:, e, :], single[e][:], mask1[:, e * T:(e + 1) * T], ALU.mult)
 
-        make_piece(1, 3, (4, 5))
-        scatter(0, 1, 3)
-        scatter(1, 1, 3)
-        for e in range(2):
-            nc.tensor.transpose(aside[:, e * P:(e + 1) * P], dh[1].bitcast(F32)[:, e * P:(e + 1) * P], ident[:])
-        make_piece(3, 5, (6, 2))
-        scatter(0, 3, 5)
-        scatter(1, 3, 5)
-        take_single(0, dh[3].bitcast(F32)[:, 0:P])
-        make_factor(0)
-        make_piece(5, 8, (4, 5))
-        scatter(0, 5, 8)
+        def take_singles(n, turned):
+            nc.scalar.copy(values[:, :, n * P:(n + 1) * P], turned[:, 0:P].bitcast(BF16).rearrange("p (j e) -> p e j", e=2))
 
-        mask0 = window[1][:, T:2 * T].bitcast(BF16).rearrange("p (t e) -> p t e", e=2)
-        nc.gpsimd.tensor_scalar(mask0[:, 0:MASK_SPLIT, :], clamped0.rearrange("p e t -> p t e"), 1.0 / TINY, 0.0, ALU.mult, ALU.add)
-        signs = scratch[:, 2 * P:2 * P + 2 * (T - MASK_SPLIT)].rearrange("p (t e) -> p t e", e=2)
-        nc.scalar.activation(signs, a_plane0[:, :, MASK_SPLIT:T].rearrange("p e t -> p t e"), ACT.Sign)
-        nc.scalar.activation(mask0[:, MASK_SPLIT:T, :], signs, ACT.Relu)
-        take_single(1, dh[7].bitcast(F32)[:, 0:P])
-        make_factor(1)
-        scatter(1, 5, 8)
+        turn(2, 1, aside, 0)
+        turn(2, 0, second0, 0)
+        gate_block(3)
+        turn(3, 0, second0, 1)
+        take_singles(0, aside)
+        gate_block(4)
+        turn(4, 0, second0, 2)
+        turn(4, 1, second1, 0)
+        take_pairs(0, 2, 5, second0)
+        scatter(0, 2, 5)
+        third0, third1 = bank(4), bank(6)
+        gate_block(5)
+        turn(5, 1, second1, 1)
+        turn(5, 0, third0, 0)
+        for j in (6, 7):
+            gate_block(j)
+            if j == 6:
+                aside_late = bank(PRODUCT_BANKS[j])
+                turn(3, 1, aside_late, 0)
+            turn(j, 0, third0, j - 5)
+            turn(j, 1, third1, j - 6)
+        take_singles(1, aside_late)
+        take_pairs(1, 4, 6, second1)
+        scatter(1, 4, 6)
+        scatter_single(0)
+        take_pairs(0, 5, 8, third0)
+        scatter(0, 5, 8)
+        scatter_single(1)
+        take_pairs(1, 6, 8, third1)
+        scatter(1, 6, 8)
         w1_bf = scratch[:]
-        nc.scalar.copy(w1_bf.rearrange("p (k j) -> p k j", j=4), w1_raw)
-        for h in range(2):
+        for b in reversed(range(2)):
+            nc.scalar.copy(w1_bf[:, b * HALF:(b + 1) * HALF].rearrange("p (k j) -> p k j", j=4), w1_raw[:, b].rearrange("p j k -> p k j"))
+        for h in reversed(range(2)):
             nc.scalar.copy(partner[:, h * HALF:(h + 1) * HALF], window[0][:, h * HALF:(h + 1) * HALF])
+        nc.scalar.activation(mask0[:, 2 * HALF:], clamped0[:, 2 * HALF:], ACT.Copy, scale=1.0 / TINY)
 
         views = [tile[:].bitcast(BF16).rearrange("p (u t e) -> p t u e", u=2, e=2) for tile in (partner, window[1])]
         w1_w = keep.tile([P, K], U32, name="w1_w", tag="pairs1", align_bytes=64)

@@ -28,7 +28,7 @@ QUARTER = 256
 SCALE_ROWS = 100
 BYTE_CUTS = ((0, PIECE), (PIECE, 5 * P), (5 * P, SLOTS))
 OVERLAP = 64
-PRODUCT_BANKS = (0, 1, 2, 3, 1, 2, 3, 1)
+PRODUCT_BANKS = (0, 1, 2, 1, 0, 2, 1, 3)
 LATE_BYTES = 4 * PASSES * C
 TINY = 2.0 ** -126
 
@@ -109,7 +109,7 @@ def tile_moe_sub_relu_kernel(tc, dy_words, dy_scales, w2t_words, w2t_scales, w1t
 
         for n in range(2):
             gather_bytes(n, keep.tile([P, BYTE_CUTS[n][1] - BYTE_CUTS[n][0]], U8, name="both%d" % n, tag="both%d" % n, align_bytes=64))
-        gather_words(0, 0, C, keep.tile([P, C], U32, name="words0", align_bytes=64)[:])
+        gather_words(0, 0, C, keep.tile([P, C], U32, name="words0", tag="words0", align_bytes=64)[:])
         a_first = late.tile([P, HALF + T], F32, name="a_first", offset=W2_BYTES + 3 * P, align_bytes=64)
         a_next = a_first[:, 0:HALF].rearrange("p (e t) -> p e t", e=2)
         nc.sync.dma_start(a_next, a_plane0[:, :, QUARTER:HALF])
@@ -184,16 +184,14 @@ def tile_moe_sub_relu_kernel(tc, dy_words, dy_scales, w2t_words, w2t_scales, w1t
         def scatter(u, first, end):
             nc.vector.tensor_copy(window[u][:].indirect(entries(first * P, (end - first) * P)), pairs[:, u, first * P:end * P])
 
-        lead, second0, aside, second1 = bank(4), bank(5), bank(6), bank(7)
+        first0, first1, second0, aside, second1 = bank(4), bank(3), bank(5), bank(6), bank(7)
         for j in range(2):
             gate_block(j)
-            for u in range(2):
-                turn(j, u, lead, 2 * u + j)
+            turn(j, 0, first0, j)
         gate_block(2)
-        nc.scalar.copy(pairs[:, :, 0:PIECE], lead[:].rearrange("p (u j) -> p u j", u=2))
+        take_pairs(0, 0, 2, first0)
         scatter(0, 0, 2)
-        scatter(1, 0, 2)
-        partner = keep.tile([P, 2 * T], F32, name="partner", tag="dh0", align_bytes=64)
+        partner = keep.tile([P, 2 * T], F32, name="partner", tag="words0", align_bytes=64)
         w1_raw = partner[:, 0:T].rearrange("p (b j k) -> p b j k", b=2, j=4)
         for b in range(2):
             nc.sync.dma_start(w1_raw[:, b], w1t.rearrange("(p j) k -> p j k", j=4)[:, :, b * P:(b + 1) * P])
@@ -201,41 +199,48 @@ def tile_moe_sub_relu_kernel(tc, dy_words, dy_scales, w2t_words, w2t_scales, w1t
         scratch = keep.tile([P, 4 * K], BF16, name="scratch", align_bytes=64)
         values = scratch[:].bitcast(F32).rearrange("p (e j) -> p e j", e=2)
 
-        def scatter_single(e):
-            nc.scalar.activation(single[e][:].indirect(entries(2 * P, PIECE)), values[:, e, :], ACT.Copy)
-            nc.gpsimd.tensor_tensor(factor1[:, e, :], single[e][:], mask1[:, e * T:(e + 1) * T], ALU.mult)
-
         def take_singles(n, turned):
             nc.scalar.copy(values[:, :, n * P:(n + 1) * P], turned[:, 0:P].bitcast(BF16).rearrange("p (j e) -> p e j", e=2))
 
-        turn(2, 1, aside, 0)
-        turn(2, 0, second0, 0)
+        def scatter_single(e, first, end):
+            nc.scalar.activation(single[e][:].indirect(entries(2 * P + first, end - first)), values[:, e, first:end], ACT.Copy)
+
+        def make_factor(e):
+            nc.gpsimd.tensor_tensor(factor1[:, e, :], single[e][:], mask1[:, e * T:(e + 1) * T], ALU.mult)
+
         gate_block(3)
-        turn(3, 0, second0, 1)
+        for j in range(2):
+            turn(j, 1, first1, j)
+        take_pairs(1, 0, 2, first1)
+        scatter(1, 0, 2)
+        turn(2, 1, aside, 0)
         take_singles(0, aside)
-        gate_block(4)
-        turn(4, 0, second0, 2)
-        turn(4, 1, second1, 0)
-        take_pairs(0, 2, 5, second0)
-        scatter(0, 2, 5)
+        for j in (2, 3):
+            turn(j, 0, second0, j - 2)
+        take_pairs(0, 2, 4, second0)
+        scatter(0, 2, 4)
+        scatter_single(0, 0, P)
         third0, third1 = bank(4), bank(6)
-        gate_block(5)
-        turn(5, 1, second1, 1)
-        turn(5, 0, third0, 0)
+        for j in (4, 5):
+            gate_block(j)
+            turn(j, 1, second1, j - 4)
+            turn(j, 0, third0, j - 4)
         for j in (6, 7):
             gate_block(j)
-            if j == 6:
-                aside_late = bank(PRODUCT_BANKS[j])
-                turn(3, 1, aside_late, 0)
-            turn(j, 0, third0, j - 5)
+            turn(j, 0, third0, j - 4)
+        aside_late = bank(PRODUCT_BANKS[7])
+        turn(3, 1, aside_late, 0)
+        for j in (6, 7):
             turn(j, 1, third1, j - 6)
-        take_singles(1, aside_late)
         take_pairs(1, 4, 6, second1)
         scatter(1, 4, 6)
-        scatter_single(0)
-        take_pairs(0, 5, 8, third0)
-        scatter(0, 5, 8)
-        scatter_single(1)
+        take_pairs(0, 4, 8, third0)
+        scatter(0, 4, 8)
+        take_singles(1, aside_late)
+        scatter_single(0, P, PIECE)
+        make_factor(0)
+        scatter_single(1, 0, PIECE)
+        make_factor(1)
         take_pairs(1, 6, 8, third1)
         scatter(1, 6, 8)
         w1_bf = scratch[:]

@@ -127,8 +127,8 @@ def tile_moe_sub_relu_kernel(tc, dy_words, dy_scales, w2t_words, w2t_scales, w1t
         for s in reversed(range(PASSES)):
             gather_words(s, C, SLOTS, late_words[:, s * C:(s + 1) * C])
 
-        clamped0 = keep.tile([P, 2 * T], BF16, name="clamped0", align_bytes=64)
-        clamped1 = keep.tile([P, 2 * T], BF16, name="clamped1", align_bytes=64)
+        clamped0 = keep.tile([P, T], BF16, name="clamped0", align_bytes=64)
+        clamped1 = keep.tile([P, 3 * T], BF16, name="clamped1", align_bytes=64)
         mask1 = keep.tile([P, 2 * T], BF16, name="mask1", align_bytes=64)
         mask0 = window[1][:, T:2 * T].bitcast(BF16)
 
@@ -142,12 +142,13 @@ def tile_moe_sub_relu_kernel(tc, dy_words, dy_scales, w2t_words, w2t_scales, w1t
             nc.gpsimd.tensor_scalar(dst, values, 1.0 / TINY, 0.0, ALU.mult, ALU.add)
 
         clamp_woven(0, QUARTER, a_early[:])
+        rescale(mask0[:, 0:HALF], clamped0[:, 0:HALF])
         clamp_woven(QUARTER, HALF, a_next)
-        rescale(mask0[:, 0:2 * HALF], clamped0[:, 0:2 * HALF])
         clamp(clamped1[:, 0:T], a_first[:, HALF:])
+        rescale(mask0[:, HALF:T], clamped0[:, HALF:T])
         rescale(mask1[:, 0:T], clamped1[:, 0:T])
         clamp(clamped1[:, T:2 * T], a_second[:, 0:T])
-        clamp_woven(HALF, T, a_late)
+        clamp(clamped1[:, 2 * T:2 * T + HALF], a_second[:, T:T + HALF])
         rescale(mask1[:, T:2 * T], clamped1[:, T:2 * T])
 
         def product(j):
@@ -172,7 +173,7 @@ def tile_moe_sub_relu_kernel(tc, dy_words, dy_scales, w2t_words, w2t_scales, w1t
 
         def gate_block(j):
             y = product(j)
-            dh[j] = keep.tile([P, H], BF16, name="dh%d" % j, tag="dh%d" % j, align_bytes=64)[:]
+            dh[j] = keep.tile([P, H], BF16, name="dh%d" % j, tag="dh%d" % j, align_bytes=64)[:] if j < 7 else scratch[:, H:2 * H]
             nc.scalar.activation(dh[j].rearrange("p (u q e) -> p u q e", u=2, e=2), y, ACT.Copy, scale=gate_col[:, j:j + 1])
 
         def turn(j, u, turned, place):
@@ -197,13 +198,13 @@ def tile_moe_sub_relu_kernel(tc, dy_words, dy_scales, w2t_words, w2t_scales, w1t
             nc.sync.dma_start(w1_raw[:, b], w1t.rearrange("(p j) k -> p j k", j=4)[:, :, b * P:(b + 1) * P])
         factor1 = partner[:, T:2 * T].bitcast(BF16).rearrange("p (t e) -> p e t", e=2)
         scratch = keep.tile([P, 4 * K], BF16, name="scratch", align_bytes=64)
-        values = scratch[:].bitcast(F32).rearrange("p (e j) -> p e j", e=2)
+        values = scratch[:].bitcast(F32)
 
-        def take_singles(n, turned):
-            nc.scalar.copy(values[:, :, n * P:(n + 1) * P], turned[:, 0:P].bitcast(BF16).rearrange("p (j e) -> p e j", e=2))
+        def halves(turned):
+            return turned[:, 0:P].bitcast(BF16).rearrange("p (j e) -> p e j", e=2)
 
-        def scatter_single(e, first, end):
-            nc.scalar.activation(single[e][:].indirect(entries(2 * P + first, end - first)), values[:, e, first:end], ACT.Copy)
+        def scatter_single(e, first, count, source):
+            nc.scalar.activation(single[e][:].indirect(entries(first, count)), source, ACT.Copy)
 
         def make_factor(e):
             nc.gpsimd.tensor_tensor(factor1[:, e, :], single[e][:], mask1[:, e * T:(e + 1) * T], ALU.mult)
@@ -214,41 +215,46 @@ def tile_moe_sub_relu_kernel(tc, dy_words, dy_scales, w2t_words, w2t_scales, w1t
         take_pairs(1, 0, 2, first1)
         scatter(1, 0, 2)
         turn(2, 1, aside, 0)
-        take_singles(0, aside)
+        nc.scalar.copy(values[:, 0:2 * P].rearrange("p (e j) -> p e j", e=2), halves(aside))
         for j in (2, 3):
             turn(j, 0, second0, j - 2)
         take_pairs(0, 2, 4, second0)
         scatter(0, 2, 4)
-        scatter_single(0, 0, P)
+        scatter_single(0, 2 * P, P, values[:, 0:P])
         third0, third1 = bank(4), bank(6)
         for j in (4, 5):
             gate_block(j)
             turn(j, 1, second1, j - 4)
             turn(j, 0, third0, j - 4)
-        for j in (6, 7):
-            gate_block(j)
-            turn(j, 0, third0, j - 4)
-        aside_late = bank(PRODUCT_BANKS[7])
+        gate_block(6)
+        turn(6, 0, third0, 2)
+        aside_late = bank(PRODUCT_BANKS[6])
         turn(3, 1, aside_late, 0)
-        for j in (6, 7):
-            turn(j, 1, third1, j - 6)
         take_pairs(1, 4, 6, second1)
         scatter(1, 4, 6)
+        late_values = dh[0].bitcast(F32)[:, 0:P]
+        nc.scalar.copy(late_values, halves(aside_late)[:, 0, :])
+        gate_block(7)
+        turn(7, 0, third0, 3)
+        for j in (6, 7):
+            turn(j, 1, third1, j - 6)
+        scatter_single(0, 3 * P, P, late_values)
+        make_factor(0)
+        clamp(clamped1[:, 2 * T + HALF:3 * T], a_second[:, T + HALF:2 * T])
         take_pairs(0, 4, 8, third0)
         scatter(0, 4, 8)
-        take_singles(1, aside_late)
-        scatter_single(0, P, PIECE)
-        make_factor(0)
-        scatter_single(1, 0, PIECE)
-        make_factor(1)
+        nc.scalar.copy(values[:, 2 * P:3 * P], halves(aside_late)[:, 1, :])
         take_pairs(1, 6, 8, third1)
+        scatter_single(1, 2 * P, PIECE, values[:, P:3 * P])
+        make_factor(1)
         scatter(1, 6, 8)
         w1_bf = scratch[:]
         for b in reversed(range(2)):
             nc.scalar.copy(w1_bf[:, b * HALF:(b + 1) * HALF].rearrange("p (k j) -> p k j", j=4), w1_raw[:, b].rearrange("p j k -> p k j"))
         for h in reversed(range(2)):
             nc.scalar.copy(partner[:, h * HALF:(h + 1) * HALF], window[0][:, h * HALF:(h + 1) * HALF])
-        nc.scalar.activation(mask0[:, 2 * HALF:], clamped0[:, 2 * HALF:], ACT.Copy, scale=1.0 / TINY)
+        nc.scalar.activation(mask0[:, 2 * HALF:].rearrange("p (t e) -> p t e", e=2), clamped1[:, 2 * T:3 * T].rearrange("p (e t) -> p t e", e=2),
+                             ACT.Copy, scale=1.0 / TINY)
 
         views = [tile[:].bitcast(BF16).rearrange("p (u t e) -> p t u e", u=2, e=2) for tile in (partner, window[1])]
         w1_w = keep.tile([P, K], U32, name="w1_w", tag="pairs1", align_bytes=64)

@@ -26,10 +26,13 @@ W2_BYTES = 4 * PASSES * H
 HALF = 512
 QUARTER = 256
 SCALE_ROWS = 100
-BYTE_CUTS = ((0, PIECE), (PIECE, 5 * P), (5 * P, SLOTS))
+BYTE_CUTS = ((0, PIECE), (PIECE, 3 * PIECE), (3 * PIECE, SLOTS))
 OVERLAP = 64
-PRODUCT_BANKS = (0, 1, 2, 1, 0, 2, 1, 3)
+PRODUCT_BANKS = (0, 1, 2, 1, 0, 2, 1, 6)
 LATE_BYTES = 4 * PASSES * C
+EXTRA = 32
+SHARE_START = PIECE - EXTRA
+MASK_QUARTERS = 3
 TINY = 2.0 ** -126
 
 
@@ -62,7 +65,7 @@ def tile_moe_sub_relu_kernel(tc, dy_words, dy_scales, w2t_words, w2t_scales, w1t
         for tile in moved:
             nc.vector.memset(tile[:].bitcast(I32), 0)
 
-        window = [keep.tile([P, (u + 1) * T], F32, name="window%d" % u, tag="window%d" % u, align_bytes=64) for u in range(2)]
+        window = [keep.tile([P, T + u * MASK_QUARTERS * QUARTER], F32, name="window%d" % u, tag="window%d" % u, align_bytes=64) for u in range(2)]
         single = [keep.tile([P, T], F32, name="single%d" % e) for e in range(2)]
         for e in range(2):
             nc.gpsimd.memset(single[e][:], 1.0)
@@ -109,7 +112,9 @@ def tile_moe_sub_relu_kernel(tc, dy_words, dy_scales, w2t_words, w2t_scales, w1t
 
         for n in range(2):
             gather_bytes(n, keep.tile([P, BYTE_CUTS[n][1] - BYTE_CUTS[n][0]], U8, name="both%d" % n, tag="both%d" % n, align_bytes=64))
-        gather_words(0, 0, C, keep.tile([P, C], U32, name="words0", tag="words0", align_bytes=64)[:])
+        words0 = keep.tile([P, C], U32, name="words0", tag="words0", align_bytes=64)
+        for lo in range(0, C, PIECE):
+            gather_words(0, lo, lo + PIECE, words0[:, lo:lo + PIECE])
         a_first = late.tile([P, HALF + T], F32, name="a_first", offset=W2_BYTES + 3 * P, align_bytes=64)
         a_next = a_first[:, 0:HALF].rearrange("p (e t) -> p e t", e=2)
         nc.sync.dma_start(a_next, a_plane0[:, :, QUARTER:HALF])
@@ -117,8 +122,9 @@ def tile_moe_sub_relu_kernel(tc, dy_words, dy_scales, w2t_words, w2t_scales, w1t
         w2_late = late.tile([P, PASSES, H], I32, name="w2_late", offset=0, align_bytes=64)
         nc.sync.dma_start(w2_late[:], w2t_words[1].rearrange("s p i d -> p s (i d)").bitcast(I32))
         w2_w = [tile[:] for tile in w2_w] + [w2_late[:, s, :] for s in range(PASSES)]
-        gather_words(1, 0, C, keep.tile([P, C], U32, name="words1", align_bytes=64)[:])
-        gather_bytes(2, late.tile([P, 3 * P], U8, name="both2", offset=W2_BYTES, align_bytes=64))
+        for lo in range(0, C, PIECE):
+            gather_words(1, lo, lo + PIECE, keep.tile([P, PIECE], U32, name="words1_%d" % lo, align_bytes=64)[:])
+        gather_bytes(2, late.tile([P, PIECE], U8, name="both2", offset=W2_BYTES, align_bytes=64))
         a_second = last.tile([P, 2 * T], F32, name="a_second", offset=LATE_BYTES, align_bytes=64)
         nc.sync.dma_start(a_second[:, 0:T], a_rows[3])
         a_late = a_second[:, T:2 * T].rearrange("p (e t) -> p e t", e=2)
@@ -130,7 +136,7 @@ def tile_moe_sub_relu_kernel(tc, dy_words, dy_scales, w2t_words, w2t_scales, w1t
         clamped0 = keep.tile([P, T], BF16, name="clamped0", align_bytes=64)
         clamped1 = keep.tile([P, 3 * T], BF16, name="clamped1", align_bytes=64)
         mask1 = keep.tile([P, 2 * T], BF16, name="mask1", align_bytes=64)
-        mask0 = window[1][:, T:2 * T].bitcast(BF16)
+        mask0 = window[1][:, T:].bitcast(BF16)
 
         def clamp(dst, values):
             nc.gpsimd.tensor_scalar(dst, values, TINY, 0.0, ALU.min, ALU.max)
@@ -173,7 +179,7 @@ def tile_moe_sub_relu_kernel(tc, dy_words, dy_scales, w2t_words, w2t_scales, w1t
 
         def gate_block(j):
             y = product(j)
-            dh[j] = keep.tile([P, H], BF16, name="dh%d" % j, tag="dh%d" % j, align_bytes=64)[:] if j < 7 else scratch[:, H:2 * H]
+            dh[j] = keep.tile([P, H], BF16, name="dh%d" % j, tag="dh%d" % j, align_bytes=64)[:]
             nc.scalar.activation(dh[j].rearrange("p (u q e) -> p u q e", u=2, e=2), y, ACT.Copy, scale=gate_col[:, j:j + 1])
 
         def turn(j, u, turned, place):
@@ -182,10 +188,13 @@ def tile_moe_sub_relu_kernel(tc, dy_words, dy_scales, w2t_words, w2t_scales, w1t
         def take_pairs(u, first, end, turned):
             nc.scalar.copy(pairs[:, u, first * P:end * P], turned[:, 0:(end - first) * P])
 
-        def scatter(u, first, end):
-            nc.vector.tensor_copy(window[u][:].indirect(entries(first * P, (end - first) * P)), pairs[:, u, first * P:end * P])
+        def scatter_slots(u, first, end):
+            nc.vector.tensor_copy(window[u][:].indirect(entries(first, end - first)), pairs[:, u, first:end])
 
-        first0, first1, second0, aside, second1 = bank(4), bank(3), bank(5), bank(6), bank(7)
+        def scatter(u, first, end):
+            scatter_slots(u, first * P, end * P)
+
+        first0, first1, second0, second1 = bank(4), bank(3), bank(5), bank(7)
         for j in range(2):
             gate_block(j)
             turn(j, 0, first0, j)
@@ -197,66 +206,75 @@ def tile_moe_sub_relu_kernel(tc, dy_words, dy_scales, w2t_words, w2t_scales, w1t
         for b in range(2):
             nc.sync.dma_start(w1_raw[:, b], w1t.rearrange("(p j) k -> p j k", j=4)[:, :, b * P:(b + 1) * P])
         factor1 = partner[:, T:2 * T].bitcast(BF16).rearrange("p (t e) -> p e t", e=2)
-        scratch = keep.tile([P, 4 * K], BF16, name="scratch", align_bytes=64)
-        values = scratch[:].bitcast(F32)
+        scratch = keep.tile([P, 6 * K], BF16, name="scratch", align_bytes=64)
+        values = scratch[:].bitcast(F32).rearrange("p (e j) -> p e j", e=2)
 
-        def halves(turned):
-            return turned[:, 0:P].bitcast(BF16).rearrange("p (j e) -> p e j", e=2)
+        def take_singles(first, count, turned):
+            nc.scalar.copy(values[:, :, first:first + count], turned.bitcast(BF16).rearrange("p (j e) -> p e j", e=2))
 
-        def scatter_single(e, first, count, source):
-            nc.scalar.activation(single[e][:].indirect(entries(first, count)), source, ACT.Copy)
+        def scatter_single(e, first, end):
+            nc.scalar.activation(single[e][:].indirect(entries(SHARE_START + first, end - first)), values[:, e, first:end], ACT.Copy)
 
         def make_factor(e):
             nc.gpsimd.tensor_tensor(factor1[:, e, :], single[e][:], mask1[:, e * T:(e + 1) * T], ALU.mult)
 
         gate_block(3)
-        for j in range(2):
+        for j in range(3):
             turn(j, 1, first1, j)
-        take_pairs(1, 0, 2, first1)
-        scatter(1, 0, 2)
-        turn(2, 1, aside, 0)
-        nc.scalar.copy(values[:, 0:2 * P].rearrange("p (e j) -> p e j", e=2), halves(aside))
+        nc.scalar.copy(pairs[:, 1, 0:SHARE_START], first1[:, 0:SHARE_START])
+        scatter_slots(1, 0, SHARE_START)
+        take_singles(0, EXTRA + P, first1[:, SHARE_START:3 * P])
         for j in (2, 3):
             turn(j, 0, second0, j - 2)
         take_pairs(0, 2, 4, second0)
         scatter(0, 2, 4)
-        scatter_single(0, 2 * P, P, values[:, 0:P])
-        third0, third1 = bank(4), bank(6)
+        scatter_single(0, 0, P)
+        third0, third1 = bank(4), bank(3)
         for j in (4, 5):
             gate_block(j)
             turn(j, 1, second1, j - 4)
             turn(j, 0, third0, j - 4)
-        gate_block(6)
-        turn(6, 0, third0, 2)
-        aside_late = bank(PRODUCT_BANKS[6])
-        turn(3, 1, aside_late, 0)
+        for j in (6, 7):
+            gate_block(j)
+            turn(j, 0, third0, j - 4)
+            if j == 6:
+                turn(6, 1, third1, 0)
+                turn(3, 1, third1, 2)
         take_pairs(1, 4, 6, second1)
         scatter(1, 4, 6)
-        late_values = dh[0].bitcast(F32)[:, 0:P]
-        nc.scalar.copy(late_values, halves(aside_late)[:, 0, :])
-        gate_block(7)
-        turn(7, 0, third0, 3)
-        for j in (6, 7):
-            turn(j, 1, third1, j - 6)
-        scatter_single(0, 3 * P, P, late_values)
-        make_factor(0)
-        clamp(clamped1[:, 2 * T + HALF:3 * T], a_second[:, T + HALF:2 * T])
         take_pairs(0, 4, 8, third0)
         scatter(0, 4, 8)
-        nc.scalar.copy(values[:, 2 * P:3 * P], halves(aside_late)[:, 1, :])
-        take_pairs(1, 6, 8, third1)
-        scatter_single(1, 2 * P, PIECE, values[:, P:3 * P])
+        take_singles(EXTRA + P, P, third1[:, 2 * P:3 * P])
+        turn(7, 1, third1, 1)
+        scatter_single(0, P, EXTRA + PIECE)
+        clamp(clamped1[:, 2 * T + HALF:3 * T], a_second[:, T + HALF:2 * T])
+        make_factor(0)
+        scatter_single(1, 0, EXTRA + PIECE)
         make_factor(1)
+        take_pairs(1, 6, 8, third1)
         scatter(1, 6, 8)
-        w1_bf = scratch[:]
+        w1_bf = scratch[:, K:5 * K]
         for b in reversed(range(2)):
             nc.scalar.copy(w1_bf[:, b * HALF:(b + 1) * HALF].rearrange("p (k j) -> p k j", j=4), w1_raw[:, b].rearrange("p j k -> p k j"))
         for h in reversed(range(2)):
             nc.scalar.copy(partner[:, h * HALF:(h + 1) * HALF], window[0][:, h * HALF:(h + 1) * HALF])
-        nc.scalar.activation(mask0[:, 2 * HALF:].rearrange("p (t e) -> p t e", e=2), clamped1[:, 2 * T:3 * T].rearrange("p (e t) -> p t e", e=2),
-                             ACT.Copy, scale=1.0 / TINY)
+        late_clamped = clamped1[:, 2 * T:3 * T].rearrange("p (e t) -> p t e", e=2)
 
-        views = [tile[:].bitcast(BF16).rearrange("p (u t e) -> p t u e", u=2, e=2) for tile in (partner, window[1])]
+        def finish_mask0(g):
+            place = (g % MASK_QUARTERS) * HALF
+            nc.scalar.activation(mask0[:, place:place + HALF].rearrange("p (t e) -> p t e", e=2),
+                                 late_clamped[:, (g - 2) * QUARTER:(g - 1) * QUARTER, :], ACT.Copy, scale=1.0 / TINY)
+
+        copied = partner[:].bitcast(BF16).rearrange("p (u t e) -> p t u e", u=2, e=2)
+        quarters = window[1][:].bitcast(BF16).rearrange("p (x t e) -> p t x e", t=QUARTER, e=2)
+
+        def multiply(g):
+            place = T // QUARTER + g % MASK_QUARTERS
+            tokens = slice(g * QUARTER, (g + 1) * QUARTER)
+            nc.vector.tensor_tensor(da[:, tokens, :, :], copied[:, tokens, :, :],
+                                    quarters[:, :, place:(g - 1 if g else None):g - place, :], ALU.mult)
+
+        finish_mask0(2)
         w1_w = keep.tile([P, K], U32, name="w1_w", tag="pairs1", align_bytes=64)
         w1_sc = keep.tile([P, K], U8, name="w1_sc", align_bytes=64)
         da = keep.tile([P, T, 2, 2], BF16, name="da", align_bytes=64)
@@ -291,8 +309,9 @@ def tile_moe_sub_relu_kernel(tc, dy_words, dy_scales, w2t_words, w2t_scales, w1t
                 rhs=w2_w[0].bitcast(E5M2), rhs_scale=w2_sc[:, 0:H], start=True, stop=True)
         for h in range(2):
             for g in (2 * h, 2 * h + 1):
-                tokens = slice(g * QUARTER, (g + 1) * QUARTER)
-                nc.vector.tensor_tensor(da[:, tokens, :, :], views[0][:, tokens, :, :], views[1][:, tokens, ::-1, :], ALU.mult)
+                multiply(g)
+            if h == 0:
+                finish_mask0(3)
             for g in (2 * h, 2 * h + 1):
                 quantise(g)
             for g in (2 * h, 2 * h + 1):

@@ -31,7 +31,9 @@ OVERLAP = 64
 PRODUCT_BANKS = (0, 1, 2, 1, 0, 2, 1, 6)
 LATE_BYTES = 4 * PASSES * C
 EXTRA = 32
-SHARE_START = PIECE - EXTRA
+SHARE_START = PIECE
+SHARE_END = C + EXTRA
+SHARE = SHARE_END - SHARE_START
 MASK_QUARTERS = 3
 TINY = 2.0 ** -126
 
@@ -223,40 +225,41 @@ def tile_moe_sub_relu_kernel(tc, dy_words, dy_scales, w2t_words, w2t_scales, w1t
             turn(j, 1, first1, j)
         nc.scalar.copy(pairs[:, 1, 0:SHARE_START], first1[:, 0:SHARE_START])
         scatter_slots(1, 0, SHARE_START)
-        take_singles(0, EXTRA + P, first1[:, SHARE_START:3 * P])
+        take_singles(0, P, first1[:, SHARE_START:3 * P])
         for j in (2, 3):
             turn(j, 0, second0, j - 2)
         take_pairs(0, 2, 4, second0)
         scatter(0, 2, 4)
         scatter_single(0, 0, P)
-        third0, third1 = bank(4), bank(3)
+        third0 = bank(4)
         for j in (4, 5):
             gate_block(j)
-            turn(j, 1, second1, j - 4)
+            turn(j, 1, second1, j - 2)
             turn(j, 0, third0, j - 4)
+        turn(3, 1, second1, 1)
         for j in (6, 7):
             gate_block(j)
-            turn(j, 0, third0, j - 4)
             if j == 6:
-                turn(6, 1, third1, 0)
-                turn(3, 1, third1, 2)
-        take_pairs(1, 4, 6, second1)
-        scatter(1, 4, 6)
+                turn(6, 1, second1, 0)
+            turn(j, 0, third0, j - 4)
+        nc.scalar.copy(pairs[:, 1, SHARE_END:6 * P], second1[:, 2 * P + EXTRA:4 * P])
+        scatter_slots(1, SHARE_END, 6 * P)
+        take_singles(P, P + EXTRA, second1[:, P:2 * P + EXTRA])
         take_pairs(0, 4, 8, third0)
         scatter(0, 4, 8)
-        take_singles(EXTRA + P, P, third1[:, 2 * P:3 * P])
-        turn(7, 1, third1, 1)
-        scatter_single(0, P, EXTRA + PIECE)
+        turn(7, 1, second1, 1)
+        scatter_single(0, P, SHARE)
         clamp(clamped1[:, 2 * T + HALF:3 * T], a_second[:, T + HALF:2 * T])
         make_factor(0)
-        scatter_single(1, 0, EXTRA + PIECE)
+        scatter_single(1, 0, SHARE)
         make_factor(1)
-        take_pairs(1, 6, 8, third1)
+        take_pairs(1, 6, 8, second1)
         scatter(1, 6, 8)
-        w1_bf = scratch[:, K:5 * K]
-        for b in reversed(range(2)):
-            nc.scalar.copy(w1_bf[:, b * HALF:(b + 1) * HALF].rearrange("p (k j) -> p k j", j=4), w1_raw[:, b].rearrange("p j k -> p k j"))
-        for h in reversed(range(2)):
+        w1_bf = scratch[:, 2 * K:6 * K]
+        for b in range(2):
+            nc.scalar.copy(w1_bf[:, b * HALF:(b + 1) * HALF].rearrange("p (c i j) -> p c j i", i=4, j=4),
+                           w1_raw[:, b].rearrange("p j (c i) -> p c j i", i=4))
+        for h in range(2):
             nc.scalar.copy(partner[:, h * HALF:(h + 1) * HALF], window[0][:, h * HALF:(h + 1) * HALF])
         late_clamped = clamped1[:, 2 * T:3 * T].rearrange("p (e t) -> p t e", e=2)
 

@@ -26,15 +26,15 @@ W2_BYTES = 4 * PASSES * H
 HALF = 512
 QUARTER = 256
 SCALE_ROWS = 100
-BYTE_CUTS = ((0, PIECE), (PIECE, 3 * PIECE), (3 * PIECE, SLOTS))
+BYTE_CUTS = ((0, PIECE), (PIECE, 5 * P), (5 * P, SLOTS))
 OVERLAP = 64
-PRODUCT_BANKS = (0, 1, 2, 1, 0, 2, 1, 6)
+PRODUCT_BANKS = (0, 1, 2, 0, 1, 2, 0, 6)
 LATE_BYTES = 4 * PASSES * C
-EXTRA = 32
+EXTRA = 0
 SHARE_START = PIECE
 SHARE_END = C + EXTRA
 SHARE = SHARE_END - SHARE_START
-MASK_QUARTERS = 3
+MASK_QUARTERS = 4
 TINY = 2.0 ** -126
 
 
@@ -114,9 +114,7 @@ def tile_moe_sub_relu_kernel(tc, dy_words, dy_scales, w2t_words, w2t_scales, w1t
 
         for n in range(2):
             gather_bytes(n, keep.tile([P, BYTE_CUTS[n][1] - BYTE_CUTS[n][0]], U8, name="both%d" % n, tag="both%d" % n, align_bytes=64))
-        words0 = keep.tile([P, C], U32, name="words0", tag="words0", align_bytes=64)
-        for lo in range(0, C, PIECE):
-            gather_words(0, lo, lo + PIECE, words0[:, lo:lo + PIECE])
+        gather_words(0, 0, C, keep.tile([P, C], U32, name="words0", tag="words0", align_bytes=64)[:])
         a_first = late.tile([P, HALF + T], F32, name="a_first", offset=W2_BYTES + 3 * P, align_bytes=64)
         a_next = a_first[:, 0:HALF].rearrange("p (e t) -> p e t", e=2)
         nc.sync.dma_start(a_next, a_plane0[:, :, QUARTER:HALF])
@@ -124,9 +122,8 @@ def tile_moe_sub_relu_kernel(tc, dy_words, dy_scales, w2t_words, w2t_scales, w1t
         w2_late = late.tile([P, PASSES, H], I32, name="w2_late", offset=0, align_bytes=64)
         nc.sync.dma_start(w2_late[:], w2t_words[1].rearrange("s p i d -> p s (i d)").bitcast(I32))
         w2_w = [tile[:] for tile in w2_w] + [w2_late[:, s, :] for s in range(PASSES)]
-        for lo in range(0, C, PIECE):
-            gather_words(1, lo, lo + PIECE, keep.tile([P, PIECE], U32, name="words1_%d" % lo, align_bytes=64)[:])
-        gather_bytes(2, late.tile([P, PIECE], U8, name="both2", offset=W2_BYTES, align_bytes=64))
+        gather_words(1, 0, C, keep.tile([P, C], U32, name="words1", align_bytes=64)[:])
+        gather_bytes(2, late.tile([P, 3 * P], U8, name="both2", offset=W2_BYTES, align_bytes=64))
         a_second = last.tile([P, 2 * T], F32, name="a_second", offset=LATE_BYTES, align_bytes=64)
         nc.sync.dma_start(a_second[:, 0:T], a_rows[3])
         a_late = a_second[:, T:2 * T].rearrange("p (e t) -> p e t", e=2)
@@ -152,10 +149,10 @@ def tile_moe_sub_relu_kernel(tc, dy_words, dy_scales, w2t_words, w2t_scales, w1t
         clamp_woven(0, QUARTER, a_early[:])
         rescale(mask0[:, 0:HALF], clamped0[:, 0:HALF])
         clamp_woven(QUARTER, HALF, a_next)
-        clamp(clamped1[:, 0:T], a_first[:, HALF:])
         rescale(mask0[:, HALF:T], clamped0[:, HALF:T])
-        rescale(mask1[:, 0:T], clamped1[:, 0:T])
+        clamp(clamped1[:, 0:T], a_first[:, HALF:])
         clamp(clamped1[:, T:2 * T], a_second[:, 0:T])
+        rescale(mask1[:, 0:T], clamped1[:, 0:T])
         clamp(clamped1[:, 2 * T:2 * T + HALF], a_second[:, T:T + HALF])
         rescale(mask1[:, T:2 * T], clamped1[:, T:2 * T])
 
@@ -197,12 +194,14 @@ def tile_moe_sub_relu_kernel(tc, dy_words, dy_scales, w2t_words, w2t_scales, w1t
             scatter_slots(u, first * P, end * P)
 
         first0, first1, second0, second1 = bank(4), bank(3), bank(5), bank(7)
-        for j in range(2):
-            gate_block(j)
-            turn(j, 0, first0, j)
+        gate_block(0)
+        turn(0, 0, first0, 0)
+        gate_block(1)
+        take_pairs(0, 0, 1, first0)
+        scatter(0, 0, 1)
         gate_block(2)
-        take_pairs(0, 0, 2, first0)
-        scatter(0, 0, 2)
+        for j in range(2):
+            turn(j, 1, first1, j)
         partner = keep.tile([P, 2 * T], F32, name="partner", tag="words0", align_bytes=64)
         w1_raw = partner[:, 0:T].rearrange("p (b j k) -> p b j k", b=2, j=4)
         for b in range(2):
@@ -220,18 +219,17 @@ def tile_moe_sub_relu_kernel(tc, dy_words, dy_scales, w2t_words, w2t_scales, w1t
         def make_factor(e):
             nc.gpsimd.tensor_tensor(factor1[:, e, :], single[e][:], mask1[:, e * T:(e + 1) * T], ALU.mult)
 
-        gate_block(3)
-        for j in range(3):
-            turn(j, 1, first1, j)
         nc.scalar.copy(pairs[:, 1, 0:SHARE_START], first1[:, 0:SHARE_START])
         scatter_slots(1, 0, SHARE_START)
-        take_singles(0, P, first1[:, SHARE_START:3 * P])
-        for j in (2, 3):
-            turn(j, 0, second0, j - 2)
-        take_pairs(0, 2, 4, second0)
-        scatter(0, 2, 4)
-        scatter_single(0, 0, P)
-        third0 = bank(4)
+        gate_block(3)
+        aside = bank(4)
+        turn(2, 1, aside, 0)
+        take_singles(0, P, aside[:, 0:P])
+        for j in (1, 2, 3):
+            turn(j, 0, second0, j - 1)
+        take_pairs(0, 1, 4, second0)
+        scatter(0, 1, 4)
+        third0 = bank(3)
         for j in (4, 5):
             gate_block(j)
             turn(j, 1, second1, j - 2)
@@ -248,7 +246,7 @@ def tile_moe_sub_relu_kernel(tc, dy_words, dy_scales, w2t_words, w2t_scales, w1t
         take_pairs(0, 4, 8, third0)
         scatter(0, 4, 8)
         turn(7, 1, second1, 1)
-        scatter_single(0, P, SHARE)
+        scatter_single(0, 0, SHARE)
         clamp(clamped1[:, 2 * T + HALF:3 * T], a_second[:, T + HALF:2 * T])
         make_factor(0)
         scatter_single(1, 0, SHARE)

@@ -26,7 +26,7 @@ W2_BYTES = 4 * PASSES * H
 HALF = 512
 QUARTER = 256
 SCALE_ROWS = 100
-BYTE_CUTS = ((0, PIECE), (PIECE, 5 * P), (5 * P, SLOTS))
+BYTE_CUTS = ((0, PIECE), (PIECE, 3 * PIECE), (3 * PIECE, SLOTS))
 OVERLAP = 64
 PRODUCT_BANKS = (0, 1, 2, 0, 1, 2, 0, 6)
 LATE_BYTES = 4 * PASSES * C
@@ -114,7 +114,9 @@ def tile_moe_sub_relu_kernel(tc, dy_words, dy_scales, w2t_words, w2t_scales, w1t
 
         for n in range(2):
             gather_bytes(n, keep.tile([P, BYTE_CUTS[n][1] - BYTE_CUTS[n][0]], U8, name="both%d" % n, tag="both%d" % n, align_bytes=64))
-        gather_words(0, 0, C, keep.tile([P, C], U32, name="words0", tag="words0", align_bytes=64)[:])
+        words0 = keep.tile([P, C], U32, name="words0", tag="words0", align_bytes=64)
+        for lo in range(0, C, PIECE):
+            gather_words(0, lo, lo + PIECE, words0[:, lo:lo + PIECE])
         a_first = late.tile([P, HALF + T], F32, name="a_first", offset=W2_BYTES + 3 * P, align_bytes=64)
         a_next = a_first[:, 0:HALF].rearrange("p (e t) -> p e t", e=2)
         nc.sync.dma_start(a_next, a_plane0[:, :, QUARTER:HALF])
@@ -122,8 +124,9 @@ def tile_moe_sub_relu_kernel(tc, dy_words, dy_scales, w2t_words, w2t_scales, w1t
         w2_late = late.tile([P, PASSES, H], I32, name="w2_late", offset=0, align_bytes=64)
         nc.sync.dma_start(w2_late[:], w2t_words[1].rearrange("s p i d -> p s (i d)").bitcast(I32))
         w2_w = [tile[:] for tile in w2_w] + [w2_late[:, s, :] for s in range(PASSES)]
-        gather_words(1, 0, C, keep.tile([P, C], U32, name="words1", align_bytes=64)[:])
-        gather_bytes(2, late.tile([P, 3 * P], U8, name="both2", offset=W2_BYTES, align_bytes=64))
+        for lo in range(0, C, PIECE):
+            gather_words(1, lo, lo + PIECE, keep.tile([P, PIECE], U32, name="words1_%d" % lo, align_bytes=64)[:])
+        gather_bytes(2, late.tile([P, PIECE], U8, name="both2", offset=W2_BYTES, align_bytes=64))
         a_second = last.tile([P, 2 * T], F32, name="a_second", offset=LATE_BYTES, align_bytes=64)
         nc.sync.dma_start(a_second[:, 0:T], a_rows[3])
         a_late = a_second[:, T:2 * T].rearrange("p (e t) -> p e t", e=2)
@@ -153,7 +156,8 @@ def tile_moe_sub_relu_kernel(tc, dy_words, dy_scales, w2t_words, w2t_scales, w1t
         clamp(clamped1[:, 0:T], a_first[:, HALF:])
         clamp(clamped1[:, T:2 * T], a_second[:, 0:T])
         rescale(mask1[:, 0:T], clamped1[:, 0:T])
-        clamp(clamped1[:, 2 * T:2 * T + HALF], a_second[:, T:T + HALF])
+        third_clamped = clamped1[:, 2 * T:2 * T + HALF].rearrange("p (e t) -> p e t", e=2)
+        clamp(third_clamped, a_late[:, :, 0:QUARTER])
         rescale(mask1[:, T:2 * T], clamped1[:, T:2 * T])
 
         def product(j):
@@ -247,7 +251,6 @@ def tile_moe_sub_relu_kernel(tc, dy_words, dy_scales, w2t_words, w2t_scales, w1t
         scatter(0, 4, 8)
         turn(7, 1, second1, 1)
         scatter_single(0, 0, SHARE)
-        clamp(clamped1[:, 2 * T + HALF:3 * T], a_second[:, T + HALF:2 * T])
         make_factor(0)
         scatter_single(1, 0, SHARE)
         make_factor(1)
@@ -257,14 +260,13 @@ def tile_moe_sub_relu_kernel(tc, dy_words, dy_scales, w2t_words, w2t_scales, w1t
         for b in range(2):
             nc.scalar.copy(w1_bf[:, b * HALF:(b + 1) * HALF].rearrange("p (c i j) -> p c j i", i=4, j=4),
                            w1_raw[:, b].rearrange("p j (c i) -> p c j i", i=4))
-        for h in range(2):
-            nc.scalar.copy(partner[:, h * HALF:(h + 1) * HALF], window[0][:, h * HALF:(h + 1) * HALF])
-        late_clamped = clamped1[:, 2 * T:3 * T].rearrange("p (e t) -> p t e", e=2)
-
-        def finish_mask0(g):
-            place = (g % MASK_QUARTERS) * HALF
-            nc.scalar.activation(mask0[:, place:place + HALF].rearrange("p (t e) -> p t e", e=2),
-                                 late_clamped[:, (g - 2) * QUARTER:(g - 1) * QUARTER, :], ACT.Copy, scale=1.0 / TINY)
+        nc.scalar.copy(partner[:, 0:HALF], window[0][:, 0:HALF])
+        signs = scratch[:, 0:HALF]
+        nc.scalar.activation(signs.rearrange("p (t e) -> p t e", e=2), a_late[:, :, QUARTER:HALF].rearrange("p e t -> p t e"), ACT.Sign)
+        nc.scalar.activation(mask0[:, T:T + HALF].rearrange("p (t e) -> p t e", e=2), third_clamped.rearrange("p e t -> p t e"),
+                             ACT.Copy, scale=1.0 / TINY)
+        nc.scalar.copy(partner[:, HALF:T], window[0][:, HALF:T])
+        nc.scalar.activation(mask0[:, T + HALF:2 * T], signs, ACT.Relu)
 
         copied = partner[:].bitcast(BF16).rearrange("p (u t e) -> p t u e", u=2, e=2)
         quarters = window[1][:].bitcast(BF16).rearrange("p (x t e) -> p t x e", t=QUARTER, e=2)
@@ -275,7 +277,6 @@ def tile_moe_sub_relu_kernel(tc, dy_words, dy_scales, w2t_words, w2t_scales, w1t
             nc.vector.tensor_tensor(da[:, tokens, :, :], copied[:, tokens, :, :],
                                     quarters[:, :, place:(g - 1 if g else None):g - place, :], ALU.mult)
 
-        finish_mask0(2)
         w1_w = keep.tile([P, K], U32, name="w1_w", tag="pairs1", align_bytes=64)
         w1_sc = keep.tile([P, K], U8, name="w1_sc", align_bytes=64)
         da = keep.tile([P, T, 2, 2], BF16, name="da", align_bytes=64)
@@ -311,8 +312,6 @@ def tile_moe_sub_relu_kernel(tc, dy_words, dy_scales, w2t_words, w2t_scales, w1t
         for h in range(2):
             for g in (2 * h, 2 * h + 1):
                 multiply(g)
-            if h == 0:
-                finish_mask0(3)
             for g in (2 * h, 2 * h + 1):
                 quantise(g)
             for g in (2 * h, 2 * h + 1):

@@ -30,7 +30,7 @@ BYTE_CUTS = ((0, PIECE), (PIECE, 3 * PIECE), (3 * PIECE, SLOTS))
 OVERLAP = 64
 PRODUCT_BANKS = (0, 1, 2, 0, 1, 2, 0, 6)
 LATE_BYTES = 4 * PASSES * C
-EXTRA = 0
+EXTRA = -32
 SHARE_START = PIECE
 SHARE_END = C + EXTRA
 SHARE = SHARE_END - SHARE_START

@@ -26,7 +26,7 @@ W2_BYTES = 4 * PASSES * H
 HALF = 512
 QUARTER = 256
 SCALE_ROWS = 100
-BYTE_CUTS = ((0, PIECE), (PIECE, 3 * PIECE), (3 * PIECE, SLOTS))
+BYTE_CUTS = ((0, PIECE), (PIECE, 5 * P), (5 * P, SLOTS))
 OVERLAP = 64
 PRODUCT_BANKS = (0, 1, 2, 0, 1, 2, 0, 6)
 LATE_BYTES = 4 * PASSES * C
@@ -114,9 +114,7 @@ def tile_moe_sub_relu_kernel(tc, dy_words, dy_scales, w2t_words, w2t_scales, w1t
 
         for n in range(2):
             gather_bytes(n, keep.tile([P, BYTE_CUTS[n][1] - BYTE_CUTS[n][0]], U8, name="both%d" % n, tag="both%d" % n, align_bytes=64))
-        words0 = keep.tile([P, C], U32, name="words0", tag="words0", align_bytes=64)
-        for lo in range(0, C, PIECE):
-            gather_words(0, lo, lo + PIECE, words0[:, lo:lo + PIECE])
+        gather_words(0, 0, C, keep.tile([P, C], U32, name="words0", tag="words0", align_bytes=64)[:])
         a_first = late.tile([P, HALF + T], F32, name="a_first", offset=W2_BYTES + 3 * P, align_bytes=64)
         a_next = a_first[:, 0:HALF].rearrange("p (e t) -> p e t", e=2)
         nc.sync.dma_start(a_next, a_plane0[:, :, QUARTER:HALF])
@@ -124,9 +122,8 @@ def tile_moe_sub_relu_kernel(tc, dy_words, dy_scales, w2t_words, w2t_scales, w1t
         w2_late = late.tile([P, PASSES, H], I32, name="w2_late", offset=0, align_bytes=64)
         nc.sync.dma_start(w2_late[:], w2t_words[1].rearrange("s p i d -> p s (i d)").bitcast(I32))
         w2_w = [tile[:] for tile in w2_w] + [w2_late[:, s, :] for s in range(PASSES)]
-        for lo in range(0, C, PIECE):
-            gather_words(1, lo, lo + PIECE, keep.tile([P, PIECE], U32, name="words1_%d" % lo, align_bytes=64)[:])
-        gather_bytes(2, late.tile([P, PIECE], U8, name="both2", offset=W2_BYTES, align_bytes=64))
+        gather_words(1, 0, C, keep.tile([P, C], U32, name="words1", align_bytes=64)[:])
+        gather_bytes(2, late.tile([P, 3 * P], U8, name="both2", offset=W2_BYTES, align_bytes=64))
         a_second = last.tile([P, 2 * T], F32, name="a_second", offset=LATE_BYTES, align_bytes=64)
         nc.sync.dma_start(a_second[:, 0:T], a_rows[3])
         a_late = a_second[:, T:2 * T].rearrange("p (e t) -> p e t", e=2)
@@ -207,9 +204,8 @@ def tile_moe_sub_relu_kernel(tc, dy_words, dy_scales, w2t_words, w2t_scales, w1t
         for j in range(2):
             turn(j, 1, first1, j)
         partner = keep.tile([P, 2 * T], F32, name="partner", tag="words0", align_bytes=64)
-        w1_raw = partner[:, 0:T].rearrange("p (b j k) -> p b j k", b=2, j=4)
-        for b in range(2):
-            nc.sync.dma_start(w1_raw[:, b], w1t.rearrange("(p j) k -> p j k", j=4)[:, :, b * P:(b + 1) * P])
+        w1_raw = partner[:, 0:T]
+        nc.sync.dma_start(w1_raw, w1t.rearrange("(p j) k -> p (j k)", j=4))
         factor1 = partner[:, T:2 * T].bitcast(BF16).rearrange("p (t e) -> p e t", e=2)
         scratch = keep.tile([P, 6 * K], BF16, name="scratch", align_bytes=64)
         values = scratch[:].bitcast(F32).rearrange("p (e j) -> p e j", e=2)
@@ -257,12 +253,10 @@ def tile_moe_sub_relu_kernel(tc, dy_words, dy_scales, w2t_words, w2t_scales, w1t
         take_pairs(1, 6, 8, second1)
         scatter(1, 6, 8)
         w1_bf = scratch[:, 2 * K:6 * K]
-        for b in range(2):
-            nc.scalar.copy(w1_bf[:, b * HALF:(b + 1) * HALF].rearrange("p (c i j) -> p c j i", i=4, j=4),
-                           w1_raw[:, b].rearrange("p j (c i) -> p c j i", i=4))
-        nc.scalar.copy(partner[:, 0:HALF], window[0][:, 0:HALF])
+        nc.scalar.copy(w1_bf.rearrange("p (c i j) -> p c j i", i=4, j=4), w1_raw.rearrange("p (j c i) -> p c j i", j=4, i=4))
         signs = scratch[:, 0:HALF]
         nc.scalar.activation(signs.rearrange("p (t e) -> p t e", e=2), a_late[:, :, QUARTER:HALF].rearrange("p e t -> p t e"), ACT.Sign)
+        nc.scalar.copy(partner[:, 0:HALF], window[0][:, 0:HALF])
         nc.scalar.activation(mask0[:, T:T + HALF].rearrange("p (t e) -> p t e", e=2), third_clamped.rearrange("p e t -> p t e"),
                              ACT.Copy, scale=1.0 / TINY)
         nc.scalar.copy(partner[:, HALF:T], window[0][:, HALF:T])

from contextlib import ExitStack

import concourse.mybir as mybir
from concourse.masks import make_identity

K, T, E, C, H, N = 256, 1024, 2, 512, 512, 1024
FLOPS = 2 * N * H * E * C + 2 * H * K * T

F32 = mybir.dt.float32
BF16 = mybir.dt.bfloat16
I32 = mybir.dt.int32
U32 = mybir.dt.uint32
U16 = mybir.dt.uint16
U8 = mybir.dt.uint8
E4M3 = mybir.dt.float8_e4m3fn_x4
E5M2 = mybir.dt.float8_e5m2_x4
ACT = mybir.ActivationFunctionType
ALU = mybir.AluOpType

P = 128
PASSES = N // 512
SLOTS = E * C
PIECE = 256
PIECES = SLOTS // PIECE
W2_BYTES = 4 * PASSES * H
HALF = 512
QUARTER = 256
SCALE_ROWS = 100
BYTE_CUTS = ((0, PIECE), (PIECE, 5 * P), (5 * P, SLOTS))
OVERLAP = 64
PRODUCT_BANKS = (0, 1, 2, 0, 1, 2, 0, 6)
LATE_BYTES = 4 * PASSES * C
EXTRA = -32
SHARE_START = PIECE
SHARE_END = C + EXTRA
SHARE = SHARE_END - SHARE_START
MASK_QUARTERS = 4
TINY = 2.0 ** -126


def tile_moe_sub_relu_kernel(tc, dy_words, dy_scales, w2t_words, w2t_scales, w1t, a, gate, offs, out):
    nc = tc.nc
    with ExitStack() as ctx:
        keep = ctx.enter_context(tc.tile_pool(name="keep", bufs=1))
        last = ctx.enter_context(tc.tile_pool(name="last", bufs=1))
        late = ctx.enter_context(tc.tile_pool(name="late", bufs=1))
        psum = ctx.enter_context(tc.psum_pool(name="psum", bufs=1))

        def bank(n):
            return psum.tile([P, HALF], F32, name="bank%d" % n, tag="bank%d" % n)

        offsets = keep.tile([P, SLOTS // 16], U16, name="offsets")
        nc.sync.dma_start(offsets[:], offs)

        def entries(first, count):
            return offsets[:, first // 16:(first + count) // 16]

        dy_sc = last.tile([P, T], U8, name="dy_sc", offset=LATE_BYTES - T // 2, align_bytes=64)
        w2_sc = keep.tile([P, E * PASSES * H], U8, name="w2_sc", align_bytes=64)
        moved = [keep.tile([P, hi - lo], U8, name="moved%d" % lo, align_bytes=64) for lo, hi in BYTE_CUTS]
        gate_rows = late.tile([P, P], F32, name="gate_rows", offset=W2_BYTES - OVERLAP, align_bytes=64)
        ident = keep.tile([P, P], F32, name="ident")
        nc.gpsimd.memset(dy_sc[:].bitcast(I32), 0)
        nc.gpsimd.memset(gate_rows[:], 0.0)
        nc.gpsimd.memset(w2_sc[:].bitcast(I32), 0)
        make_identity(nc, ident[:])
        for tile in moved:
            nc.vector.memset(tile[:].bitcast(I32), 0)

        window = [keep.tile([P, T + u * MASK_QUARTERS * QUARTER], F32, name="window%d" % u, tag="window%d" % u, align_bytes=64) for u in range(2)]
        single = [keep.tile([P, T], F32, name="single%d" % e) for e in range(2)]
        for e in range(2):
            nc.gpsimd.memset(single[e][:], 1.0)
        nc.scalar.activation(window[1][:, 0:T].bitcast(BF16), ident[:, 0:1].to_broadcast([P, 2 * T]), ACT.Copy, bias=1.0, scale=0.0)

        w2_w = [keep.tile([P, H], I32, name="w2_w%d" % s, align_bytes=64) for s in range(PASSES)]
        nc.sync.dma_start(w2_w[0][:], w2t_words[0, 0].rearrange("p i d -> p (i d)").bitcast(I32))
        for q in range(4):
            nc.sync.dma_start(dy_sc[32 * q:32 * q + 4 * PASSES, :].bitcast(I32), dy_scales.bitcast(I32)[:, 4 * q:4 * q + 4, :])
        dy_w = keep.tile([P, PASSES * T], I32, name="dy_w", align_bytes=64)
        for s in range(PASSES):
            nc.sync.dma_start(dy_w[:, s * T:(s + 1) * T], dy_words[s].rearrange("p t d -> p (t d)").bitcast(I32))
            if s == 0:
                nc.sync.dma_start(gate_rows[0:SLOTS // P, :], gate[0].rearrange("(c p) -> c p", p=P))
        w2_sc_src = w2t_scales.bitcast(I32).rearrange("e s (q r) w -> r q (e s) w", r=4)
        for r in range(4):
            nc.sync.dma_start(w2_sc[r:P:32, :].bitcast(I32).rearrange("q (x w) -> q x w", x=E * PASSES), w2_sc_src[r])
        nc.sync.dma_start(w2_w[1][:], w2t_words[0, 1].rearrange("p i d -> p (i d)").bitcast(I32))
        a_rows = a.rearrange("(p r) t -> r p t", r=4)
        a_plane0 = a.rearrange("(p u e) t -> u p e t", u=2, e=2)[0]
        a_early = keep.tile([P, 2, QUARTER], F32, name="a_early", align_bytes=64)
        nc.sync.dma_start(a_early[:], a_plane0[:, :, 0:QUARTER])

        gate_ps = bank(7)
        nc.tensor.transpose(gate_ps[:, 0:P], gate_rows[:], ident[:])
        gate_col = keep.tile([P, SLOTS // P], F32, name="gate_col")
        nc.scalar.copy(gate_col[:], gate_ps[:, 0:SLOTS // P])

        g_sc = {}

        def gather_bytes(n, both):
            lo, hi = BYTE_CUTS[n]
            nc.vector.tensor_copy(both[:], dy_sc[:].indirect(entries(lo, hi - lo)))
            nc.sync.dma_start(moved[n][0:SCALE_ROWS, :].bitcast(I32), both[4:SCALE_ROWS + 4, :].bitcast(I32))
            for j in range(lo // P, hi // P):
                g_sc[j] = [tile[:, j * P - lo:(j + 1) * P - lo] for tile in (both, moved[n])]

        g_w = {}

        def gather_words(s, lo, hi, words):
            nc.vector.tensor_copy(words, dy_w[:, s * T:(s + 1) * T].bitcast(U32).indirect(entries(lo, hi - lo)))
            for j in range(lo // P, hi // P):
                g_w[j, s] = words[:, j * P - lo:(j + 1) * P - lo]

        for n in range(2):
            gather_bytes(n, keep.tile([P, BYTE_CUTS[n][1] - BYTE_CUTS[n][0]], U8, name="both%d" % n, tag="both%d" % n, align_bytes=64))
        gather_words(0, 0, C, keep.tile([P, C], U32, name="words0", tag="words0", align_bytes=64)[:])
        a_first = late.tile([P, HALF + T], F32, name="a_first", offset=W2_BYTES + 3 * P, align_bytes=64)
        a_next = a_first[:, 0:HALF].rearrange("p (e t) -> p e t", e=2)
        nc.sync.dma_start(a_next, a_plane0[:, :, QUARTER:HALF])
        nc.sync.dma_start(a_first[:, HALF:], a_rows[2])
        w2_late = late.tile([P, PASSES, H], I32, name="w2_late", offset=0, align_bytes=64)
        nc.sync.dma_start(w2_late[:], w2t_words[1].rearrange("s p i d -> p s (i d)").bitcast(I32))
        w2_w = [tile[:] for tile in w2_w] + [w2_late[:, s, :] for s in range(PASSES)]
        gather_words(1, 0, C, keep.tile([P, C], U32, name="words1", align_bytes=64)[:])
        gather_bytes(2, late.tile([P, 3 * P], U8, name="both2", offset=W2_BYTES, align_bytes=64))
        a_second = last.tile([P, 2 * T], F32, name="a_second", offset=LATE_BYTES, align_bytes=64)
        nc.sync.dma_start(a_second[:, 0:T], a_rows[3])
        a_late = a_second[:, T:2 * T].rearrange("p (e t) -> p e t", e=2)
        nc.sync.dma_start(a_late, a_plane0[:, :, HALF:T])
        late_words = last.tile([P, LATE_BYTES // 4], U32, name="late_words", offset=0, align_bytes=64)
        for s in reversed(range(PASSES)):
            gather_words(s, C, SLOTS, late_words[:, s * C:(s + 1) * C])

        clamped0 = keep.tile([P, T], BF16, name="clamped0", align_bytes=64)
        clamped1 = keep.tile([P, 3 * T], BF16, name="clamped1", align_bytes=64)
        mask1 = keep.tile([P, 2 * T], BF16, name="mask1", align_bytes=64)
        mask0 = window[1][:, T:].bitcast(BF16)

        def clamp(dst, values):
            nc.gpsimd.tensor_scalar(dst, values, TINY, 0.0, ALU.min, ALU.max)

        def clamp_woven(first, end, values):
            clamp(clamped0[:, 2 * first:2 * end].rearrange("p (t e) -> p t e", e=2), values.rearrange("p e t -> p t e"))

        def rescale(dst, values):
            nc.gpsimd.tensor_scalar(dst, values, 1.0 / TINY, 0.0, ALU.mult, ALU.add)

        clamp_woven(0, QUARTER, a_early[:])
        rescale(mask0[:, 0:HALF], clamped0[:, 0:HALF])
        clamp_woven(QUARTER, HALF, a_next)
        rescale(mask0[:, HALF:T], clamped0[:, HALF:T])
        clamp(clamped1[:, 0:T], a_first[:, HALF:])
        clamp(clamped1[:, T:2 * T], a_second[:, 0:T])
        rescale(mask1[:, 0:T], clamped1[:, 0:T])
        third_clamped = clamped1[:, 2 * T:2 * T + HALF].rearrange("p (e t) -> p e t", e=2)
        clamp(third_clamped, a_late[:, :, 0:QUARTER])
        rescale(mask1[:, T:2 * T], clamped1[:, T:2 * T])

        def product(j):
            y = bank(PRODUCT_BANKS[j])
            e = j * P // C
            order = range(PASSES) if j < PIECE // P else reversed(range(PASSES))
            for n, s in enumerate(order):
                x = e * PASSES + s
                nc.tensor.matmul_mx(
                    out=y[:],
                    lhsT=g_w[j, s].bitcast(E5M2),
                    lhsT_scale=g_sc[j][s],
                    rhs=w2_w[x].bitcast(E4M3),
                    rhs_scale=w2_sc[:, x * H:(x + 1) * H],
                    start=(n == 0),
                    stop=(n == PASSES - 1),
                )
            return y[:].rearrange("p (q u e) -> p u q e", u=2, e=2)

        pairs = keep.tile([P, 2, SLOTS], F32, name="pairs", tag="pairs1", align_bytes=64)
        dh = {}

        def gate_block(j):
            y = product(j)
            dh[j] = keep.tile([P, H], BF16, name="dh%d" % j, tag="dh%d" % j, align_bytes=64)[:]
            nc.scalar.activation(dh[j].rearrange("p (u q e) -> p u q e", u=2, e=2), y, ACT.Copy, scale=gate_col[:, j:j + 1])

        def turn(j, u, turned, place):
            nc.tensor.transpose(turned[:, place * P:(place + 1) * P], dh[j].bitcast(F32)[:, u * P:(u + 1) * P], ident[:])

        def take_pairs(u, first, end, turned):
            nc.scalar.copy(pairs[:, u, first * P:end * P], turned[:, 0:(end - first) * P])

        def scatter_slots(u, first, end):
            nc.vector.tensor_copy(window[u][:].indirect(entries(first, end - first)), pairs[:, u, first:end])

        def scatter(u, first, end):
            scatter_slots(u, first * P, end * P)

        first0, first1, second0, second1 = bank(4), bank(3), bank(5), bank(7)
        gate_block(0)
        turn(0, 0, first0, 0)
        gate_block(1)
        take_pairs(0, 0, 1, first0)
        scatter(0, 0, 1)
        gate_block(2)
        for j in range(2):
            turn(j, 1, first1, j)
        partner = keep.tile([P, 2 * T], F32, name="partner", tag="words0", align_bytes=64)
        w1_raw = partner[:, 0:T]
        nc.sync.dma_start(w1_raw, w1t.rearrange("(p j) k -> p (j k)", j=4))
        factor1 = partner[:, T:2 * T].bitcast(BF16).rearrange("p (t e) -> p e t", e=2)
        scratch = keep.tile([P, 6 * K], BF16, name="scratch", align_bytes=64)
        values = scratch[:].bitcast(F32).rearrange("p (e j) -> p e j", e=2)

        def take_singles(first, count, turned):
            nc.scalar.copy(values[:, :, first:first + count], turned.bitcast(BF16).rearrange("p (j e) -> p e j", e=2))

        def scatter_single(e, first, end):
            nc.scalar.activation(single[e][:].indirect(entries(SHARE_START + first, end - first)), values[:, e, first:end], ACT.Copy)

        def make_factor(e):
            nc.gpsimd.tensor_tensor(factor1[:, e, :], single[e][:], mask1[:, e * T:(e + 1) * T], ALU.mult)

        nc.scalar.copy(pairs[:, 1, 0:SHARE_START], first1[:, 0:SHARE_START])
        scatter_slots(1, 0, SHARE_START)
        gate_block(3)
        aside = bank(4)
        turn(2, 1, aside, 0)
        take_singles(0, P, aside[:, 0:P])
        for j in (1, 2, 3):
            turn(j, 0, second0, j - 1)
        take_pairs(0, 1, 4, second0)
        scatter(0, 1, 4)
        third0 = bank(3)
        for j in (4, 5):
            gate_block(j)
            turn(j, 1, second1, j - 2)
            turn(j, 0, third0, j - 4)
        turn(3, 1, second1, 1)
        for j in (6, 7):
            gate_block(j)
            if j == 6:
                turn(6, 1, second1, 0)
            turn(j, 0, third0, j - 4)
        nc.scalar.copy(pairs[:, 1, SHARE_END:6 * P], second1[:, 2 * P + EXTRA:4 * P])
        scatter_slots(1, SHARE_END, 6 * P)
        take_singles(P, P + EXTRA, second1[:, P:2 * P + EXTRA])
        take_pairs(0, 4, 8, third0)
        scatter(0, 4, 8)
        turn(7, 1, second1, 1)
        scatter_single(0, 0, SHARE)
        make_factor(0)
        scatter_single(1, 0, SHARE)
        make_factor(1)
        take_pairs(1, 6, 8, second1)
        scatter(1, 6, 8)
        w1_bf = scratch[:, 2 * K:6 * K]
        nc.scalar.copy(w1_bf.rearrange("p (c i j) -> p c j i", i=4, j=4), w1_raw.rearrange("p (j c i) -> p c j i", j=4, i=4))
        signs = scratch[:, 0:HALF]
        nc.scalar.activation(signs.rearrange("p (t e) -> p t e", e=2), a_late[:, :, QUARTER:HALF].rearrange("p e t -> p t e"), ACT.Sign)
        nc.scalar.copy(partner[:, 0:HALF], window[0][:, 0:HALF])
        nc.scalar.activation(mask0[:, T:T + HALF].rearrange("p (t e) -> p t e", e=2), third_clamped.rearrange("p e t -> p t e"),
                             ACT.Copy, scale=1.0 / TINY)
        nc.scalar.copy(partner[:, HALF:T], window[0][:, HALF:T])
        nc.scalar.activation(mask0[:, T + HALF:2 * T], signs, ACT.Relu)

        copied = partner[:].bitcast(BF16).rearrange("p (u t e) -> p t u e", u=2, e=2)
        quarters = window[1][:].bitcast(BF16).rearrange("p (x t e) -> p t x e", t=QUARTER, e=2)

        def multiply(g):
            place = T // QUARTER + g % MASK_QUARTERS
            tokens = slice(g * QUARTER, (g + 1) * QUARTER)
            nc.vector.tensor_tensor(da[:, tokens, :, :], copied[:, tokens, :, :],
                                    quarters[:, :, place:(g - 1 if g else None):g - place, :], ALU.mult)

        w1_w = keep.tile([P, K], U32, name="w1_w", tag="pairs1", align_bytes=64)
        w1_sc = keep.tile([P, K], U8, name="w1_sc", align_bytes=64)
        da = keep.tile([P, T, 2, 2], BF16, name="da", align_bytes=64)
        da_w = keep.tile([P, T], U32, name="da_w", align_bytes=64)
        da_sc = keep.tile([P, T], U8, name="da_sc", align_bytes=64)

        def quantise(g):
            tokens = slice(g * QUARTER, (g + 1) * QUARTER)
            nc.vector.quantize_mx(out=da_w[:, tokens].bitcast(E5M2), scales=da_sc[:, tokens],
                                  in_=da[:, tokens, :, :].rearrange("p t u e -> p (t u e)"))

        def finish(g):
            tokens = slice(g * QUARTER, (g + 1) * QUARTER)
            for kb in range(K // P):
                cols = slice(kb * P, (kb + 1) * P)
                acc = bank(2 * g + kb)[:, 0:QUARTER]
                nc.tensor.matmul_mx(
                    out=acc, lhsT=w1_w[:, cols].bitcast(E4M3), lhsT_scale=w1_sc[:, cols],
                    rhs=da_w[:, tokens].bitcast(E5M2), rhs_scale=da_sc[:, tokens], start=True, stop=True)
                res = keep.tile([P, QUARTER], F32, name="res%d_%d" % (g, kb))
                if g >= 2 and kb == 1:
                    nc.vector.tensor_copy(res[:], acc)
                else:
                    nc.scalar.copy(res[:], acc)
                (nc.scalar if (g, kb) == (3, 0) else nc.sync).dma_start(out[cols, tokens], res[:])

        nc.vector.quantize_mx(out=w1_w[:].bitcast(E4M3), scales=w1_sc[:], in_=w1_bf)
        warm = bank(7)
        for n in range(2):
            nc.tensor.matmul_mx(
                out=warm[:], lhsT=w1_w[:, 0:P].bitcast(E4M3), lhsT_scale=w1_sc[:, 0:P],
                rhs=w2_w[0].bitcast(E5M2), rhs_scale=w2_sc[:, 0:H], start=True, stop=True)
        for h in range(2):
            for g in (2 * h, 2 * h + 1):
                multiply(g)
            for g in (2 * h, 2 * h + 1):
                quantise(g)
            for g in (2 * h, 2 * h + 1):
                finish(g)
